import numpy as np, ml_dtypes
CORES = [40,64,80,88,96,104,120,144]
N = 8
BF = ml_dtypes.bfloat16
def gentries(a):
    return np.ascontiguousarray(a.reshape(8, 16, -1).transpose(0, 2, 1)).reshape(8, -1)
def gtable(e):
    e = np.asarray(e); return np.ascontiguousarray(e.reshape(8, -1, 16).transpose(0, 2, 1)).reshape(128, -1).astype(np.int32)
def f(rng, *shape):
    return (rng.standard_normal(shape, dtype=np.float32) * np.exp2(rng.integers(-2, 3, shape[:-1] + (1,)))).astype(BF)
def wide(rng, *shape):
    v = f(rng, *shape).astype(np.float32); k = shape[:-2] + (1, shape[-1])
    return (v * np.exp2(rng.integers(-6, 7, k)) * (rng.random(k) > 0.0625)).astype(BF)
V, D, C, R = 2048, 3, 32, 2
def ranks(t):
    return t.reshape(8, D, N, V).transpose(2, 0, 1, 3)
def globe(a, bl):
    out = np.zeros((N, 8, D * V), np.int64)
    for r in range(N):
        own = np.broadcast_to(r * V + np.arange(V), (8, V))
        ghosts = (np.arange(N)[:, None, None] * V + bl[:, :, r]).transpose(1, 0, 2).reshape(8, N * C)
        out[r] = np.take_along_axis(np.concatenate([own, ghosts], 1), a[r].reshape(8, D * V).astype(np.int64), 1)
    return out.reshape(N, 8, D, V).transpose(1, 2, 0, 3).reshape(8, D, N * V)
def unpack(nb, bl):
    return np.stack([gentries(t) for t in nb]).reshape(N, 8, D, V), np.stack([gentries(t) for t in bl]).reshape(N, 8, N, C)
def pack(rng, a, bl, v):
    o = np.argsort(rng.random(a.shape), 2); a = np.take_along_axis(a, o, 2); v = np.take_along_axis(v, o, 2)
    return {"nb": np.stack([gtable(t.reshape(8, D * V)) for t in a]), "bl": np.stack([gtable(t.reshape(8, N * C)) for t in bl]),
            "w": np.ascontiguousarray(v).reshape(N, 8, D * V).astype(np.float32).astype(BF), "x": f(rng, N, 128, V)}
def graphs(rng, p):
    bl = np.argsort(rng.random((N, 8, N, V)), axis=-1)[..., :C]
    a = np.full((N, 8, D, V), -1, np.int64)
    for g in range(8):
        for d in range(D):
            for r in range(N):
                for q in range(r):
                    o = rng.permutation(C); u = bl[r, g, q]; t = bl[q, g, r][o]
                    k = (a[r, g, d, u] < 0) & (a[q, g, d, t] < 0) & (rng.random(C) < p)
                    a[r, g, d, u[k]] = V + q * C + o[k]; a[q, g, d, t[k]] = V + r * C + np.flatnonzero(k)
            for r in range(N):
                e = rng.permutation(np.flatnonzero(a[r, g, d] < 0)); h = len(e) // 2
                a[r, g, d, e[:h]] = e[h:2 * h]; a[r, g, d, e[h:2 * h]] = e[:h]
                if len(e) > 2 * h: a[r, g, d, e[-1]] = (e[-1] + 1) % V
        for r in range(N):
            alias = np.full(V, -1, np.int64); alias[bl[r, g, r]] = V + r * C + np.arange(C)
            b = a[r, g]; n = np.where(b < V, alias[np.minimum(b, V - 1)], -1)
            a[r, g] = np.where((n >= 0) & (rng.random((D, V)) < 0.5), n, b)
    return a, bl
def both(a, bl, z):
    return np.array(ranks(np.take_along_axis(z, np.minimum(globe(a, bl), np.arange(N * V)), 2)))
def setup_inputs(rng):
    a, bl = graphs(rng, 0.6)
    return pack(rng, a, bl, both(a, bl, np.exp2(4 * rng.random((8, D, N * V)))))
def setup_inputs_ties(rng):
    a, bl = graphs(rng, 0.6); z = rng.integers(1, 4, (8, D, N * V)).astype(np.float64); z[rng.integers(0, 8)] = 1
    z *= np.exp2(rng.integers(-20, 21, (8, 1, 1)))
    return pack(rng, a, bl, both(a, bl, z))
def setup_inputs_borders(rng):
    a, bl = graphs(rng, 1.0); v = both(a, bl, np.exp2(3 * rng.random((8, D, N * V))))
    far = ranks(globe(a, bl) // V != np.arange(N * V) // V)
    return pack(rng, a, bl, v * np.where(far, 8, 1))
def setup_inputs_hubs(rng):
    a, bl = graphs(rng, 0.6); v = both(a, bl, np.exp2(4 * rng.random((8, D, N * V))))
    for r in range(N):
        for g in range(8):
            e = rng.permutation(V); h = e[:16]; leaves = e[16:V // 2]; b = a[r, g]; c = v[r, g]
            b[:, leaves] = h[rng.integers(0, 16, (D, len(leaves)))]
            b[0, h] = h[np.arange(16) ^ 1]; c[0, h] = 256
    return pack(rng, a, bl, v)
def setup_inputs_any(rng):
    bl = rng.integers(0, V, (N, 8, N, C)); bl[..., C // 2:] = bl[..., :1]; bl[..., 1] = 0; bl[..., 2] = V - 1
    a = rng.integers(0, V + N * C, (N, 8, D, V)); j = np.arange(V)
    a = np.where(ranks(globe(a, bl) == np.arange(N * V)), (j + 1) % V, a)
    o = rng.permutation(8); a[:, o[0]] = (j + 1) % V; a[:, o[1]] = j ^ 1
    for r in range(N):
        for g in o[2:5]:
            q = r ^ 1
            a[r, g, :, bl[r, g, q, 0]] = V + q * C + rng.choice(np.r_[0, C // 2:C], D)
    return pack(rng, a, bl, np.exp2(4 * rng.random((N, 8, D, V))))
def setup_inputs_spread(rng):
    a, bl = graphs(rng, 0.6); z = np.exp2(rng.integers(-3, 4, (8, D, N * V)) + rng.random((8, D, N * V)))
    d = pack(rng, a, bl, both(a, bl, z)); d["x"] = wide(rng, N, 128, V); return d
def check_inputs(d):
    bad = []
    if d["bl"].min() < 0 or d["bl"].max() >= V: bad.append("bl")
    if d["nb"].min() < 0 or d["nb"].max() >= V + N * C: bad.append("nb")
    if not bad and (globe(*unpack(d["nb"], d["bl"])) == np.arange(N * V)).any(): bad.append("own neighbour")
    u = d["w"].astype(np.float32)
    if not (np.isfinite(u).all() and (u > 0).all()): bad.append("w")
    v = np.abs(d["x"].astype(np.float32))
    if not np.isfinite(v).all(): bad.append("x")
    if not 4.0 * D * float(u.max()) * float(v.max()) < 2.0 ** 127: bad.append("range")
    return bad
def reference(nb, bl, w, x):
    i = np.arange(N * V); A = globe(*unpack(nb, bl))
    u = w.astype(np.float64).reshape(N, 8, D, V).transpose(1, 2, 0, 3).reshape(8, D, N * V)
    mate = np.tile(i, (8, 1)); free = np.ones((8, N * V), bool)
    for t in range(R):
        k = np.where(np.take_along_axis(free[:, None], A, 2), u, 0.0)
        P = np.take_along_axis(A, np.argmax(k, 1)[:, None], 1)[:, 0]
        P = np.where(free & (np.max(k, 1) > 0), P, -1)
        hit = (P >= 0) & (np.take_along_axis(P, np.maximum(P, 0), 1) == i)
        mate = np.where(hit, P, mate); free = free & ~hit
    two = mate != i; first = np.minimum(mate, i); rep = first == i
    num = (np.add.accumulate(rep.reshape(8, N, V).astype(np.int64), 2) - 1 + V * np.arange(N)[:, None]).reshape(8, N * V)
    cm = np.take_along_axis(num, first, 1).reshape(8, N, V)
    xx = np.ascontiguousarray(x.astype(np.float64).reshape(N, 8, 16, V).transpose(1, 2, 0, 3)).reshape(8, 16, N * V)
    X = xx + np.where(two[:, None], np.take_along_axis(xx, mate[:, None], 2), 0.0)
    s = np.zeros((8, 16, N * V))
    for d in range(D):
        s += u[:, d, None] * np.take_along_axis(X, A[:, d, None], 2)
    s = s + np.where(two[:, None], np.take_along_axis(s, mate[:, None], 2), 0.0)
    y = np.zeros((8, 16, N * V))
    for g in range(8):
        y[g][:, num[g, rep[g]]] = s[g][:, rep[g]]
    y = np.ascontiguousarray(y.reshape(8, 16, N, V).transpose(2, 0, 1, 3)).reshape(N, 128, V)
    return {"y": y.astype(np.float32), "cm": np.stack([gtable(cm[:, r]) for r in range(N)]).astype(np.float32)}

@@ -1,0 +1,562 @@
+from concourse.mybir import AluOpType, ActivationFunctionType
+from concourse.bass import DstId, RemoteDMATransfer
+
+N, V, C, D = 8, 2048, 32, 3
+GH, NONE = V, V + N * C
+EXT = NONE + 16
+
+
+def buffers(*groups):
+    out = {}
+    for names, width, dtype in groups:
+        for n in names.split():
+            out[n] = ("sbuf", [128, width], dtype)
+    return out
+
+
+SCRATCH = buffers(
+    ("bli bsh bms", 16, "int32"), ("nbi", 384, "int32"), ("pi", 8, "int32"),
+    ("wa tr", 384, "bfloat16"), ("wb", 6144, "bfloat16"), ("s0 s1", 160, "bfloat16"), ("e1 ehl", 144, "bfloat16"),
+    ("gn go nt rep", 128, "bfloat16"), ("xe hl m1 nx", EXT, "bfloat16"), ("lo", NONE, "bfloat16"),
+    ("xb m1b nxb", 256, "bfloat16"), ("fb", 1024, "bfloat16"), ("f1 f2 f3 mm hg cg x2", V, "bfloat16"),
+    ("lw", 2 * V, "bfloat16"), ("rX r2 r6", C, "bfloat16"),
+    ("blo pcb bmo ro1 ro3 lr1 lr3 zz", 16, "uint16"), ("r1 r3", 2, "uint16"), ("boff", 48, "uint16"), ("bpo", 64, "uint16"),
+    ("pco mo lam no rhoo l1", 128, "uint16"), ("nbo po", 384, "uint16"),
+    ("pc ub qb id16 kk kt", 16, "float32"), ("r4 r5", C, "float32"), ("g40", 320, "float32"), ("bp db", 48, "float32"),
+    ("xi", 160, "float32"), ("eall", 144, "float32"), ("gm gf idf ones va va2 w1s wm wl dn ta tb tc te", 128, "float32"),
+    ("ua pcf gt pz mt lt inc nn rho rn cmf", 128, "float32"), ("nbf pa da", 384, "float32"),
+    ("jm m16 m0 bs gbb bmask xcb mb xm xxb sb", 256, "float32"), ("pg", 768, "float32"), ("gs", 1024, "float32"),
+    ("rt t1 t2 xx sx", EXT, "float32"), ("p1 p2 p3 yy", V, "float32"), ("sp", V + 8, "float32"))
+PSUM = {"gw": 1024, "v0": 512, "v1": 512, "a0": 512, "a1": 512, "a2": 512, "a3": 512}
+for _n in PSUM:
+    SCRATCH[_n] = ("psum", [128, PSUM[_n]], "float32")
+EXCH = {"X": ("xb", "xe", GH, C), "1": ("ro1", "lr1", 0, 2), "2": ("m1b", "m1", GH, C), "3": ("ro3", "lr3", 0, 2),
+        "4": ("xxb", "xx", GH, C), "6": ("nxb", "nx", GH, C), "5": ("sb", "sx", GH, C)}
+ORDER = ["X", "1", "2", "3", "4", "6", "5"]
+DMAS = ["bl", "z1", "z3", "nb", "w0", "w1", "w2", "x", "wb", "lo", "cm"] + ["y%d" % i for i in range(8)]
+SEMAPHORES = (["v", "s", "t", "p", "loc", "rloc"] + ["d" + n for n in DMAS] + ["arr" + k for k in ORDER]
+              + ["hop" + k for k in ORDER])
+
+
+def pick(engines, i, n):
+    m = 0
+    for e in engines[i * n:(i + 1) * n]:
+        m |= 1 << e
+    return m
+
+
+def plan(src, T, topo):
+    near, far = [], []
+    for d in T.cores:
+        if d != src:
+            (near if topo.may_write(src, d) else far).append(d)
+    hops = [c for c in topo.cores_of(src) if c != src and all(topo.may_write(c, d) for d in far)]
+    straight = [(d, pick(topo.engines(src, d), i, 2)) for i, d in enumerate(near)]
+    over = []
+    for i, d in enumerate(far):
+        h = hops[i]
+        over.append((h, pick(topo.engines(src, h), i, 4), d, topo.mask(h, d)))
+    return straight, over
+
+
+def bits(m):
+    return bin(m).count("1")
+
+
+def hop_program(g, core, T, topo):
+    for src in topo.cores_of(core):
+        if T.rank_of(src) is None:
+            continue
+        r = T.rank_of(src)
+        for h, m_in, d, m_out in plan(src, T, topo)[1]:
+            if h != core:
+                continue
+            rid, pid = topo.addr(d, core)
+            for k in ORDER:
+                _, land, c0, w = EXCH[k]
+                g.wait_ge(T.sem["hop" + k], bits(m_in))
+                g.remote_dma(T[land][:, c0 + w * r:c0 + w * r + w], T["r" + k][:], T.sem["arr" + k], T.sem.rloc,
+                             pid, rid, m_out)
+            g.wait_ge(T.sem.rloc, bits(m_out) * len(ORDER))
+
+
+def rank_program(g, core, T, topo):
+    rank = T.rank_of(core)
+    if rank is None:
+        hop_program(g, core, T, topo)
+        return
+    A = AluOpType
+    COPY, IDENT = ActivationFunctionType.Copy, ActivationFunctionType.Identity
+    q_of = {"v": g.vector, "s": g.scalar, "t": g.tensor, "g": g, "y": g.sync}
+    count = {"v": 0, "s": 0, "t": 0, "p": 0}
+    waited = {"v": {}, "s": {}, "t": {}, "g": {}, "y": {}}
+    log = {}
+    totals = {}
+
+    def need(queue, tokens):
+        best = {}
+        for s, n in tokens:
+            best[s] = max(n, best.get(s, 0))
+        for s in sorted(best):
+            if waited[queue].get(s, 0) < best[s]:
+                q_of[queue].wait_ge(T.sem[s], best[s])
+                waited[queue][s] = best[s]
+
+    def deps(queue, reads, writes):
+        out = []
+        for regs, wr in ((reads, False), (writes, True)):
+            for name, lo, hi in regs:
+                ps = name in PSUM
+                for l, h, w, tok, qq in log.get(name, []):
+                    if ps and qq != queue:
+                        if l // 512 * 512 < -(-hi // 512) * 512 and lo // 512 * 512 < -(-h // 512) * 512:
+                            out.append(tok)
+                    elif l < hi and lo < h and (w or wr) and not (ps and queue == "t"):
+                        out.append(tok)
+        return out
+
+    def note(queue, reads, writes, tok):
+        for regs, wr in ((reads, False), (writes, True)):
+            for name, lo, hi in regs:
+                log.setdefault(name, []).append((lo, hi, wr, tok, queue))
+
+    def ap(r):
+        if r[0] == "ind":
+            return ap(r[1]).indirect(ap(r[2]))
+        name, lo, hi = r[0], r[1], r[2]
+        return T[name][:, lo:hi] if len(r) == 3 else T[name][:, lo:hi:r[3]]
+
+    def regs(rs):
+        out = []
+        for r in rs:
+            if isinstance(r, tuple):
+                if r[0] == "ind":
+                    out += regs([r[1], r[2]])
+                else:
+                    out.append((r[0], r[1], r[2]))
+        return out
+
+    def val(x):
+        return ap(x) if isinstance(x, tuple) else x
+
+    def run(queue, reads, outs, emit):
+        rd, wr = regs(reads), []
+        for o in outs:
+            if o[0] == "ind":
+                wr += regs([o[1]])
+                rd += regs([o[2]])
+            else:
+                wr += regs([o])
+        need(queue, deps(queue, rd, wr))
+        s = "p" if queue == "g" else queue
+        count[s] += 1
+        emit().then_inc(T.sem[s], 1)
+        note(queue, rd, wr, (s, count[s]))
+
+    def tt(out, a, b, op):
+        run("v", [a, b], [out], lambda: g.vector.tensor_tensor(ap(out), ap(a), ap(b), op))
+
+    def ts(out, a, s1, op0, s2=None, op1=None):
+        if op1 is None:
+            run("v", [a, s1], [out], lambda: g.vector.tensor_scalar(ap(out), ap(a), val(s1), None, op0))
+        else:
+            run("v", [a, s1, s2], [out], lambda: g.vector.tensor_scalar(ap(out), ap(a), val(s1), val(s2), op0, op1))
+
+    def cp(out, a):
+        run("v", [a], [out], lambda: g.vector.tensor_copy(ap(out), ap(a)))
+
+    def sc(out, a):
+        run("s", [a], [out], lambda: g.scalar.activation(ap(out), ap(a), COPY))
+
+    def sa(out, a, scale, bias):
+        run("s", [a], [out], lambda: g.scalar.activation(ap(out), ap(a), IDENT, bias=float(bias), scale=float(scale)))
+
+    def iota(out, pattern, base, ch):
+        run("g", [], [out], lambda: g.iota(ap(out), pattern, base, ch, allow_small_or_imprecise_dtypes=True))
+
+    def mm(group):
+        rd = regs([m[1] for m in group] + [m[2] for m in group])
+        wr = regs([m[0] for m in group])
+        need("t", deps("t", rd, wr))
+        ins = None
+        for o, l, r, st, sp in group:
+            ins = g.tensor.matmul(ap(o), ap(l), ap(r), st, sp)
+        count["t"] += 1
+        ins.then_inc(T.sem.t, 1)
+        note("t", list(dict.fromkeys(rd)), list(dict.fromkeys(wr)), ("t", count["t"]))
+
+    def to_a(ps, c0, n, lhs, src, base=0):
+        mm([((ps, c0, c0 + n), (lhs, 15 - k, 143 - k), (src, base + k, base + 16 * n, 16), k == 0, k == 15)
+            for k in range(16)])
+
+    def dma(queue, sem, out, in_, reads, writes):
+        need(queue, deps(queue, reads, writes))
+        q_of[queue].dma_start(out, in_).then_inc(T.sem["d" + sem], 16)
+        totals["d" + sem] = totals.get("d" + sem, 0) + 16
+        note(queue, reads, writes, ("d" + sem, totals["d" + sem]))
+
+    straight, over = plan(core, T, topo)
+    sent = [0]
+
+    def send(k):
+        src, land, c0, w = EXCH[k]
+        need("g", deps("g", [(src, 0, w * N)], []))
+
+        def block(d):
+            q = T.rank_of(d)
+            return T[src][:, w * q:w * q + w]
+        calls = []
+        for h, m_in, d, _ in over:
+            rid, pid = topo.addr(h, core)
+            calls.append(RemoteDMATransfer(dst_ids=[DstId(rid=rid, pnc=pid)], dma_engine_mask=m_in, remote_sem=T.sem["hop" + k],
+                                           src=block(d), dst=T["r" + k][:]))
+            sent[0] += bits(m_in)
+        g.remote_dma_fused(calls, local_sem=T.sem.loc)
+        calls = []
+        for d, m in straight:
+            rid, pid = topo.addr(d, core)
+            calls.append(RemoteDMATransfer(dst_ids=[DstId(rid=rid, pnc=pid)], dma_engine_mask=m, remote_sem=T.sem["arr" + k],
+                                           src=block(d), dst=T[land][:, c0 + w * rank:c0 + w * rank + w]))
+            sent[0] += bits(m)
+        g.remote_dma_fused(calls, local_sem=T.sem.loc)
+
+    def arrive(k):
+        n = 0
+        for c in T.cores:
+            if c != core:
+                near, far = plan(c, T, topo)
+                n += sum(bits(m) for d, m in near if d == core) + sum(bits(m) for _, _, d, m in far if d == core)
+        _, land, c0, w = EXCH[k]
+        totals["arr" + k] = n
+        note("net", [], [(land, c0, c0 + w * N)], ("arr" + k, n))
+
+    def alias(land, src):
+        sc((land, GH + C * rank, GH + C * rank + C), (src, C * rank, C * rank + C))
+
+    base = rank * V
+    own = (2 * rank, 2 * rank + 2)
+    dma("y", "bl", T.bli[:], T.bl[:], [], [("bli", 0, 16)])
+    for d in range(D):
+        dma("s" if d == 1 else "y", "w%d" % d, T.wa[:, 128 * d:128 * d + 128], T.w[:, V * d:V * d + V], [],
+            [("wa", 128 * d, 128 * d + 128)])
+    dma("s", "nb", T.nbi[:], T.nb[:], [], [("nbi", 0, 384)])
+    dma("y", "x", T.xe[:, 0:V], T.x[:], [], [("xe", 0, V)])
+
+    iota(("pi", 0, 1), [[1, 1]], 0, 1)
+    iota(("xi", 0, 160), [[1, 160]], 0, 0)
+    iota(("rt", 0, 512), [[1, 512]], base, 0)
+    iota(("gm", 0, 128), [[16, 8], [0, 16]], 0, 0)
+    iota(("jm", 0, 256), [[0, 16], [1, 16]], 0, 0)
+    iota(("kk", 0, 16), [[-C, N], [0, 2]], 40 * rank + 1 - GH, 0)
+    iota(("hl", 0, 1024), [[1, 8], [0, 128]], 16 * rank, 0)
+
+    def col(i):
+        return ("pc", i, i + 1)
+
+    def a(name, i=0):
+        return (name, 128 * i, 128 * i + 128)
+    ts(("pi", 2, 3), ("pi", 0, 1), 4, A.arith_shift_right, 1, A.bitwise_and)
+    ts(("pi", 1, 2), ("pi", 0, 1), 15, A.bitwise_and)
+    ts(col(1), ("pi", 0, 1), 16, A.add)
+    cp(col(3), ("pi", 2, 3))
+    ts(col(2), ("pi", 2, 3), -1, A.mult, 1, A.add)
+    ts(("s0", 0, 160), ("xi", 0, 160), col(1), A.is_equal, col(2), A.mult)
+    ts(("s1", 0, 160), ("xi", 0, 160), col(1), A.is_equal, col(3), A.mult)
+    cp(col(4), ("pi", 1, 2))
+    tt(col(5), ("pi", 0, 1), ("pi", 1, 2), A.subtract)
+    run("v", [], [("zz", 0, 16)], lambda: g.vector.memset(T.zz[:], 0))
+    ts(("id16", 0, 16), ("xi", 0, 16), col(4), A.is_equal)
+    for k in ("1", "3"):
+        dma("y", "z" + k, T["lr" + k][:, own[0]:own[1]], T.zz[:, 0:2], [("zz", 0, 2)], [("lr" + k,) + own])
+    for i in range(1, 4):
+        sa(("rt", 512 * i, 512 * i + 512), ("rt", 0, 512), 1, 512 * i)
+    sa(("rt", NONE, NONE + 8), ("rt", 0, 8), 0, -1)
+    run("v", [("wa", 0, 384)], [("tr", 0, 384)], lambda: g.vector.transpose(T.tr[:], T.wa[:]))
+    for d in range(D):
+        grp = []
+        for i in range(8):
+            b, h = i // 2, i % 2
+            for gg in range(2):
+                st = 16 - 16 * (gg - h)
+                grp.append((("a0", 128 * d + i, 128 * d + 128, 8), ("s%d" % h, st, st + 128),
+                            ("tr", 128 * d + 32 * b + 16 * gg, 128 * d + 32 * b + 16 * gg + 16), gg == 0, gg == 1))
+        mm(grp)
+    cp(("nbf", 0, 384), ("nbi", 0, 384))
+    sc(("v0", 0, 384), ("nbf", 0, 384))
+    nb, nbp = [a("nbf", d) for d in range(D)], [a("v0", d) for d in range(D)]
+    cp(("blo", 0, 16), ("bli", 0, 16))
+    ts(("bms", 0, 16), ("bli", 0, 16), 15, A.bitwise_and)
+    ts(("bsh", 0, 16), ("bli", 0, 16), 4, A.arith_shift_right)
+    cp(("bmo", 0, 16), ("bms", 0, 16))
+    for d in range(D):
+        ts(("boff", 16 * d, 16 * d + 16), ("bsh", 0, 16), 128 * d, A.add)
+    ts(col(6), col(5), 15, A.add)
+    sc(("bmask", 0, 256), ("ind", ("id16", 0, 16), ("bmo", 0, 16)))
+    sc(("gbb", 0, 256), ("ind", ("rt", 0, V), ("blo", 0, 16)))
+    sa(("g40", 0, 320), ("rt", 0, 320), 0, -1)
+    for q in range(N):
+        sc(("g40", 40 * q + 1, 40 * q + 33), ("gbb", C * q, C * q + C))
+    sa(("rt", GH, NONE), ("rt", 0, 256), 0, -1)
+    alias("rt", "gbb")
+    sc(("xb", 0, 256), ("ind", ("xe", 0, V), ("blo", 0, 16)))
+    send("X")
+    alias("xe", "xb")
+    sc(("gw", 0, 1024), ("rt", 1024, V))
+    ts(("eall", 0, 143), ("xi", 0, 143), col(6), A.is_equal)
+    ts(a("gf"), a("gm"), col(5), A.is_equal)
+    tt(a("dn"), nb[1], nbp[0], A.subtract)
+    tt(a("v1", 3), nb[0], nbp[1], A.add)
+    cp(a("w1s"), a("a0", 1))
+    tt(a("v1", 0), a("w1s"), a("a0", 0), A.is_gt)
+    tt(a("wm"), a("w1s"), a("a0", 0), A.max)
+    tt(a("ta"), a("dn"), a("v1", 0), A.mult)
+    tt(a("v1", 1), a("a0", 2), a("wm"), A.is_gt)
+    tt(a("tb"), a("ta"), nbp[0], A.add)
+    tt(a("tc"), nbp[2], a("tb"), A.subtract)
+    tt(a("v1", 2), a("tc"), a("v1", 1), A.mult)
+    tt(a("pa"), a("tb"), a("v1", 2), A.add)
+
+    def border(d):
+        tt(("pg", 256 * d, 256 * d + 256), ("ind", ("pa", 0, 384 if d else 128), ("boff", 16 * d, 16 * d + 16)),
+           ("bmask", 0, 256), A.mult)
+    border(0)
+    mm([(("a1", 0, 256), a("gf"), ("pg", 0, 256), True, True)])
+    cp(a("po"), a("pa"))
+    ts(("m16", 0, 256), ("jm", 0, 256), col(4), A.is_equal)
+    ts(("m0", 0, 256), ("jm", 0, 256), 0, A.is_gt)
+    tt(("bs", 0, 256), ("m16", 0, 256), ("a1", 0, 256), A.mult)
+    run("v", [("m0", 0, 256), ("bs", 0, 256)], [("pg", 0, 256)],
+        lambda: g.vector.tensor_tensor_scan(T.pg[:, 0:256], T.m0[:], T.bs[:], 0.0, A.mult, A.add))
+
+    def name_slots(out, src):
+        tt(("kt", 0, 16), src, ("kk", 0, 16), A.add)
+        ts((out, 0, 16), ("kt", 0, 16), 40 * rank, A.max, 40 * rank + 33, A.min)
+    name_slots("ro1", ("pg", 15, 256, 16))
+    send("1")
+    iota(("hl", 1024, V), [[1, 8], [0, 128]], 16 * rank + 8, 0)
+    iota(("hl", GH, NONE), [[16, N], [0, C]], 0, 0)
+    iota(("va", 0, 128), [[16, 128]], base, 1)
+    iota(("lo", 0, 128), [[1, 128]], 0, 0)
+    cp(("t1", 0, 1024), ("ind", ("rt", 0, NONE + 8), ("po", 0, 64)))
+    sc(("t1", 1024, V), ("ind", ("rt", 0, NONE + 8), ("po", 64, 128)))
+    cp(("bpo", 0, 16), ("pg", 15, 256, 16))
+    cp(("bp", 0, 16), ("pg", 15, 256, 16))
+    sc(("x2", 0, V), ("xe", 0, V))
+    tt(a("wl"), a("w1s"), a("a0", 0), A.min)
+    tt(a("ta"), a("v1", 3), a("tb"), A.subtract)
+    tt(a("v1", 0), a("a0", 2), a("wl"), A.is_gt)
+    tt(a("tc"), nbp[2], a("ta"), A.subtract)
+    tt(a("v1", 3), nb[2], a("v1", 3), A.add)
+    tt(a("te"), a("tc"), a("v1", 0), A.mult)
+    tt(a("v1", 3), a("v1", 3), a("pa"), A.subtract)
+    tt(a("pa", 2), nbp[2], a("te"), A.subtract)
+    tt(a("pa", 1), a("v1", 3), a("pa", 2), A.subtract)
+    border(1)
+    border(2)
+    to_a("a2", 0, 32, "eall", "pg", 256)
+    ts(col(7), col(4), 0, A.is_equal)
+    ts(col(8), col(4), 1, A.is_equal)
+    ts(("e1", 0, 143), ("xi", 0, 143), col(6), A.is_equal, col(7), A.mult)
+    ts(("nbo", 0, 384), ("nbf", 0, 384), 0, A.add)
+
+    def resolve(land, tab):
+        sc((tab, GH, NONE), ("ind", ("g40", 0, 320), (land, 0, 16)))
+        sc((tab, GH + C * rank, GH + C * rank + C), ("ind", (tab, 0, V), ("blo",) + own))
+    arrive("1")
+    resolve("lr1", "t1")
+    tt(("m1b", 0, 256), ("ind", ("t1", 0, NONE), ("bpo", 0, 16)), ("gbb", 0, 256), A.is_equal)
+    send("2")
+
+    def mutual(out, tab, lst, width, a0, a1):
+        sc(("gs", 0, 1024), ("ind", (tab, 0, width), (lst, 64, 128)))
+        tt((out, 0, 1024), ("ind", (tab, 0, width), (lst, 0, 64)), ("rt", 0, 1024), A.is_equal)
+        to_a(a0[0], a0[1], 64, "e1", out, 0)
+        tt((out, 1024, V), ("gs", 0, 1024), ("gw", 0, 1024), A.is_equal)
+        to_a(a1[0], a1[1], 64, "e1", out, 1024)
+    mutual("m1", "t1", "po", NONE, ("a3", 0), ("a3", 64))
+    alias("m1", "m1b")
+    sa(a("da", 2), a("pa", 2), -1, NONE)
+    sa(("lo", GH, NONE), ("rt", 0, 256), 0, 0)
+    for n in (128, 256, 512, 1024):
+        sc(("lo", n, 2 * n), ("lo", 0, n))
+    dma("y", "lo", T.hl[1::16, 0:NONE], T.lo[1::16, 0:NONE], [("lo", 0, NONE)], [("hl", 0, NONE)])
+    cp(("po", 256, 384), a("pa", 2))
+    cp(("bpo", 16, 48), ("a2", 0, 32))
+    cp(("bp", 16, 48), ("a2", 0, 32))
+    cp(("bpo", 48, 64), ("blo", 0, 16))
+    cp(("po", 128, 256), a("pa", 1))
+    tt(("db", 0, 16), ("bp", 16, 32), ("bp", 0, 16), A.subtract)
+    tt(("db", 16, 32), ("bp", 32, 48), ("bp", 16, 32), A.subtract)
+    sa(("db", 32, 48), ("bp", 32, 48), -1, NONE)
+    tt(a("ta"), a("pa", 1), a("pa", 0), A.subtract)
+    tt(a("v1", 0), a("pa", 2), a("pa", 1), A.subtract)
+    ts(a("v1", 1), a("a3"), -1, A.mult, 1, A.add)
+    tt(a("v1", 2), a("ta"), a("v1", 1), A.mult)
+    for c in range(16):
+        dma("y", "wb", T.wb[c::16, :], T.w[:], [("m1", 0, V)], [])
+    note("y", [], [("wb", 0, 6144)], ("dwb", totals["dwb"]))
+    arrive("2")
+    fl = ("m1", 0, NONE)
+    sc(("fb", 0, 1024), ("ind", fl, ("bpo", 0, 64)))
+    to_a("a0", 0, 64, "e1", "fb")
+
+    def flags(eng, f, d, h):
+        eng((f, 1024 * h, 1024 * h + 1024), ("ind", fl, ("po", 128 * d + 64 * h, 128 * d + 64 * h + 64)))
+
+    def ps16(i):
+        return ("a0", 16 * i, 16 * i + 16)
+
+    def b16(n, i):
+        return (n, 16 * i, 16 * i + 16)
+    ub, ua = ("ub", 0, 16), a("ua")
+    flags(cp, "f3", 2, 0)
+    flags(sc, "f1", 0, 0)
+    to_a("a1", 0, 64, "e1", "f3", 0)
+    flags(cp, "f3", 2, 1)
+    to_a("a3", 0, 64, "e1", "f1", 0)
+    to_a("a1", 64, 64, "e1", "f3", 1024)
+    ts(("qb", 0, 16), ps16(3), -1, A.mult, 1, A.add)
+    tt(ub, ps16(2), b16("db", 2), A.mult)
+    tt(ub, ub, b16("db", 1), A.add)
+    tt(ub, ub, ps16(1), A.mult)
+    tt(ub, ub, b16("db", 0), A.add)
+    tt(ub, ub, ps16(0), A.mult)
+    tt(ub, ub, ("qb", 0, 16), A.mult)
+    tt(ub, ub, b16("bp", 0), A.add)
+    name_slots("ro3", ub)
+    send("3")
+    cp(("pcb", 0, 16), ub)
+    flags(sc, "f2", 1, 0)
+    flags(sc, "f2", 1, 1)
+    flags(sc, "f1", 0, 1)
+    to_a("a2", 0, 64, "e1", "f2", 0)
+    to_a("a2", 64, 64, "e1", "f2", 1024)
+    to_a("a3", 64, 64, "e1", "f1", 1024)
+    tt(ua, a("a1"), a("da", 2), A.mult)
+    tt(ua, ua, a("v1", 0), A.add)
+    tt(ua, ua, a("v1", 1), A.mult)
+    sa(("xe", NONE, EXT), ("rt", 0, 16), 0, 0)
+    arrive("X")
+    sc(("xcb", 0, 256), ("ind", ("xe", 0, EXT), ("pcb", 0, 16)))
+    sc(("a1", 0, 256), ("xcb", 0, 256))
+    sc(("a1", 256, 512), ("xb", 0, 256))
+    sa(("t2", NONE, NONE + 8), ("rt", 0, 8), 0, -1)
+    ts(a("va"), a("va"), col(5), A.subtract)
+    ts(a("gn"), a("gm"), col(5), A.is_equal)
+    ts(col(9), col(7), 128, A.mult)
+    ts(a("va2"), a("va"), V - base, A.add)
+    tt(col(10), col(8), col(9), A.add)
+    ts(a("go"), a("gn"), -1, A.mult)
+    run("g", [a("go")], [a("nt")], lambda: g.affine_select(T.nt[:], T.go[:], [[-1, 128]], A.is_ge, 0.0, 0, 1))
+    ts(("ehl", 0, 143), ("xi", 0, 143), col(6), A.is_equal, col(10), A.mult)
+    ts(a("idf"), ("xi", 16, 144), col(1), A.is_equal)
+    tt(ua, ua, a("a2"), A.mult)
+    tt(ua, ua, a("v1", 2), A.add)
+    tt(a("v1", 3), ua, a("a3"), A.mult)
+    tt(a("pcf"), a("pa"), a("v1", 3), A.add)
+    cp(a("pco"), a("pcf"))
+    full = ("rt", 0, NONE + 8)
+    cp(("t2", 0, 1024), ("ind", full, ("pco", 0, 64)))
+    sc(("t2", 1024, V), ("ind", full, ("pco", 64, 128)))
+    arrive("3")
+    resolve("lr3", "t2")
+    tt(("mb", 0, 256), ("ind", ("t2", 0, NONE + 8), ("pcb", 0, 16)), ("gbb", 0, 256), A.is_equal)
+    tt(("xm", 0, 256), ("mb", 0, 256), ("a1", 0, 256), A.mult)
+    tt(("xxb", 0, 256), ("xm", 0, 256), ("a1", 256, 512), A.add)
+    send("4")
+    mutual("mm", "t2", "pco", NONE + 8, ("a0", 0), ("a2", 0))
+    sa(a("pz"), a("pcf"), 1, -NONE)
+    sa(("hl", NONE, EXT), ("rt", 0, 16), 0, 0)
+    sc(("hl", GH + C * rank, GH + C * rank + C), ("ind", ("hl", 0, V), ("blo",) + own))
+    alias("xx", "xxb")
+    sc(("hg", 0, V), ("ind", ("hl", 0, EXT), ("pco", 0, 128)))
+    to_a("a3", 0, 128, "ehl", "hg")
+    sa(a("ones"), ("rt", 0, 128), 0, 1)
+    for h, ma in ((0, ("a0", 0, 64)), (1, ("a2", 0, 64))):
+        c0, c1 = 64 * h, 64 * h + 64
+        tt(("mt", c0, c1), ("pz", c0, c1), ma, A.mult)
+        ts(("mo", c0, c1), ("mt", c0, c1), NONE, A.add)
+        tt(("xx", 1024 * h, 1024 * h + 1024), ("ind", ("xe", 0, EXT), ("mo", c0, c1)), ("x2", 1024 * h, 1024 * h + 1024), A.add)
+
+    def weights(bank, d, lo, n):
+        sc((bank, 0, n), ("wb", V * d + lo, V * d + lo + n))
+    weights("gw", 2, 0, 1024)
+    weights("v0", 2, 1024, 512)
+    tt(a("gt"), a("a3"), a("va"), A.is_gt)
+    tt(("rep", 0, 64), ("gt", 0, 64), ("a0", 0, 64), A.is_ge)
+    tt(("rep", 64, 128), ("gt", 64, 128), ("a2", 0, 64), A.is_ge)
+    weights("a0", 2, 1536, 512)
+    weights("a2", 1, 1024, 512)
+    mm([(a("a1"), a("gn"), a("rep"), True, True)])
+    mm([(a("a3"), a("nt"), a("rep"), True, True)])
+    ts(a("v1", 1), a("rep"), -1, A.mult, 1, A.add)
+    tt(a("lt"), a("pz"), a("v1", 1), A.mult)
+    ts(a("lam"), a("lt"), NONE, A.add)
+    run("v", [a("ones"), a("a1")], [a("inc")],
+        lambda: g.vector.tensor_tensor_scan(T.inc[:], T.ones[:], T.a1[:, 0:128], 0.0, A.mult, A.add))
+    tt(a("nn"), a("inc"), a("a3"), A.add)
+    arrive("4")
+
+    def prod(buf, d, h):
+        tt((buf, 1024 * h, 1024 * h + 1024), ("ind", ("xx", 0, NONE), ("nbo", 128 * d + 64 * h, 128 * d + 64 * h + 64)),
+           ("wb", V * d + 1024 * h, V * d + 1024 * h + 1024), A.mult)
+
+    def gather(buf, d, h):
+        sc((buf, 1024 * h, 1024 * h + 1024), ("ind", ("xx", 0, NONE), ("nbo", 128 * d + 64 * h, 128 * d + 64 * h + 64)))
+    gather("p3", 2, 1)
+    weights("a3", 1, 1536, 512)
+    gather("p2", 1, 1)
+    gather("p3", 2, 0)
+    prod("p1", 0, 0)
+    prod("p1", 0, 1)
+    cp(a("no"), a("nn"))
+    tt(a("rho"), a("va2"), a("nn"), A.subtract)
+    sa(a("rn"), a("nn"), 1, base)
+    tt(a("v1", 0), a("rho"), a("v1", 1), A.mult)
+    tt(a("rho"), a("nn"), a("v1", 0), A.add)
+    cp(a("rhoo"), a("rho"))
+    sa(("nx", NONE, EXT), ("rt", 0, 16), 0, 0)
+    sc(("nx", 0, V), ("ind", ("hl", 0, V), ("no", 0, 128)))
+    sc(("nxb", 0, 256), ("ind", ("nx", 0, V), ("blo", 0, 16)))
+    send("6")
+    alias("nx", "nxb")
+    sa(("lw", 0, V), ("rt", 0, V), 0, -1)
+    last = (1536, V)
+    tt(("p3",) + last, ("p3",) + last, ("a0", 0, 512), A.mult)
+    tt(("p2",) + last, ("p2",) + last, ("a3", 0, 512), A.mult)
+    mm([(("v1", 0, 512), a("idf"), (p,) + last, p == "p1", p == "p3") for p in ("p1", "p2", "p3")])
+    prod("p2", 1, 0)
+    for lo, n, bank, w1 in ((0, 1024, "gw", None), (1024, 512, "v0", "a2")):
+        acc = (bank, 0, n)
+        tt(acc, ("p3", lo, lo + n), acc, A.mult)
+        if w1:
+            tt(("p2", lo, lo + n), ("p2", lo, lo + n), (w1, 0, n), A.mult)
+        tt(acc, ("p2", lo, lo + n), acc, A.add)
+        tt(("sx", lo, lo + n), ("p1", lo, lo + n), acc, A.add)
+    sc(("sx",) + last, ("v1", 0, 512))
+    sc(("sb", 0, 256), ("ind", ("sx", 0, V), ("blo", 0, 16)))
+    send("5")
+    alias("sx", "sb")
+    sc(("p3", 0, 1024), ("sx", 0, 1024))
+    sc(("gw", 0, 1024), ("sx", 1024, V))
+    sa(("sx", NONE, NONE + 8), ("rt", 0, 8), 0, 0)
+    sa(("sp", 0, 8), ("rt", 0, 8), 0, 0)
+    tt(a("cmf"), a("rn"), a("rep"), A.mult)
+    run("v", [("hl", 0, V)], [("ind", ("lw", 0, 2 * V), ("rhoo", 0, 128))],
+        lambda: g.vector.tensor_copy(ap(("ind", ("lw", 0, 2 * V), ("rhoo", 0, 128))), T.hl[:, 0:V]))
+    to_a("a3", 0, 128, "ehl", "lw")
+    arrive("6")
+    sc(("cg", 0, V), ("ind", ("nx", 0, EXT), ("lam", 0, 128)))
+    to_a("a1", 0, 128, "ehl", "cg")
+    arrive("5")
+    sc(("p1", 1024, V), ("ind", ("sx", 0, NONE + 8), ("mo", 64, 128)))
+    tt(("sp", 8, 1032), ("ind", ("sx", 0, NONE + 8), ("mo", 0, 64)), ("p3", 0, 1024), A.add)
+    tt(("sp", 1032, V + 8), ("p1", 1024, V), ("gw", 0, 1024), A.add)
+    ts(a("l1"), a("a3"), 8 - base, A.add, 0, A.max)
+    for i in range(8):
+        (sc if i % 2 else cp)(("yy", 256 * i, 256 * i + 256), ("ind", ("sp", 0, V + 8), ("l1", 16 * i, 16 * i + 16)))
+    for i in range(8):
+        dma("y", "y%d" % i, T.y[:, 256 * i:256 * i + 256], T.yy[:, 256 * i:256 * i + 256], [("yy", 256 * i, 256 * i + 256)], [])
+    tt(a("cmf"), a("cmf"), a("a1"), A.add)
+    dma("y", "cm", T.cm[:], T.cmf[:], [a("cmf")], [])
+    need("g", [("loc", sent[0])] + [(s, count[s]) for s in ("v", "s", "t", "p")] + sorted(totals.items()))

@@ -2,8 +2,15 @@ from concourse.mybir import AluOpType, ActivationFunctionType
 from concourse.bass import DstId, RemoteDMATransfer
 
 N, V, C, D = 8, 2048, 32, 3
-GH, NONE = V, V + N * C
-EXT = NONE + 16
+L = V + N * C
+O = 16
+W = O + L
+STEP, GONE, KEEP = 4096, 16384, 32768
+REP0 = 2080
+XV = 1280
+NXV = 768
+Q = 512
+LISTS = "gm gf idf six va vo w0s w1s wm ta tb tc pa c32 zf ua mt lamf inc nnx rmin lamx".split()
 
 
 def buffers(*groups):
@@ -15,25 +22,29 @@ def buffers(*groups):
 
 
 SCRATCH = buffers(
-    ("bli bsh bms", 16, "int32"), ("nbi", 384, "int32"), ("pi", 8, "int32"),
-    ("wa tr", 384, "bfloat16"), ("wb", 6144, "bfloat16"), ("s0 s1", 160, "bfloat16"), ("e1 ehl", 144, "bfloat16"),
-    ("gn go nt rep", 128, "bfloat16"), ("xe hl m1 nx", EXT, "bfloat16"), ("lo", NONE, "bfloat16"),
-    ("xb m1b nxb", 256, "bfloat16"), ("fb", 1024, "bfloat16"), ("f1 f2 f3 mm hg cg x2", V, "bfloat16"),
-    ("lw", 2 * V, "bfloat16"), ("rX r2 r6", C, "bfloat16"),
-    ("blo pcb bmo ro1 ro3 lr1 lr3 zz", 16, "uint16"), ("r1 r3", 2, "uint16"), ("boff", 48, "uint16"), ("bpo", 64, "uint16"),
-    ("pco mo lam no rhoo l1", 128, "uint16"), ("nbo po", 384, "uint16"),
-    ("pc ub qb id16 kk kt", 16, "float32"), ("r4 r5", C, "float32"), ("g40", 320, "float32"), ("bp db", 48, "float32"),
-    ("xi", 160, "float32"), ("eall", 144, "float32"), ("gm gf idf ones va va2 w1s wm wl dn ta tb tc te", 128, "float32"),
-    ("ua pcf gt pz mt lt inc nn rho rn cmf", 128, "float32"), ("nbf pa da", 384, "float32"),
-    ("jm m16 m0 bs gbb bmask xcb mb xm xxb sb", 256, "float32"), ("pg", 768, "float32"), ("gs", 1024, "float32"),
-    ("rt t1 t2 xx sx", EXT, "float32"), ("p1 p2 p3 yy", V, "float32"), ("sp", V + 8, "float32"))
-PSUM = {"gw": 1024, "v0": 512, "v1": 512, "a0": 512, "a1": 512, "a2": 512, "a3": 512}
+    ("bli bsh bms ubi ubj", 16, "int32"), ("nbi", 384, "int32"), ("pi", 8, "int32"), ("bki bkj", 48, "int32"),
+    ("ui uj", 128, "int32"),
+    ("wa", 384, "bfloat16"), ("w8", 6144, "bfloat16"), ("s0 s1", 160, "bfloat16"), ("e1n ehl", 144, "bfloat16"),
+    ("gn nt nr g10 g20 g21 idb idp idn pair sel8", 128, "bfloat16"), ("xe hl t2", W, "bfloat16"), ("m1 nx", L, "bfloat16"),
+    ("xb m1b nxb hlb eqb hgh", 256, "bfloat16"), ("g48h", 400, "bfloat16"), ("fb xg", 768, "bfloat16"),
+    ("f0 f1 f2 g5 cg", V, "bfloat16"), ("x2", XV, "bfloat16"), ("lw", REP0 + V, "bfloat16"), ("rX r2 r6", C, "bfloat16"),
+    ("blo pcb bmo ro1 ro3 lr1 lr3 zz bpo", 16, "uint16"), ("r1 r3", 2, "uint16"), ("boff bnb", 48, "uint16"),
+    ("blo48", 26, "uint16"), ("po pco mo lam no rhoo l1", 128, "uint16"), ("nbo", 384, "uint16"),
+    ("pc", 24, "float32"), ("ub zb cb id16 kk kk3 kt bc", 16, "float32"), ("r4 r5", C, "float32"), ("g48", 400, "float32"),
+    ("bkf", 48, "float32"), ("xi", 160, "float32"), ("eall", 144, "float32"),
+    ("cmf", 128, "float32"), ("lists", 128 * len(LISTS), "float32"),
+    ("nbf ks", 384, "float32"), ("jm m16 m0 bs pgs gbb bmask xcb xm xxb sb", 256, "float32"), ("pg", 768, "float32"),
+    ("gs", 1024, "float32"), ("rt t1 xx", L, "float32"), ("sx", W, "float32"), ("p0 p1 p2 yy", V, "float32"),
+    ("sp", V + 8, "float32"))
+PSUM = {"q%d" % i: 1024 for i in range(4)}
 for _n in PSUM:
     SCRATCH[_n] = ("psum", [128, PSUM[_n]], "float32")
-EXCH = {"X": ("xb", "xe", GH, C), "1": ("ro1", "lr1", 0, 2), "2": ("m1b", "m1", GH, C), "3": ("ro3", "lr3", 0, 2),
-        "4": ("xxb", "xx", GH, C), "6": ("nxb", "nx", GH, C), "5": ("sb", "sx", GH, C)}
+SCRATCH["tr"] = ("sbuf", [128, D, 128], "bfloat16")
+ROWS8 = ("w8", "sel8")
+EXCH = {"X": ("xb", "xe", O + V, C), "1": ("ro1", "lr1", 0, 2), "2": ("m1b", "m1", V, C), "3": ("ro3", "lr3", 0, 2),
+        "4": ("xxb", "xx", V, C), "6": ("nxb", "nx", V, C), "5": ("sb", "sx", O + V, C)}
 ORDER = ["X", "1", "2", "3", "4", "6", "5"]
-DMAS = ["bl", "z1", "z3", "nb", "w0", "w1", "w2", "x", "wb", "lo", "cm"] + ["y%d" % i for i in range(8)]
+DMAS = ["bl", "z1", "z3", "nb", "w0", "w1", "w2", "x", "x2", "w8", "sel", "cm"] + ["y%d" % i for i in range(4)]
 SEMAPHORES = (["v", "s", "t", "p", "loc", "rloc"] + ["d" + n for n in DMAS] + ["arr" + k for k in ORDER]
               + ["hop" + k for k in ORDER])
 
@@ -86,7 +97,7 @@ def rank_program(g, core, T, topo):
         hop_program(g, core, T, topo)
         return
     A = AluOpType
-    COPY, IDENT = ActivationFunctionType.Copy, ActivationFunctionType.Identity
+    COPY, IDENT, SIGN = ActivationFunctionType.Copy, ActivationFunctionType.Identity, ActivationFunctionType.Sign
     q_of = {"v": g.vector, "s": g.scalar, "t": g.tensor, "g": g, "y": g.sync}
     count = {"v": 0, "s": 0, "t": 0, "p": 0}
     waited = {"v": {}, "s": {}, "t": {}, "g": {}, "y": {}}
@@ -124,6 +135,13 @@ def rank_program(g, core, T, topo):
         if r[0] == "ind":
             return ap(r[1]).indirect(ap(r[2]))
         name, lo, hi = r[0], r[1], r[2]
+        if name in LISTS:
+            c0 = 128 * LISTS.index(name)
+            return T.lists[:, c0 + lo:c0 + hi]
+        if name == "tr":
+            return T.tr[:, :, lo:hi]
+        if name in ROWS8:
+            return T[name][0:8, lo:hi]
         return T[name][:, lo:hi] if len(r) == 3 else T[name][:, lo:hi:r[3]]
 
     def regs(rs):
@@ -165,11 +183,18 @@ def rank_program(g, core, T, topo):
     def cp(out, a):
         run("v", [a], [out], lambda: g.vector.tensor_copy(ap(out), ap(a)))
 
+    def fill(out, c):
+        run("v", [], [out], lambda: g.vector.memset(ap(out), c))
+
+    def scan(out, d0, d1, first, op0, op1):
+        run("v", [d0, d1, first], [out], lambda: g.vector.tensor_tensor_scan(ap(out), ap(d0), ap(d1), val(first), op0, op1))
+
     def sc(out, a):
         run("s", [a], [out], lambda: g.scalar.activation(ap(out), ap(a), COPY))
 
-    def sa(out, a, scale, bias):
-        run("s", [a], [out], lambda: g.scalar.activation(ap(out), ap(a), IDENT, bias=float(bias), scale=float(scale)))
+    def sa(out, a, scale, bias, func=IDENT):
+        sv, bv = [ap(z) if isinstance(z, tuple) else float(z) for z in (scale, bias)]
+        run("s", [a, scale, bias], [out], lambda: g.scalar.activation(ap(out), ap(a), func, bias=bv, scale=sv))
 
     def iota(out, pattern, base, ch):
         run("g", [], [out], lambda: g.iota(ap(out), pattern, base, ch, allow_small_or_imprecise_dtypes=True))
@@ -185,9 +210,16 @@ def rank_program(g, core, T, topo):
         ins.then_inc(T.sem.t, 1)
         note("t", list(dict.fromkeys(rd)), list(dict.fromkeys(wr)), ("t", count["t"]))
 
-    def to_a(ps, c0, n, lhs, src, base=0):
-        mm([((ps, c0, c0 + n), (lhs, 15 - k, 143 - k), (src, base + k, base + 16 * n, 16), k == 0, k == 15)
-            for k in range(16)])
+    def msum(out, terms):
+        mm([(out, l, r, i == 0, i == len(terms) - 1) for i, (l, r) in enumerate(terms)])
+
+    def bank(k, lo=0, n=Q):
+        c0 = Q * (k % 2) + lo
+        return ("q%d" % (k // 2), c0, c0 + n)
+
+    def to_a(out, lhs, src, base=0, onto=False):
+        n = out[2] - out[1]
+        mm([(out, (lhs, 15 - k, 143 - k), (src, base + k, base + 16 * n, 16), k == 0 and not onto, k == 15) for k in range(16)])
 
     def dma(queue, sem, out, in_, reads, writes):
         need(queue, deps(queue, reads, writes))
@@ -230,31 +262,36 @@ def rank_program(g, core, T, topo):
         totals["arr" + k] = n
         note("net", [], [(land, c0, c0 + w * N)], ("arr" + k, n))
 
-    def alias(land, src):
-        sc((land, GH + C * rank, GH + C * rank + C), (src, C * rank, C * rank + C))
-
-    base = rank * V
-    own = (2 * rank, 2 * rank + 2)
-    dma("y", "bl", T.bli[:], T.bl[:], [], [("bli", 0, 16)])
-    for d in range(D):
-        dma("s" if d == 1 else "y", "w%d" % d, T.wa[:, 128 * d:128 * d + 128], T.w[:, V * d:V * d + V], [],
-            [("wa", 128 * d, 128 * d + 128)])
-    dma("s", "nb", T.nbi[:], T.nb[:], [], [("nbi", 0, 384)])
-    dma("y", "x", T.xe[:, 0:V], T.x[:], [], [("xe", 0, V)])
-
-    iota(("pi", 0, 1), [[1, 1]], 0, 1)
-    iota(("xi", 0, 160), [[1, 160]], 0, 0)
-    iota(("rt", 0, 512), [[1, 512]], base, 0)
-    iota(("gm", 0, 128), [[16, 8], [0, 16]], 0, 0)
-    iota(("jm", 0, 256), [[0, 16], [1, 16]], 0, 0)
-    iota(("kk", 0, 16), [[-C, N], [0, 2]], 40 * rank + 1 - GH, 0)
-    iota(("hl", 0, 1024), [[1, 8], [0, 128]], 16 * rank, 0)
+    def alias(k):
+        src, land, c0, w = EXCH[k]
+        sc((land, c0 + w * rank, c0 + w * rank + w), (src, w * rank, w * rank + w))
 
     def col(i):
         return ("pc", i, i + 1)
 
     def a(name, i=0):
         return (name, 128 * i, 128 * i + 128)
+
+    def ind(win, lo, hi, lst, c0, c1):
+        return ("ind", (win, lo, hi), (lst, c0, c1))
+
+    base = rank * V
+    own = (2 * rank, 2 * rank + 2)
+    mine = (V + C * rank, V + C * rank + C)
+    dma("y", "bl", T.bli[:], T.bl[:], [], [("bli", 0, 16)])
+    for d in range(D):
+        dma("s" if d == 1 else "y", "w%d" % d, T.wa[:, 128 * d:128 * d + 128], T.w[:, V * d:V * d + V], [], [a("wa", d)])
+    dma("y", "x", T.xe[:, O:O + V], T.x[:], [], [("xe", O, O + V)])
+    dma("y", "nb", T.nbi[:], T.nb[:], [], [("nbi", 0, 384)])
+
+    iota(("pi", 0, 1), [[1, 1]], 0, 1)
+    iota(("xi", 0, 160), [[1, 160]], 0, 0)
+    iota(("rt", 0, 512), [[1, 512]], base, 0)
+    iota(("gm", 0, 128), [[16, 8], [0, 16]], 0, 0)
+    iota(("jm", 0, 256), [[0, 16], [1, 16]], 0, 0)
+    iota(("kk", 0, 16), [[-C, N], [0, 2]], 48 * rank + 16 - V, 0)
+    iota(("va", 0, 128), [[16, 128]], base, 1)
+
     ts(("pi", 2, 3), ("pi", 0, 1), 4, A.arith_shift_right, 1, A.bitwise_and)
     ts(("pi", 1, 2), ("pi", 0, 1), 15, A.bitwise_and)
     ts(col(1), ("pi", 0, 1), 16, A.add)
@@ -264,299 +301,330 @@ def rank_program(g, core, T, topo):
     ts(("s1", 0, 160), ("xi", 0, 160), col(1), A.is_equal, col(3), A.mult)
     cp(col(4), ("pi", 1, 2))
     tt(col(5), ("pi", 0, 1), ("pi", 1, 2), A.subtract)
-    run("v", [], [("zz", 0, 16)], lambda: g.vector.memset(T.zz[:], 0))
+    fill(("zz", 0, 16), 0)
     ts(("id16", 0, 16), ("xi", 0, 16), col(4), A.is_equal)
+    ts(a("idf"), ("xi", 16, 144), col(1), A.is_equal)
+    ts(col(6), col(5), 15, A.add)
+    ts(col(7), col(4), 1, A.is_equal)
+    ts(col(8), col(4), 1, A.not_equal)
+    fill(("blo48", 0, 26), V + C * ((rank + 1) % N))
     for k in ("1", "3"):
         dma("y", "z" + k, T["lr" + k][:, own[0]:own[1]], T.zz[:, 0:2], [("zz", 0, 2)], [("lr" + k,) + own])
+    dma("y", "x2", T.x2[:], T.x[:, 0:XV], [], [("x2", 0, XV)])
+    dma("y", "w8", T.w8[0:8, :], T.w[:], [], [("w8", 0, D * V)])
     for i in range(1, 4):
         sa(("rt", 512 * i, 512 * i + 512), ("rt", 0, 512), 1, 512 * i)
-    sa(("rt", NONE, NONE + 8), ("rt", 0, 8), 0, -1)
-    run("v", [("wa", 0, 384)], [("tr", 0, 384)], lambda: g.vector.transpose(T.tr[:], T.wa[:]))
-    for d in range(D):
-        grp = []
-        for i in range(8):
-            b, h = i // 2, i % 2
-            for gg in range(2):
-                st = 16 - 16 * (gg - h)
-                grp.append((("a0", 128 * d + i, 128 * d + 128, 8), ("s%d" % h, st, st + 128),
-                            ("tr", 128 * d + 32 * b + 16 * gg, 128 * d + 32 * b + 16 * gg + 16), gg == 0, gg == 1))
-        mm(grp)
-    cp(("nbf", 0, 384), ("nbi", 0, 384))
-    sc(("v0", 0, 384), ("nbf", 0, 384))
-    nb, nbp = [a("nbf", d) for d in range(D)], [a("v0", d) for d in range(D)]
+    sa(("rt", V, L), ("rt", 0, 256), 0, -1)
     cp(("blo", 0, 16), ("bli", 0, 16))
     ts(("bms", 0, 16), ("bli", 0, 16), 15, A.bitwise_and)
     ts(("bsh", 0, 16), ("bli", 0, 16), 4, A.arith_shift_right)
     cp(("bmo", 0, 16), ("bms", 0, 16))
     for d in range(D):
         ts(("boff", 16 * d, 16 * d + 16), ("bsh", 0, 16), 128 * d, A.add)
-    ts(col(6), col(5), 15, A.add)
-    sc(("bmask", 0, 256), ("ind", ("id16", 0, 16), ("bmo", 0, 16)))
-    sc(("gbb", 0, 256), ("ind", ("rt", 0, V), ("blo", 0, 16)))
-    sa(("g40", 0, 320), ("rt", 0, 320), 0, -1)
-    for q in range(N):
-        sc(("g40", 40 * q + 1, 40 * q + 33), ("gbb", C * q, C * q + C))
-    sa(("rt", GH, NONE), ("rt", 0, 256), 0, -1)
-    alias("rt", "gbb")
-    sc(("xb", 0, 256), ("ind", ("xe", 0, V), ("blo", 0, 16)))
-    send("X")
-    alias("xe", "xb")
-    sc(("gw", 0, 1024), ("rt", 1024, V))
-    ts(("eall", 0, 143), ("xi", 0, 143), col(6), A.is_equal)
     ts(a("gf"), a("gm"), col(5), A.is_equal)
-    tt(a("dn"), nb[1], nbp[0], A.subtract)
-    tt(a("v1", 3), nb[0], nbp[1], A.add)
-    cp(a("w1s"), a("a0", 1))
-    tt(a("v1", 0), a("w1s"), a("a0", 0), A.is_gt)
-    tt(a("wm"), a("w1s"), a("a0", 0), A.max)
-    tt(a("ta"), a("dn"), a("v1", 0), A.mult)
-    tt(a("v1", 1), a("a0", 2), a("wm"), A.is_gt)
-    tt(a("tb"), a("ta"), nbp[0], A.add)
-    tt(a("tc"), nbp[2], a("tb"), A.subtract)
-    tt(a("v1", 2), a("tc"), a("v1", 1), A.mult)
-    tt(a("pa"), a("tb"), a("v1", 2), A.add)
-
-    def border(d):
-        tt(("pg", 256 * d, 256 * d + 256), ("ind", ("pa", 0, 384 if d else 128), ("boff", 16 * d, 16 * d + 16)),
-           ("bmask", 0, 256), A.mult)
-    border(0)
-    mm([(("a1", 0, 256), a("gf"), ("pg", 0, 256), True, True)])
-    cp(a("po"), a("pa"))
     ts(("m16", 0, 256), ("jm", 0, 256), col(4), A.is_equal)
-    ts(("m0", 0, 256), ("jm", 0, 256), 0, A.is_gt)
-    tt(("bs", 0, 256), ("m16", 0, 256), ("a1", 0, 256), A.mult)
-    run("v", [("m0", 0, 256), ("bs", 0, 256)], [("pg", 0, 256)],
-        lambda: g.vector.tensor_tensor_scan(T.pg[:, 0:256], T.m0[:], T.bs[:], 0.0, A.mult, A.add))
+    for d in range(D):
+        run("v", [a("wa", d)], [a("tr")], lambda: g.vector.transpose(T.tr[:, d, :], ap(a("wa", d))))
+    wp = [bank(2, 128 * d, 128) for d in range(D)]
+    grp = []
+    for i in range(8):
+        b, h = i // 2, i % 2
+        for gg in range(2):
+            st = 16 - 16 * (gg - h)
+            grp.append((("q1", i, 384, 8), ("s%d" % h, st, st + 128), ("tr", 32 * b + 16 * gg, 32 * b + 16 * gg + 16),
+                        gg == 0, gg == 1))
+    mm(grp)
+    for j in range(2):
+        cp(("blo48", 1 + j, 25, 3), ("bli", j, 16, 2))
+    ts(("bc", 0, 16), ("xi", 0, 16), col(8), A.mult)
+    ts(col(12), col(8), 16 * rank, A.mult)
+    ts(col(9), col(4), 0, A.is_equal, -GONE, A.mult)
+    ts(("eall", 0, 143), ("xi", 0, 143), col(6), A.is_equal)
+    nb = [("nbi", 128 * d, 128 * d + 128) for d in range(D)]
+    tmp = [bank(6, 128 * i, 128) for i in range(4)]
+    tmq = [bank(5, 128 * i, 128) for i in range(4)]
+    sc(("xb", 0, 256), ind("xe", O, O + V, "blo", 0, 16))
+    send("X")
+    sc(("bmask", 0, 256), ind("id16", 0, 16, "bmo", 0, 16))
+    sa(("m0", 0, 256), ("jm", 0, 256), 1, 0, SIGN)
+    sc(("gbb", 0, 256), ind("rt", 0, V, "blo", 0, 16))
+    sc(("rt",) + mine, ("gbb", C * rank, C * rank + C))
+    cp(a("w1s"), wp[1])
+    tt(a("g10"), a("w1s"), wp[0], A.is_gt)
+    tt(a("wm"), a("w1s"), wp[0], A.max)
+    cp(tmq[0], nb[0])
+    tt(tmp[1], wp[2], a("wm"), A.is_gt)
+    tt(tmp[0], nb[1], tmq[0], A.subtract)
+    tt(tmq[1], nb[2], tmq[0], A.subtract)
+    tt(a("ta"), a("g10"), tmp[0], A.mult)
+    tt(a("tc"), tmq[1], a("ta"), A.subtract)
+    tt(a("tb"), a("ta"), tmq[0], A.add)
+    tt(tmp[2], a("tc"), tmp[1], A.mult)
+    tt(a("pa"), a("tb"), tmp[2], A.add)
 
-    def name_slots(out, src):
-        tt(("kt", 0, 16), src, ("kk", 0, 16), A.add)
-        ts((out, 0, 16), ("kt", 0, 16), 40 * rank, A.max, 40 * rank + 33, A.min)
-    name_slots("ro1", ("pg", 15, 256, 16))
+    def border(src, d):
+        tt(("pg", 256 * d, 256 * d + 256), ind(src[0], src[1], src[2], "boff", 16 * d, 16 * d + 16), ("bmask", 0, 256), A.mult)
+    border(a("pa"), 0)
+    msum(bank(7, 0, 256), [(a("gf"), ("pg", 0, 256))])
+    cp(a("po"), a("pa"))
+    sc(a("w0s"), wp[0])
+    sa(a("idp"), a("idf"), STEP, 0)
+    sa(a("idn"), a("idf"), -STEP, 0)
+    tt(a("g21"), wp[2], a("w1s"), A.is_gt)
+    tt(a("g20"), wp[2], a("w0s"), A.is_gt)
+    signs = ((("idn", "g10"), ("idn", "g20")), (("idp", "g10"), ("idn", "g21")), (("idp", "g20"), ("idp", "g21")))
+    for d in range(D):
+        msum(bank(3, 128 * d, 128), [(a(m), a(z)) for m, z in signs[d]])
+    for d in range(D):
+        ts(a("nbf", d), nb[d], O + STEP * (2 - d), A.add)
+    tt(("bs", 0, 256), ("m16", 0, 256), bank(7, 0, 256), A.mult)
+    scan(("pgs", 0, 256), ("m0", 0, 256), ("bs", 0, 256), 0.0, A.mult, A.add)
+    bp = ("pgs", 15, 256, 16)
+
+    def name_slots(out, src, kk):
+        tt(("kt", 0, 16), src, (kk, 0, 16), A.add)
+        ts((out, 0, 16), ("kt", 0, 16), 48 * rank + 15, A.max, 48 * rank + 48, A.min)
+    name_slots("ro1", bp, "kk")
     send("1")
-    iota(("hl", 1024, V), [[1, 8], [0, 128]], 16 * rank + 8, 0)
-    iota(("hl", GH, NONE), [[16, N], [0, C]], 0, 0)
-    iota(("va", 0, 128), [[16, 128]], base, 1)
-    iota(("lo", 0, 128), [[1, 128]], 0, 0)
-    cp(("t1", 0, 1024), ("ind", ("rt", 0, NONE + 8), ("po", 0, 64)))
-    sc(("t1", 1024, V), ("ind", ("rt", 0, NONE + 8), ("po", 64, 128)))
-    cp(("bpo", 0, 16), ("pg", 15, 256, 16))
-    cp(("bp", 0, 16), ("pg", 15, 256, 16))
-    sc(("x2", 0, V), ("xe", 0, V))
-    tt(a("wl"), a("w1s"), a("a0", 0), A.min)
-    tt(a("ta"), a("v1", 3), a("tb"), A.subtract)
-    tt(a("v1", 0), a("a0", 2), a("wl"), A.is_gt)
-    tt(a("tc"), nbp[2], a("ta"), A.subtract)
-    tt(a("v1", 3), nb[2], a("v1", 3), A.add)
-    tt(a("te"), a("tc"), a("v1", 0), A.mult)
-    tt(a("v1", 3), a("v1", 3), a("pa"), A.subtract)
-    tt(a("pa", 2), nbp[2], a("te"), A.subtract)
-    tt(a("pa", 1), a("v1", 3), a("pa", 2), A.subtract)
-    border(1)
-    border(2)
-    to_a("a2", 0, 32, "eall", "pg", 256)
-    ts(col(7), col(4), 0, A.is_equal)
-    ts(col(8), col(4), 1, A.is_equal)
-    ts(("e1", 0, 143), ("xi", 0, 143), col(6), A.is_equal, col(7), A.mult)
-    ts(("nbo", 0, 384), ("nbf", 0, 384), 0, A.add)
+    sc(a("gn"), a("gf"))
+    dma("y", "sel", T.sel8[0:8, :], T.gn[0::16, :], [a("gn")], [a("sel8")])
+    iota(("hgh", 0, 256), [[16, N], [0, C]], 0, 0)
+    run("g", [a("gn")], [a("nt")], lambda: g.affine_select(T.nt[:], T.gn[:], [[-1, 128]], A.is_gt, 0.0, 0, 1))
+    sc(("t1", 1024, V), ind("rt", 0, L, "po", 64, 128))
+    tt(("ks", 0, 384), ("nbf", 0, 384), bank(3, 0, 384), A.add)
+    for d in range(D):
+        border(("ks", 0, 384), d)
+    to_a(bank(4, 64, 48), "eall", "pg")
+    cp(("t1", 0, 1024), ind("rt", 0, L, "po", 0, 64))
+    cp(("bpo", 0, 16), bp)
+    cp(("t1",) + mine, ("ind", ("t1", 0, V), ("blo",) + own))
+    sc(("g48", 0, 400), ind("rt", 0, L, "blo48", 0, 25))
+    sc(("q0", 0, 1024), ("rt", 1024, V))
+    sa(("hl", O, O + 128), ("xi", 0, 128), col(7), col(12))
+    for i in (1, 2, 4, 8):
+        sa(("hl", O + 128 * i, O + 256 * i), ("hl", O, O + 128 * i), 1, ("bc", i, i + 1))
+    ts(("e1n", 0, 143), ("xi", 0, 143), col(6), A.is_equal, col(9), A.mult)
 
-    def resolve(land, tab):
-        sc((tab, GH, NONE), ("ind", ("g40", 0, 320), (land, 0, 16)))
-        sc((tab, GH + C * rank, GH + C * rank + C), ("ind", (tab, 0, V), ("blo",) + own))
+    def resolve(land, names, tab, c0):
+        for eng, q0, q1 in ((cp, 0, rank), (sc, rank + 1, N)):
+            if q0 < q1:
+                eng((tab, c0 + V + C * q0, c0 + V + C * q1), ind(names, 0, 400, land, 2 * q0, 2 * q1))
     arrive("1")
-    resolve("lr1", "t1")
-    tt(("m1b", 0, 256), ("ind", ("t1", 0, NONE), ("bpo", 0, 16)), ("gbb", 0, 256), A.is_equal)
+    resolve("lr1", "g48", "t1", 0)
+    tt(("m1b", 0, 256), ind("t1", 0, L, "bpo", 0, 16), ("gbb", 0, 256), A.is_equal)
     send("2")
-
-    def mutual(out, tab, lst, width, a0, a1):
-        sc(("gs", 0, 1024), ("ind", (tab, 0, width), (lst, 64, 128)))
-        tt((out, 0, 1024), ("ind", (tab, 0, width), (lst, 0, 64)), ("rt", 0, 1024), A.is_equal)
-        to_a(a0[0], a0[1], 64, "e1", out, 0)
-        tt((out, 1024, V), ("gs", 0, 1024), ("gw", 0, 1024), A.is_equal)
-        to_a(a1[0], a1[1], 64, "e1", out, 1024)
-    mutual("m1", "t1", "po", NONE, ("a3", 0), ("a3", 64))
-    alias("m1", "m1b")
-    sa(a("da", 2), a("pa", 2), -1, NONE)
-    sa(("lo", GH, NONE), ("rt", 0, 256), 0, 0)
-    for n in (128, 256, 512, 1024):
-        sc(("lo", n, 2 * n), ("lo", 0, n))
-    dma("y", "lo", T.hl[1::16, 0:NONE], T.lo[1::16, 0:NONE], [("lo", 0, NONE)], [("hl", 0, NONE)])
-    cp(("po", 256, 384), a("pa", 2))
-    cp(("bpo", 16, 48), ("a2", 0, 32))
-    cp(("bp", 16, 48), ("a2", 0, 32))
-    cp(("bpo", 48, 64), ("blo", 0, 16))
-    cp(("po", 128, 256), a("pa", 1))
-    tt(("db", 0, 16), ("bp", 16, 32), ("bp", 0, 16), A.subtract)
-    tt(("db", 16, 32), ("bp", 32, 48), ("bp", 16, 32), A.subtract)
-    sa(("db", 32, 48), ("bp", 32, 48), -1, NONE)
-    tt(a("ta"), a("pa", 1), a("pa", 0), A.subtract)
-    tt(a("v1", 0), a("pa", 2), a("pa", 1), A.subtract)
-    ts(a("v1", 1), a("a3"), -1, A.mult, 1, A.add)
-    tt(a("v1", 2), a("ta"), a("v1", 1), A.mult)
-    for c in range(16):
-        dma("y", "wb", T.wb[c::16, :], T.w[:], [("m1", 0, V)], [])
-    note("y", [], [("wb", 0, 6144)], ("dwb", totals["dwb"]))
-    arrive("2")
-    fl = ("m1", 0, NONE)
-    sc(("fb", 0, 1024), ("ind", fl, ("bpo", 0, 64)))
-    to_a("a0", 0, 64, "e1", "fb")
-
-    def flags(eng, f, d, h):
-        eng((f, 1024 * h, 1024 * h + 1024), ("ind", fl, ("po", 128 * d + 64 * h, 128 * d + 64 * h + 64)))
-
-    def ps16(i):
-        return ("a0", 16 * i, 16 * i + 16)
-
-    def b16(n, i):
-        return (n, 16 * i, 16 * i + 16)
-    ub, ua = ("ub", 0, 16), a("ua")
-    flags(cp, "f3", 2, 0)
-    flags(sc, "f1", 0, 0)
-    to_a("a1", 0, 64, "e1", "f3", 0)
-    flags(cp, "f3", 2, 1)
-    to_a("a3", 0, 64, "e1", "f1", 0)
-    to_a("a1", 64, 64, "e1", "f3", 1024)
-    ts(("qb", 0, 16), ps16(3), -1, A.mult, 1, A.add)
-    tt(ub, ps16(2), b16("db", 2), A.mult)
-    tt(ub, ub, b16("db", 1), A.add)
-    tt(ub, ub, ps16(1), A.mult)
-    tt(ub, ub, b16("db", 0), A.add)
-    tt(ub, ub, ps16(0), A.mult)
-    tt(ub, ub, ("qb", 0, 16), A.mult)
-    tt(ub, ub, b16("bp", 0), A.add)
-    name_slots("ro3", ub)
-    send("3")
-    cp(("pcb", 0, 16), ub)
-    flags(sc, "f2", 1, 0)
-    flags(sc, "f2", 1, 1)
-    flags(sc, "f1", 0, 1)
-    to_a("a2", 0, 64, "e1", "f2", 0)
-    to_a("a2", 64, 64, "e1", "f2", 1024)
-    to_a("a3", 64, 64, "e1", "f1", 1024)
-    tt(ua, a("a1"), a("da", 2), A.mult)
-    tt(ua, ua, a("v1", 0), A.add)
-    tt(ua, ua, a("v1", 1), A.mult)
-    sa(("xe", NONE, EXT), ("rt", 0, 16), 0, 0)
-    arrive("X")
-    sc(("xcb", 0, 256), ("ind", ("xe", 0, EXT), ("pcb", 0, 16)))
-    sc(("a1", 0, 256), ("xcb", 0, 256))
-    sc(("a1", 256, 512), ("xb", 0, 256))
-    sa(("t2", NONE, NONE + 8), ("rt", 0, 8), 0, -1)
+    sc(("gs", 0, 1024), ind("t1", 0, L, "po", 64, 128))
+    tt(("m1", 0, 1024), ind("t1", 0, L, "po", 0, 64), ("rt", 0, 1024), A.is_equal)
+    to_a(bank(6, 128, 16), "e1n", "m1b")
+    to_a(bank(7, 0, 64), "e1n", "m1", 0)
+    tt(("m1", 1024, V), ("gs", 0, 1024), ("q0", 0, 1024), A.is_equal)
+    to_a(bank(7, 64, 64), "e1n", "m1", 1024)
+    sc(("bkf", 0, 48), bank(4, 64, 48))
+    alias("2")
+    sa(("cb", 0, 16), bp, -1.0 / GONE, -(O + KEEP) / GONE)
+    sa(a("c32"), a("pa"), -1.0 / GONE, -(O + KEEP) / GONE)
+    sa(("kk3", 0, 16), ("kk", 0, 16), 1, -O)
+    cp(("bki", 0, 48), ("bkf", 0, 48))
+    ts(("bkj", 0, 48), ("bki", 0, 48), STEP - 1, A.bitwise_and)
+    ts(("bnb", 0, 48), ("bkj", 0, 48), -O, A.add)
+    alias("X")
+    sa(("hl", O + V, W), ("hgh", 0, 256), col(8), 0)
+    sc(("hlb", 0, 256), ind("hl", O, O + V, "blo", 0, 16))
+    sc(("g48h", 0, 400), ind("hl", O, W, "blo48", 0, 25))
+    sc(("hl", O + mine[0], O + mine[1]), ("hlb", C * rank, C * rank + C))
+    sc(a("idb"), a("idf"))
+    tt(("zb", 0, 16), ("cb", 0, 16), bank(6, 128, 16), A.mult)
+    kb = [("q%d" % d, Q - 64, Q + 64) for d in range(D)]
+    mm([(bank(6, 0, 48), a("idf"), ("bkf", 0, 48), True, False)])
+    for d in range(D):
+        for h in range(2):
+            mm([((kb[d][0], Q - 64 + 64 * h, Q + 64 * h), a("idf"), ("ks", 128 * d + 64 * h, 128 * d + 64 * h + 64), True, False)])
+    cp(("nbo", 0, 384), ("nbi", 0, 384))
+    ts(col(10), col(4), 0, A.is_equal, 128, A.mult)
+    ts(col(13), col(4), 2, A.is_lt)
+    tt(col(11), col(10), col(7), A.add)
+    ts(col(14), col(4), -16 - (STEP - REP0), A.add)
+    ts(("ehl", 0, 143), ("xi", 0, 143), col(6), A.is_equal, col(11), A.mult)
+    tt(a("zf"), a("c32"), bank(7, 0, 128), A.mult)
+    for t, c in (("hl", 255), ("t2", 255), ("xe", 0), ("sx", 0)):
+        fill((t, 0, O), c)
+    fill(("sp", V, V + 8), 0)
     ts(a("va"), a("va"), col(5), A.subtract)
-    ts(a("gn"), a("gm"), col(5), A.is_equal)
-    ts(col(9), col(7), 128, A.mult)
-    ts(a("va2"), a("va"), V - base, A.add)
-    tt(col(10), col(8), col(9), A.add)
-    ts(a("go"), a("gn"), -1, A.mult)
-    run("g", [a("go")], [a("nt")], lambda: g.affine_select(T.nt[:], T.go[:], [[-1, 128]], A.is_ge, 0.0, 0, 1))
-    ts(("ehl", 0, 143), ("xi", 0, 143), col(6), A.is_equal, col(10), A.mult)
-    ts(a("idf"), ("xi", 16, 144), col(1), A.is_equal)
-    tt(ua, ua, a("a2"), A.mult)
-    tt(ua, ua, a("v1", 2), A.add)
-    tt(a("v1", 3), ua, a("a3"), A.mult)
-    tt(a("pcf"), a("pa"), a("v1", 3), A.add)
-    cp(a("pco"), a("pcf"))
-    full = ("rt", 0, NONE + 8)
-    cp(("t2", 0, 1024), ("ind", full, ("pco", 0, 64)))
-    sc(("t2", 1024, V), ("ind", full, ("pco", 64, 128)))
-    arrive("3")
-    resolve("lr3", "t2")
-    tt(("mb", 0, 256), ("ind", ("t2", 0, NONE + 8), ("pcb", 0, 16)), ("gbb", 0, 256), A.is_equal)
-    tt(("xm", 0, 256), ("mb", 0, 256), ("a1", 0, 256), A.mult)
-    tt(("xxb", 0, 256), ("xm", 0, 256), ("a1", 256, 512), A.add)
-    send("4")
-    mutual("mm", "t2", "pco", NONE + 8, ("a0", 0), ("a2", 0))
-    sa(a("pz"), a("pcf"), 1, -NONE)
-    sa(("hl", NONE, EXT), ("rt", 0, 16), 0, 0)
-    sc(("hl", GH + C * rank, GH + C * rank + C), ("ind", ("hl", 0, V), ("blo",) + own))
-    alias("xx", "xxb")
-    sc(("hg", 0, V), ("ind", ("hl", 0, EXT), ("pco", 0, 128)))
-    to_a("a3", 0, 128, "ehl", "hg")
-    sa(a("ones"), ("rt", 0, 128), 0, 1)
-    for h, ma in ((0, ("a0", 0, 64)), (1, ("a2", 0, 64))):
-        c0, c1 = 64 * h, 64 * h + 64
-        tt(("mt", c0, c1), ("pz", c0, c1), ma, A.mult)
-        ts(("mo", c0, c1), ("mt", c0, c1), NONE, A.add)
-        tt(("xx", 1024 * h, 1024 * h + 1024), ("ind", ("xe", 0, EXT), ("mo", c0, c1)), ("x2", 1024 * h, 1024 * h + 1024), A.add)
+    msum(bank(7, 256, 256), [(a("idb"), ("xb", 0, 256))])
+    arrive("2")
+    sc(("fb", 0, 384), ind("m1", 0, L, "bnb", 0, 24))
+    cp(("fb", 384, 768), ind("m1", 0, L, "bnb", 24, 48))
+    to_a(bank(6, 0, 48), "e1n", "fb", 0, True)
 
-    def weights(bank, d, lo, n):
-        sc((bank, 0, n), ("wb", V * d + lo, V * d + lo + n))
-    weights("gw", 2, 0, 1024)
-    weights("v0", 2, 1024, 512)
-    tt(a("gt"), a("a3"), a("va"), A.is_gt)
-    tt(("rep", 0, 64), ("gt", 0, 64), ("a0", 0, 64), A.is_ge)
-    tt(("rep", 64, 128), ("gt", 64, 128), ("a2", 0, 64), A.is_ge)
-    weights("a0", 2, 1536, 512)
-    weights("a2", 1, 1024, 512)
-    mm([(a("a1"), a("gn"), a("rep"), True, True)])
-    mm([(a("a3"), a("nt"), a("rep"), True, True)])
-    ts(a("v1", 1), a("rep"), -1, A.mult, 1, A.add)
-    tt(a("lt"), a("pz"), a("v1", 1), A.mult)
-    ts(a("lam"), a("lt"), NONE, A.add)
-    run("v", [a("ones"), a("a1")], [a("inc")],
-        lambda: g.vector.tensor_tensor_scan(T.inc[:], T.ones[:], T.a1[:, 0:128], 0.0, A.mult, A.add))
-    tt(a("nn"), a("inc"), a("a3"), A.add)
+    def flags(eng, d, h):
+        eng(("f%d" % d, 1024 * h, 1024 * h + 1024), ind("m1", 0, L, "nbo", 128 * d + 64 * h, 128 * d + 64 * h + 64))
+
+    def keys(d, h):
+        to_a((kb[d][0], kb[d][1] + 64 * h, kb[d][1] + 64 * h + 64), "e1n", "f%d" % d, 1024 * h, True)
+
+    def choose(z, k, u, ui, uj):
+        tt(u, z, k[0], A.max)
+        tt(u, u, k[1], A.max)
+        tt(ui, u, k[2], A.max)
+        ts(uj, ui, STEP - 1, A.bitwise_and)
+    flags(cp, 0, 0)
+    flags(sc, 0, 1)
+    keys(0, 0)
+    choose(("zb", 0, 16), [bank(6, 16 * d, 16) for d in range(D)], ("ub", 0, 16), ("ubi", 0, 16), ("ubj", 0, 16))
+    name_slots("ro3", ("ubj", 0, 16), "kk3")
+    send("3")
+    cp(("pcb", 0, 16), ("ubj", 0, 16))
+    keys(0, 1)
+    flags(sc, 1, 1)
+    flags(cp, 1, 0)
+    keys(1, 1)
+    keys(1, 0)
+    flags(sc, 2, 1)
+    cp(("f2", 0, 640), ind("m1", 0, L, "nbo", 256, 296))
+    sc(("f2", 640, 1024), ind("m1", 0, L, "nbo", 296, 320))
+    keys(2, 1)
+    keys(2, 0)
+    arrive("X")
+    sc(("xcb", 0, 256), ind("xe", 0, W, "pcb", 0, 16))
+    sa(a("vo"), a("va"), 1, O - base)
+    sa(a("pair"), a("gf"), col(13), 0)
+    sa(a("six"), a("gf"), 0, 16)
+    choose(a("zf"), kb, a("ua"), a("ui"), a("uj"))
+    cp(a("pco"), a("uj"))
+    cp(("t2", O, O + 1024), ind("hl", 0, W, "pco", 0, 64))
+    sc(("t2", O + 1024, O + V), ind("hl", 0, W, "pco", 64, 128))
+    half = (V - XV) // 2
+    for h in range(2):
+        mm([(bank(h, 0, half), a("idb"), ("xe", O + XV + half * h, O + XV + half * h + half), True, False)])
+    mm([(bank(4, 256, 128), a("idf"), a("vo"), True, False)])
+    to_a(bank(2, 0, 64), "ehl", "t2", O)
+    arrive("3")
+    resolve("lr3", "g48h", "t2", O)
+    cp(("t2", O + mine[0], O + mine[1]), ("ind", ("t2", O, O + V), ("blo",) + own))
+    tt(("eqb", 0, 256), ind("t2", 0, W, "pcb", 0, 16), ("hlb", 0, 256), A.is_equal)
+    msum(bank(7, 0, 256), [(a("pair"), ("eqb", 0, 256))])
+    to_a(bank(2, 64, 64), "ehl", "t2", O + 1024)
+
+    def back(eng, c0, c1):
+        eng(("g5", 16 * c0, 16 * c1), ind("t2", 0, W, "pco", c0, c1))
+    back(sc, 0, 64)
+    ts(bank(6, 0, 256), bank(7, 0, 256), -1, A.add, 0, A.max)
+    tt(("xm", 0, 256), ("xcb", 0, 256), bank(6, 0, 256), A.mult)
+    tt(("xxb", 0, 256), ("xm", 0, 256), bank(7, 256, 256), A.add)
+    send("4")
+    iota(("lw", REP0, REP0 + V), [[0, V]], 255, 0)
+    to_a(bank(3, 0, 64), "ehl", "g5", 0)
+    back(cp, 64, 96)
+    back(sc, 96, 128)
+    to_a(bank(3, 64, 64), "ehl", "g5", 1024)
+    alias("4")
+    tt(tmp[3], bank(2, 0, 128), a("va"), A.is_lt)
+    tt(tmp[0], bank(3, 0, 128), a("va"), A.is_equal)
+    tt(a("mt"), a("uj"), tmp[0], A.mult)
+    cp(a("mo"), a("mt"))
+    tt(a("lamf"), a("mt"), tmp[3], A.mult)
+    ts(a("nr"), a("lamf"), 0, A.is_gt)
+    tt(("xx", 0, XV), ind("xe", 0, W, "mo", 0, XV // 16), ("x2", 0, XV), A.add)
+    for h in range(2):
+        c0 = XV + half * h
+        sc(("xg", half * h, half * h + half), ind("xe", 0, W, "mo", c0 // 16, (c0 + half) // 16))
+
+    def weights(banks, q):
+        for d in range(D):
+            msum(bank(banks[d]), [(a("sel8"), ("w8", V * d + Q * q, V * d + Q * q + Q))])
+    mm([(bank(4, 256, 128), a("idn"), a("nr"), False, True)])
+    msum(bank(4, 0, 128), [(a("gn"), a("nr"))])
+    msum(bank(4, 128, 128), [(a("nt"), a("nr"))])
+    for h in range(2):
+        mm([(bank(h, 0, half), a("idb"), ("xg", half * h, half * h + half), False, True)])
+        sc(("xx", XV + half * h, XV + half * h + half), bank(h, 0, half))
+    weights((3, 5, 7), 0)
+    weights((0, 1, 2), 2)
+    scan(a("inc"), a("six"), bank(4, 0, 128), col(14), A.add, A.subtract)
+    tt(a("nnx"), a("inc"), bank(4, 128, 128), A.add)
+    tt(a("lamx"), a("lamf"), bank(4, 256, 128), A.max)
+    ts(a("no"), a("nnx"), STEP - REP0, A.add)
+    tt(a("rmin"), a("nnx"), bank(4, 256, 128), A.min)
+    ts(a("lam"), a("lamx"), -O, A.add)
+    ts(a("rhoo"), a("rmin"), STEP, A.add)
     arrive("4")
 
-    def prod(buf, d, h):
-        tt((buf, 1024 * h, 1024 * h + 1024), ("ind", ("xx", 0, NONE), ("nbo", 128 * d + 64 * h, 128 * d + 64 * h + 64)),
-           ("wb", V * d + 1024 * h, V * d + 1024 * h + 1024), A.mult)
+    def part(name, q, c0=0):
+        return (name, c0 + Q * q, c0 + Q * q + Q)
 
-    def gather(buf, d, h):
-        sc((buf, 1024 * h, 1024 * h + 1024), ("ind", ("xx", 0, NONE), ("nbo", 128 * d + 64 * h, 128 * d + 64 * h + 64)))
-    gather("p3", 2, 1)
-    weights("a3", 1, 1536, 512)
-    gather("p2", 1, 1)
-    gather("p3", 2, 0)
-    prod("p1", 0, 0)
-    prod("p1", 0, 1)
-    cp(a("no"), a("nn"))
-    tt(a("rho"), a("va2"), a("nn"), A.subtract)
-    sa(a("rn"), a("nn"), 1, base)
-    tt(a("v1", 0), a("rho"), a("v1", 1), A.mult)
-    tt(a("rho"), a("nn"), a("v1", 0), A.add)
-    cp(a("rhoo"), a("rho"))
-    sa(("nx", NONE, EXT), ("rt", 0, 16), 0, 0)
-    sc(("nx", 0, V), ("ind", ("hl", 0, V), ("no", 0, 128)))
-    sc(("nxb", 0, 256), ("ind", ("nx", 0, V), ("blo", 0, 16)))
+    def gathers(q):
+        for d in range(D):
+            sc(part("p%d" % d, q), ind("xx", 0, L, "nbo", 128 * d + 32 * q, 128 * d + 32 * q + 32))
+
+    def times(d, q, bk, out=None):
+        tt(out or part("p%d" % d, q), part("p%d" % d, q), bank(bk), A.mult)
+    gathers(0)
+    cp(("nx", 0, NXV), ind("hl", O, O + V, "no", 0, NXV // 16))
+    gathers(2)
+    gathers(1)
+    sc(("nx", NXV, V), ind("hl", O, O + V, "no", NXV // 16, 128))
+    sc(("nxb", 0, 256), ind("nx", 0, V, "blo", 0, 16))
     send("6")
-    alias("nx", "nxb")
-    sa(("lw", 0, V), ("rt", 0, V), 0, -1)
-    last = (1536, V)
-    tt(("p3",) + last, ("p3",) + last, ("a0", 0, 512), A.mult)
-    tt(("p2",) + last, ("p2",) + last, ("a3", 0, 512), A.mult)
-    mm([(("v1", 0, 512), a("idf"), (p,) + last, p == "p1", p == "p3") for p in ("p1", "p2", "p3")])
-    prod("p2", 1, 0)
-    for lo, n, bank, w1 in ((0, 1024, "gw", None), (1024, 512, "v0", "a2")):
-        acc = (bank, 0, n)
-        tt(acc, ("p3", lo, lo + n), acc, A.mult)
-        if w1:
-            tt(("p2", lo, lo + n), ("p2", lo, lo + n), (w1, 0, n), A.mult)
-        tt(acc, ("p2", lo, lo + n), acc, A.add)
-        tt(("sx", lo, lo + n), ("p1", lo, lo + n), acc, A.add)
-    sc(("sx",) + last, ("v1", 0, 512))
-    sc(("sb", 0, 256), ("ind", ("sx", 0, V), ("blo", 0, 16)))
+    gathers(3)
+    alias("6")
+    order = ((0, (3, 5, 7)), (2, (0, 1, 2)), (1, (4, 5, 7)), (3, (6, 1, 2)))
+    times(0, 0, 3, bank(3))
+    for i, (q, bk) in enumerate(order):
+        times(1, q, bk[1])
+        times(2, q, bk[2])
+        tt(bank(bk[0]), part("p1", q), bank(bk[0]), A.add)
+        if i < 2:
+            weights(order[i + 2][1], order[i + 2][0])
+        if i < 3:
+            times(0, order[i + 1][0], order[i + 1][1][0], bank(order[i + 1][1][0]))
+        if q % 2:
+            tt(part("sx", q, O), part("p2", q), bank(bk[0]), A.add)
+        else:
+            tt(bank(bk[0]), part("p2", q), bank(bk[0]), A.add)
+            sc(part("sx", q, O), bank(bk[0]))
+    sc(("sb", 0, 256), ind("sx", O, O + V, "blo", 0, 16))
     send("5")
-    alias("sx", "sb")
-    sc(("p3", 0, 1024), ("sx", 0, 1024))
-    sc(("gw", 0, 1024), ("sx", 1024, V))
-    sa(("sx", NONE, NONE + 8), ("rt", 0, 8), 0, 0)
-    sa(("sp", 0, 8), ("rt", 0, 8), 0, 0)
-    tt(a("cmf"), a("rn"), a("rep"), A.mult)
-    run("v", [("hl", 0, V)], [("ind", ("lw", 0, 2 * V), ("rhoo", 0, 128))],
-        lambda: g.vector.tensor_copy(ap(("ind", ("lw", 0, 2 * V), ("rhoo", 0, 128))), T.hl[:, 0:V]))
-    to_a("a3", 0, 128, "ehl", "lw")
+    alias("5")
+    lst = ind("lw", 0, REP0 + V, "rhoo", 0, 128)
+    cp(lst, ("hl", O, O + V))
+    for q in (3, 1):
+        sc(part("p0", q), part("sx", q, O))
     arrive("6")
-    sc(("cg", 0, V), ("ind", ("nx", 0, EXT), ("lam", 0, 128)))
-    to_a("a1", 0, 128, "ehl", "cg")
+    for h in range(2):
+        sc(("cg", 1024 * h, 1024 * h + 1024), ind("nx", 0, L, "lam", 64 * h, 64 * h + 64))
+        to_a(bank(1, 64 * h, 64), "ehl", "cg", 1024 * h)
+    for h in (1, 0):
+        to_a(bank(5 + 2 * h, 0, 64), "ehl", "lw", REP0 + 1024 * h)
     arrive("5")
-    sc(("p1", 1024, V), ("ind", ("sx", 0, NONE + 8), ("mo", 64, 128)))
-    tt(("sp", 8, 1032), ("ind", ("sx", 0, NONE + 8), ("mo", 0, 64)), ("p3", 0, 1024), A.add)
-    tt(("sp", 1032, V + 8), ("p1", 1024, V), ("gw", 0, 1024), A.add)
-    ts(a("l1"), a("a3"), 8 - base, A.add, 0, A.max)
-    for i in range(8):
-        (sc if i % 2 else cp)(("yy", 256 * i, 256 * i + 256), ("ind", ("sp", 0, V + 8), ("l1", 16 * i, 16 * i + 16)))
-    for i in range(8):
-        dma("y", "y%d" % i, T.y[:, 256 * i:256 * i + 256], T.yy[:, 256 * i:256 * i + 256], [("yy", 256 * i, 256 * i + 256)], [])
-    tt(a("cmf"), a("cmf"), a("a1"), A.add)
+
+    def mates(q):
+        return ind("sx", 0, W, "mo", 32 * q, 32 * q + 32)
+
+    def values(eng, q, c0, c1):
+        eng(("yy", Q * q + 16 * c0, Q * q + 16 * c1), ind("sp", Q * q, V + 8, "l1", 32 * q + c0, 32 * q + c1))
+
+    def store(q):
+        dma("y", "y%d" % q, T.y[:, Q * q:Q * q + Q], T.yy[:, Q * q:Q * q + Q], [part("yy", q)], [])
+    def reps(q):
+        ts(("l1", 32 * q, 32 * q + 32), bank(5 + 2 * (q // 2), 32 * (q % 2), 32), -base - Q * q, A.add, V - Q * q, A.min)
+    sc(part("p1", 2), mates(2))
+    sc(part("p1", 0), mates(0))
+    tt(part("sp", 3), mates(3), part("p0", 3), A.add)
+    cp(a("cmf"), bank(1, 0, 128))
     dma("y", "cm", T.cm[:], T.cmf[:], [a("cmf")], [])
+    tt(part("sp", 2), part("p1", 2), bank(0), A.add)
+    reps(3)
+    reps(2)
+    values(sc, 3, 0, 32)
+    store(3)
+    tt(part("sp", 1), mates(1), part("p0", 1), A.add)
+    reps(1)
+    reps(0)
+    values(sc, 2, 0, 32)
+    store(2)
+    tt(part("sp", 0), part("p1", 0), bank(3), A.add)
+    values(sc, 1, 0, 32)
+    store(1)
+    values(cp, 0, 0, 32)
+    store(0)
     need("g", [("loc", sent[0])] + [(s, count[s]) for s in ("v", "s", "t", "p")] + sorted(totals.items()))

@@ -7,8 +7,7 @@ O = 16
 W = O + L
 STEP, GONE, KEEP = 4096, 16384, 32768
 REP0 = 2080
-XV = 1280
-NXV = 768
+NXV = 1152
 Q = 512
 LISTS = "gm gf idf six va vo w0s w1s wm ta tb tc pa c32 zf ua mt lamf inc nnx rmin lamx".split()
 
@@ -22,29 +21,30 @@ def buffers(*groups):
 
 
 SCRATCH = buffers(
-    ("bli bsh bms ubi ubj", 16, "int32"), ("nbi", 384, "int32"), ("pi", 8, "int32"), ("bki bkj", 48, "int32"),
-    ("ui uj", 128, "int32"),
+    ("bli lr0 bsh bms ubi ubj", 16, "int32"), ("nbi", 384, "int32"), ("pi", 8, "int32"), ("bki bkj", 48, "int32"),
+    ("ui uj", 128, "int32"), ("r0", 2, "int32"),
     ("wa", 384, "bfloat16"), ("w8", 6144, "bfloat16"), ("s0 s1", 160, "bfloat16"), ("e1n ehl", 144, "bfloat16"),
     ("gn nt nr g10 g20 g21 idb idp idn pair sel8", 128, "bfloat16"), ("xe hl t2", W, "bfloat16"), ("m1 nx", L, "bfloat16"),
-    ("xb m1b nxb hlb eqb hgh", 256, "bfloat16"), ("g48h", 400, "bfloat16"), ("fb xg", 768, "bfloat16"),
-    ("f0 f1 f2 g5 cg", V, "bfloat16"), ("x2", XV, "bfloat16"), ("lw", REP0 + V, "bfloat16"), ("rX r2 r6", C, "bfloat16"),
-    ("blo pcb bmo ro1 ro3 lr1 lr3 zz bpo", 16, "uint16"), ("r1 r3", 2, "uint16"), ("boff bnb", 48, "uint16"),
-    ("blo48", 26, "uint16"), ("po pco mo lam no rhoo l1", 128, "uint16"), ("nbo", 384, "uint16"),
-    ("pc", 24, "float32"), ("ub zb cb id16 kk kk3 kt bc", 16, "float32"), ("r4 r5", C, "float32"), ("g48", 400, "float32"),
+    ("xb m1b t2b nxb hlb eqb", 256, "bfloat16"), ("fb pgw", 768, "bfloat16"),
+    ("f0 f1 f2 g5 cg", V, "bfloat16"), ("x2 xg", 1024, "bfloat16"), ("rX r2 r3 r6", C, "bfloat16"),
+    ("blo pcb bmo ro1 lr1 gho zz bpo", 16, "uint16"), ("r1", 2, "uint16"), ("boff bnb", 48, "uint16"),
+    ("blo48", 26, "uint16"), ("po pco mo lam no rhoo", 128, "uint16"), ("nbo", 384, "uint16"),
+    ("pc", 24, "float32"), ("ub zb cb id16 kk kt bc bq", 16, "float32"), ("r4 r5", C, "float32"), ("g48", 400, "float32"),
     ("bkf", 48, "float32"), ("xi", 160, "float32"), ("eall", 144, "float32"),
     ("cmf", 128, "float32"), ("lists", 128 * len(LISTS), "float32"),
-    ("nbf ks", 384, "float32"), ("jm m16 m0 bs pgs gbb bmask xcb xm xxb sb", 256, "float32"), ("pg", 768, "float32"),
-    ("gs", 1024, "float32"), ("rt t1 xx", L, "float32"), ("sx", W, "float32"), ("p0 p1 p2 yy", V, "float32"),
-    ("sp", V + 8, "float32"))
+    ("nbf ks ws", 384, "float32"), ("jm m16 m0 bs pgs gbb xcb xm xxb sb", 256, "float32"), ("pg bmask", 768, "float32"),
+    ("gs", 1024, "float32"), ("rt t1 xx", L, "float32"), ("sx", W, "float32"), ("p0 p1 p2", V, "float32"),
+    ("yy", REP0 + V, "float32"))
 PSUM = {"q%d" % i: 1024 for i in range(4)}
 for _n in PSUM:
     SCRATCH[_n] = ("psum", [128, PSUM[_n]], "float32")
 SCRATCH["tr"] = ("sbuf", [128, D, 128], "bfloat16")
 ROWS8 = ("w8", "sel8")
-EXCH = {"X": ("xb", "xe", O + V, C), "1": ("ro1", "lr1", 0, 2), "2": ("m1b", "m1", V, C), "3": ("ro3", "lr3", 0, 2),
-        "4": ("xxb", "xx", V, C), "6": ("nxb", "nx", V, C), "5": ("sb", "sx", O + V, C)}
-ORDER = ["X", "1", "2", "3", "4", "6", "5"]
-DMAS = ["bl", "z1", "z3", "nb", "w0", "w1", "w2", "x", "x2", "w8", "sel", "cm"] + ["y%d" % i for i in range(4)]
+EXCH = {"0": ("bli", "lr0", 0, 2), "1": ("ro1", "lr1", 0, 2), "X": ("xb", "xe", O + V, C), "2": ("m1b", "m1", V, C),
+        "3": ("t2b", "t2", O + V, C), "4": ("xxb", "xx", V, C), "5": ("sb", "sx", O + V, C), "6": ("nxb", "nx", V, C)}
+ORDER = ["0", "1", "2", "X", "3", "4", "5", "6"]
+UNHURRIED = ("0", "X")
+DMAS = ["bl", "z0", "z1", "nb", "w0", "w1", "w2", "x", "x2", "w8", "sel", "cm"] + ["y%d" % i for i in range(5)]
 SEMAPHORES = (["v", "s", "t", "p", "loc", "rloc"] + ["d" + n for n in DMAS] + ["arr" + k for k in ORDER]
               + ["hop" + k for k in ORDER])
 
@@ -56,13 +56,17 @@ def pick(engines, i, n):
     return m
 
 
-def plan(src, T, topo):
+def plan(src, T, topo, k=None):
     near, far = [], []
     for d in T.cores:
         if d != src:
             (near if topo.may_write(src, d) else far).append(d)
     hops = [c for c in topo.cores_of(src) if c != src and all(topo.may_write(c, d) for d in far)]
-    straight = [(d, pick(topo.engines(src, d), i, 2)) for i, d in enumerate(near)]
+    if k in UNHURRIED:
+        straight = [[(d, pick(topo.engines(src, d), i, 2)) for i, d in enumerate(near)]]
+    else:
+        straight = [[(d, pick(topo.engines(src, d), i, 4)) for i, d in enumerate(near[:2])],
+                    [(d, topo.mask(src, d)) for d in near[2:]]]
     over = []
     for i, d in enumerate(far):
         h = hops[i]
@@ -227,7 +231,7 @@ def rank_program(g, core, T, topo):
         totals["d" + sem] = totals.get("d" + sem, 0) + 16
         note(queue, reads, writes, ("d" + sem, totals["d" + sem]))
 
-    straight, over = plan(core, T, topo)
+    over = plan(core, T, topo)[1]
     sent = [0]
 
     def send(k):
@@ -240,24 +244,26 @@ def rank_program(g, core, T, topo):
         calls = []
         for h, m_in, d, _ in over:
             rid, pid = topo.addr(h, core)
-            calls.append(RemoteDMATransfer(dst_ids=[DstId(rid=rid, pnc=pid)], dma_engine_mask=m_in, remote_sem=T.sem["hop" + k],
-                                           src=block(d), dst=T["r" + k][:]))
+            calls.append(RemoteDMATransfer(dst_ids=[DstId(rid=rid, pnc=pid)], dma_engine_mask=m_in,
+                                           remote_sem=T.sem["hop" + k], src=block(d), dst=T["r" + k][:]))
             sent[0] += bits(m_in)
         g.remote_dma_fused(calls, local_sem=T.sem.loc)
-        calls = []
-        for d, m in straight:
-            rid, pid = topo.addr(d, core)
-            calls.append(RemoteDMATransfer(dst_ids=[DstId(rid=rid, pnc=pid)], dma_engine_mask=m, remote_sem=T.sem["arr" + k],
-                                           src=block(d), dst=T[land][:, c0 + w * rank:c0 + w * rank + w]))
-            sent[0] += bits(m)
-        g.remote_dma_fused(calls, local_sem=T.sem.loc)
+        for some in plan(core, T, topo, k)[0]:
+            calls = []
+            for d, m in some:
+                rid, pid = topo.addr(d, core)
+                calls.append(RemoteDMATransfer(dst_ids=[DstId(rid=rid, pnc=pid)], dma_engine_mask=m, remote_sem=T.sem["arr" + k],
+                                               src=block(d), dst=T[land][:, c0 + w * rank:c0 + w * rank + w]))
+                sent[0] += bits(m)
+            g.remote_dma_fused(calls, local_sem=T.sem.loc)
 
     def arrive(k):
         n = 0
         for c in T.cores:
             if c != core:
-                near, far = plan(c, T, topo)
-                n += sum(bits(m) for d, m in near if d == core) + sum(bits(m) for _, _, d, m in far if d == core)
+                near, far = plan(c, T, topo, k)
+                n += sum(bits(m) for some in near for d, m in some if d == core)
+                n += sum(bits(m) for _, _, d, m in far if d == core)
         _, land, c0, w = EXCH[k]
         totals["arr" + k] = n
         note("net", [], [(land, c0, c0 + w * N)], ("arr" + k, n))
@@ -280,17 +286,19 @@ def rank_program(g, core, T, topo):
     mine = (V + C * rank, V + C * rank + C)
     dma("y", "bl", T.bli[:], T.bl[:], [], [("bli", 0, 16)])
     for d in range(D):
-        dma("s" if d == 1 else "y", "w%d" % d, T.wa[:, 128 * d:128 * d + 128], T.w[:, V * d:V * d + V], [], [a("wa", d)])
-    dma("y", "x", T.xe[:, O:O + V], T.x[:], [], [("xe", O, O + V)])
+        dma("y", "w%d" % d, T.wa[:, 128 * d:128 * d + 128], T.w[:, V * d:V * d + V], [], [a("wa", d)])
     dma("y", "nb", T.nbi[:], T.nb[:], [], [("nbi", 0, 384)])
+    dma("y", "x", T.xe[:, O:O + V], T.x[:], [], [("xe", O, O + V)])
+    dma("s", "z0", T.lr0[:, own[0]:own[1]], T.bl[:, own[0]:own[1]], [], [("lr0",) + own])
 
+    fill(("zz", 0, 16), 0)
+    fill(("blo48", 0, 26), V + C * ((rank + 1) % N))
     iota(("pi", 0, 1), [[1, 1]], 0, 1)
     iota(("xi", 0, 160), [[1, 160]], 0, 0)
-    iota(("rt", 0, 512), [[1, 512]], base, 0)
     iota(("gm", 0, 128), [[16, 8], [0, 16]], 0, 0)
     iota(("jm", 0, 256), [[0, 16], [1, 16]], 0, 0)
     iota(("kk", 0, 16), [[-C, N], [0, 2]], 48 * rank + 16 - V, 0)
-    iota(("va", 0, 128), [[16, 128]], base, 1)
+    send("0")
 
     ts(("pi", 2, 3), ("pi", 0, 1), 4, A.arith_shift_right, 1, A.bitwise_and)
     ts(("pi", 1, 2), ("pi", 0, 1), 15, A.bitwise_and)
@@ -301,28 +309,19 @@ def rank_program(g, core, T, topo):
     ts(("s1", 0, 160), ("xi", 0, 160), col(1), A.is_equal, col(3), A.mult)
     cp(col(4), ("pi", 1, 2))
     tt(col(5), ("pi", 0, 1), ("pi", 1, 2), A.subtract)
-    fill(("zz", 0, 16), 0)
     ts(("id16", 0, 16), ("xi", 0, 16), col(4), A.is_equal)
     ts(a("idf"), ("xi", 16, 144), col(1), A.is_equal)
-    ts(col(6), col(5), 15, A.add)
-    ts(col(7), col(4), 1, A.is_equal)
-    ts(col(8), col(4), 1, A.not_equal)
-    fill(("blo48", 0, 26), V + C * ((rank + 1) % N))
-    for k in ("1", "3"):
-        dma("y", "z" + k, T["lr" + k][:, own[0]:own[1]], T.zz[:, 0:2], [("zz", 0, 2)], [("lr" + k,) + own])
-    dma("y", "x2", T.x2[:], T.x[:, 0:XV], [], [("x2", 0, XV)])
-    dma("y", "w8", T.w8[0:8, :], T.w[:], [], [("w8", 0, D * V)])
-    for i in range(1, 4):
-        sa(("rt", 512 * i, 512 * i + 512), ("rt", 0, 512), 1, 512 * i)
-    sa(("rt", V, L), ("rt", 0, 256), 0, -1)
-    cp(("blo", 0, 16), ("bli", 0, 16))
-    ts(("bms", 0, 16), ("bli", 0, 16), 15, A.bitwise_and)
-    ts(("bsh", 0, 16), ("bli", 0, 16), 4, A.arith_shift_right)
-    cp(("bmo", 0, 16), ("bms", 0, 16))
-    for d in range(D):
-        ts(("boff", 16 * d, 16 * d + 16), ("bsh", 0, 16), 128 * d, A.add)
     ts(a("gf"), a("gm"), col(5), A.is_equal)
-    ts(("m16", 0, 256), ("jm", 0, 256), col(4), A.is_equal)
+    dma("y", "z1", T.lr1[:, own[0]:own[1]], T.zz[:, 0:2], [("zz", 0, 2)], [("lr1",) + own])
+    dma("y", "x2", T.x2[:], T.x[:, 1024:V], [], [("x2", 0, 1024)])
+    dma("y", "w8", T.w8[0:8, :], T.w[:], [], [("w8", 0, D * V)])
+    sa(("rt", 0, 128), ("xi", 0, 128), 1, base)
+    for n in (128, 256, 512, 1024):
+        sa(("rt", n, 2 * n), ("rt", 0, n), 1, n)
+    sa(("rt", V, L), ("rt", 0, 256), 0, -1)
+    ts(("bms", 0, 16), ("bli", 0, 16), 15, A.bitwise_and)
+    cp(("blo", 0, 16), ("bli", 0, 16))
+    cp(("bmo", 0, 16), ("bms", 0, 16))
     for d in range(D):
         run("v", [a("wa", d)], [a("tr")], lambda: g.vector.transpose(T.tr[:, d, :], ap(a("wa", d))))
     wp = [bank(2, 128 * d, 128) for d in range(D)]
@@ -334,49 +333,47 @@ def rank_program(g, core, T, topo):
             grp.append((("q1", i, 384, 8), ("s%d" % h, st, st + 128), ("tr", 32 * b + 16 * gg, 32 * b + 16 * gg + 16),
                         gg == 0, gg == 1))
     mm(grp)
-    for j in range(2):
-        cp(("blo48", 1 + j, 25, 3), ("bli", j, 16, 2))
-    ts(("bc", 0, 16), ("xi", 0, 16), col(8), A.mult)
-    ts(col(12), col(8), 16 * rank, A.mult)
-    ts(col(9), col(4), 0, A.is_equal, -GONE, A.mult)
-    ts(("eall", 0, 143), ("xi", 0, 143), col(6), A.is_equal)
+    ts(("bsh", 0, 16), ("bli", 0, 16), 4, A.arith_shift_right)
+    ts(("m16", 0, 256), ("jm", 0, 256), col(4), A.is_equal)
+    for d in range(D):
+        ts(("boff", 16 * d, 16 * d + 16), ("bsh", 0, 16), 128 * d, A.add)
     nb = [("nbi", 128 * d, 128 * d + 128) for d in range(D)]
     tmp = [bank(6, 128 * i, 128) for i in range(4)]
     tmq = [bank(5, 128 * i, 128) for i in range(4)]
-    sc(("xb", 0, 256), ind("xe", O, O + V, "blo", 0, 16))
-    send("X")
     sc(("bmask", 0, 256), ind("id16", 0, 16, "bmo", 0, 16))
     sa(("m0", 0, 256), ("jm", 0, 256), 1, 0, SIGN)
     sc(("gbb", 0, 256), ind("rt", 0, V, "blo", 0, 16))
     sc(("rt",) + mine, ("gbb", C * rank, C * rank + C))
+    cp(tmq[0], nb[0])
+    tt(tmp[0], nb[1], tmq[0], A.subtract)
+    tt(tmq[1], nb[2], tmq[0], A.subtract)
     cp(a("w1s"), wp[1])
     tt(a("g10"), a("w1s"), wp[0], A.is_gt)
     tt(a("wm"), a("w1s"), wp[0], A.max)
-    cp(tmq[0], nb[0])
-    tt(tmp[1], wp[2], a("wm"), A.is_gt)
-    tt(tmp[0], nb[1], tmq[0], A.subtract)
-    tt(tmq[1], nb[2], tmq[0], A.subtract)
     tt(a("ta"), a("g10"), tmp[0], A.mult)
+    tt(tmp[1], wp[2], a("wm"), A.is_gt)
     tt(a("tc"), tmq[1], a("ta"), A.subtract)
     tt(a("tb"), a("ta"), tmq[0], A.add)
     tt(tmp[2], a("tc"), tmp[1], A.mult)
     tt(a("pa"), a("tb"), tmp[2], A.add)
 
-    def border(src, d):
-        tt(("pg", 256 * d, 256 * d + 256), ind(src[0], src[1], src[2], "boff", 16 * d, 16 * d + 16), ("bmask", 0, 256), A.mult)
-    border(a("pa"), 0)
+    tt(("pg", 0, 256), ind("pa", 0, 128, "boff", 0, 16), ("bmask", 0, 256), A.mult)
     msum(bank(7, 0, 256), [(a("gf"), ("pg", 0, 256))])
     cp(a("po"), a("pa"))
-    sc(a("w0s"), wp[0])
     sa(a("idp"), a("idf"), STEP, 0)
     sa(a("idn"), a("idf"), -STEP, 0)
+    for d in (1, 2):
+        sc(("bmask", 256 * d, 256 * d + 256), ("bmask", 0, 256))
+    sc(("ws", 0, 384), bank(2, 0, 384))
     tt(a("g21"), wp[2], a("w1s"), A.is_gt)
-    tt(a("g20"), wp[2], a("w0s"), A.is_gt)
+    tt(a("g20"), wp[2], a("ws"), A.is_gt)
     signs = ((("idn", "g10"), ("idn", "g20")), (("idp", "g10"), ("idn", "g21")), (("idp", "g20"), ("idp", "g21")))
     for d in range(D):
         msum(bank(3, 128 * d, 128), [(a(m), a(z)) for m, z in signs[d]])
-    for d in range(D):
-        ts(a("nbf", d), nb[d], O + STEP * (2 - d), A.add)
+    for j in range(2):
+        cp(("blo48", 1 + j, 25, 3), ("bli", j, 16, 2))
+    ts(col(7), col(4), 1, A.is_equal)
+    ts(col(8), col(4), 1, A.not_equal)
     tt(("bs", 0, 256), ("m16", 0, 256), bank(7, 0, 256), A.mult)
     scan(("pgs", 0, 256), ("m0", 0, 256), ("bs", 0, 256), 0.0, A.mult, A.add)
     bp = ("pgs", 15, 256, 16)
@@ -388,12 +385,17 @@ def rank_program(g, core, T, topo):
     send("1")
     sc(a("gn"), a("gf"))
     dma("y", "sel", T.sel8[0:8, :], T.gn[0::16, :], [a("gn")], [a("sel8")])
-    iota(("hgh", 0, 256), [[16, N], [0, C]], 0, 0)
-    run("g", [a("gn")], [a("nt")], lambda: g.affine_select(T.nt[:], T.gn[:], [[-1, 128]], A.is_gt, 0.0, 0, 1))
     sc(("t1", 1024, V), ind("rt", 0, L, "po", 64, 128))
-    tt(("ks", 0, 384), ("nbf", 0, 384), bank(3, 0, 384), A.add)
+    sc(("xb", 0, 256), ind("xe", O, O + V, "blo", 0, 16))
+    run("g", [a("gn")], [a("nt")], lambda: g.affine_select(T.nt[:], T.gn[:], [[-1, 128]], A.is_gt, 0.0, 0, 1))
+    ts(col(6), col(5), 15, A.add)
+    ts(("bc", 0, 16), ("xi", 0, 16), col(8), A.mult)
+    ts(col(12), col(8), 16 * rank, A.mult)
     for d in range(D):
-        border(("ks", 0, 384), d)
+        ts(a("nbf", d), nb[d], O + STEP * (2 - d), A.add)
+    ts(("eall", 0, 143), ("xi", 0, 143), col(6), A.is_equal)
+    tt(("ks", 0, 384), ("nbf", 0, 384), bank(3, 0, 384), A.add)
+    tt(("pg", 0, 768), ind("ks", 0, 384, "boff", 0, 48), ("bmask", 0, 768), A.mult)
     to_a(bank(4, 64, 48), "eall", "pg")
     cp(("t1", 0, 1024), ind("rt", 0, L, "po", 0, 64))
     cp(("bpo", 0, 16), bp)
@@ -403,16 +405,15 @@ def rank_program(g, core, T, topo):
     sa(("hl", O, O + 128), ("xi", 0, 128), col(7), col(12))
     for i in (1, 2, 4, 8):
         sa(("hl", O + 128 * i, O + 256 * i), ("hl", O, O + 128 * i), 1, ("bc", i, i + 1))
+    ts(col(9), col(4), 0, A.is_equal, -GONE, A.mult)
     ts(("e1n", 0, 143), ("xi", 0, 143), col(6), A.is_equal, col(9), A.mult)
-
-    def resolve(land, names, tab, c0):
-        for eng, q0, q1 in ((cp, 0, rank), (sc, rank + 1, N)):
-            if q0 < q1:
-                eng((tab, c0 + V + C * q0, c0 + V + C * q1), ind(names, 0, 400, land, 2 * q0, 2 * q1))
     arrive("1")
-    resolve("lr1", "g48", "t1", 0)
+    for eng, q0, q1 in ((cp, 0, rank), (sc, rank + 1, N)):
+        if q0 < q1:
+            eng(("t1", V + C * q0, V + C * q1), ind("g48", 0, 400, "lr1", 2 * q0, 2 * q1))
     tt(("m1b", 0, 256), ind("t1", 0, L, "bpo", 0, 16), ("gbb", 0, 256), A.is_equal)
     send("2")
+    send("X")
     sc(("gs", 0, 1024), ind("t1", 0, L, "po", 64, 128))
     tt(("m1", 0, 1024), ind("t1", 0, L, "po", 0, 64), ("rt", 0, 1024), A.is_equal)
     to_a(bank(6, 128, 16), "e1n", "m1b")
@@ -423,16 +424,19 @@ def rank_program(g, core, T, topo):
     alias("2")
     sa(("cb", 0, 16), bp, -1.0 / GONE, -(O + KEEP) / GONE)
     sa(a("c32"), a("pa"), -1.0 / GONE, -(O + KEEP) / GONE)
-    sa(("kk3", 0, 16), ("kk", 0, 16), 1, -O)
     cp(("bki", 0, 48), ("bkf", 0, 48))
+    arrive("0")
+    cp(("gho", 0, 16), ("lr0", 0, 16))
+    ts(("bq", 0, N), ("bc", 0, N), 16, A.mult, col(12), A.subtract)
     ts(("bkj", 0, 48), ("bki", 0, 48), STEP - 1, A.bitwise_and)
+    ts(col(15), col(4), base, A.add)
     ts(("bnb", 0, 48), ("bkj", 0, 48), -O, A.add)
     alias("X")
-    sa(("hl", O + V, W), ("hgh", 0, 256), col(8), 0)
     sc(("hlb", 0, 256), ind("hl", O, O + V, "blo", 0, 16))
-    sc(("g48h", 0, 400), ind("hl", O, W, "blo48", 0, 25))
-    sc(("hl", O + mine[0], O + mine[1]), ("hlb", C * rank, C * rank + C))
     sc(a("idb"), a("idf"))
+    for q in range(N):
+        sa(("hl", O + V + C * q, O + V + C * q + C), ind("hl", O, O + V, "gho", 2 * q, 2 * q + 2), 1, ("bq", q, q + 1))
+    sa(a("va"), ("xi", 0, 128), 16, col(15))
     tt(("zb", 0, 16), ("cb", 0, 16), bank(6, 128, 16), A.mult)
     kb = [("q%d" % d, Q - 64, Q + 64) for d in range(D)]
     mm([(bank(6, 0, 48), a("idf"), ("bkf", 0, 48), True, False)])
@@ -448,8 +452,6 @@ def rank_program(g, core, T, topo):
     tt(a("zf"), a("c32"), bank(7, 0, 128), A.mult)
     for t, c in (("hl", 255), ("t2", 255), ("xe", 0), ("sx", 0)):
         fill((t, 0, O), c)
-    fill(("sp", V, V + 8), 0)
-    ts(a("va"), a("va"), col(5), A.subtract)
     msum(bank(7, 256, 256), [(a("idb"), ("xb", 0, 256))])
     arrive("2")
     sc(("fb", 0, 384), ind("m1", 0, L, "bnb", 0, 24))
@@ -462,18 +464,20 @@ def rank_program(g, core, T, topo):
     def keys(d, h):
         to_a((kb[d][0], kb[d][1] + 64 * h, kb[d][1] + 64 * h + 64), "e1n", "f%d" % d, 1024 * h, True)
 
-    def choose(z, k, u, ui, uj):
+    def choose(z, k, u, ui, uj, meanwhile=None):
         tt(u, z, k[0], A.max)
         tt(u, u, k[1], A.max)
+        if meanwhile:
+            meanwhile()
         tt(ui, u, k[2], A.max)
         ts(uj, ui, STEP - 1, A.bitwise_and)
     flags(cp, 0, 0)
     flags(sc, 0, 1)
     keys(0, 0)
     choose(("zb", 0, 16), [bank(6, 16 * d, 16) for d in range(D)], ("ub", 0, 16), ("ubi", 0, 16), ("ubj", 0, 16))
-    name_slots("ro3", ("ubj", 0, 16), "kk3")
-    send("3")
     cp(("pcb", 0, 16), ("ubj", 0, 16))
+    cp(("t2b", 0, 256), ind("hl", 0, W, "pcb", 0, 16))
+    send("3")
     keys(0, 1)
     flags(sc, 1, 1)
     flags(cp, 1, 0)
@@ -486,24 +490,21 @@ def rank_program(g, core, T, topo):
     keys(2, 0)
     arrive("X")
     sc(("xcb", 0, 256), ind("xe", 0, W, "pcb", 0, 16))
+    alias("3")
     sa(a("vo"), a("va"), 1, O - base)
     sa(a("pair"), a("gf"), col(13), 0)
     sa(a("six"), a("gf"), 0, 16)
-    choose(a("zf"), kb, a("ua"), a("ui"), a("uj"))
+    choose(a("zf"), kb, a("ua"), a("ui"), a("uj"),
+           lambda: tt(("pgw", 0, 768), ind("ws", 0, 384, "boff", 0, 48), ("bmask", 0, 768), A.mult))
     cp(a("pco"), a("uj"))
     cp(("t2", O, O + 1024), ind("hl", 0, W, "pco", 0, 64))
     sc(("t2", O + 1024, O + V), ind("hl", 0, W, "pco", 64, 128))
-    half = (V - XV) // 2
     for h in range(2):
-        mm([(bank(h, 0, half), a("idb"), ("xe", O + XV + half * h, O + XV + half * h + half), True, False)])
-    mm([(bank(4, 256, 128), a("idf"), a("vo"), True, False)])
-    to_a(bank(2, 0, 64), "ehl", "t2", O)
+        mm([(bank(h), a("idb"), ("xe", O + Q * h, O + Q * h + Q), True, False)])
     arrive("3")
-    resolve("lr3", "g48h", "t2", O)
-    cp(("t2", O + mine[0], O + mine[1]), ("ind", ("t2", O, O + V), ("blo",) + own))
     tt(("eqb", 0, 256), ind("t2", 0, W, "pcb", 0, 16), ("hlb", 0, 256), A.is_equal)
     msum(bank(7, 0, 256), [(a("pair"), ("eqb", 0, 256))])
-    to_a(bank(2, 64, 64), "ehl", "t2", O + 1024)
+    to_a(bank(2, 0, 64), "ehl", "t2", O)
 
     def back(eng, c0, c1):
         eng(("g5", 16 * c0, 16 * c1), ind("t2", 0, W, "pco", c0, c1))
@@ -512,41 +513,40 @@ def rank_program(g, core, T, topo):
     tt(("xm", 0, 256), ("xcb", 0, 256), bank(6, 0, 256), A.mult)
     tt(("xxb", 0, 256), ("xm", 0, 256), bank(7, 256, 256), A.add)
     send("4")
-    iota(("lw", REP0, REP0 + V), [[0, V]], 255, 0)
+    iota(("yy", REP0, REP0 + V), [[0, V]], 0, 0)
     to_a(bank(3, 0, 64), "ehl", "g5", 0)
-    back(cp, 64, 96)
-    back(sc, 96, 128)
-    to_a(bank(3, 64, 64), "ehl", "g5", 1024)
+    back(cp, 64, 88)
+    back(sc, 88, 128)
+    to_a(bank(5, 0, 64), "ehl", "g5", 1024)
     alias("4")
+    for h in range(2):
+        c0, c1 = 64 * h, 64 * h + 64
+        tt(bank(6, c0, 64), bank(3 + 2 * h, 0, 64), ("va", c0, c1), A.is_equal)
+        tt(("mt", c0, c1), ("uj", c0, c1), bank(6, c0, 64), A.mult)
+        cp(("mo", c0, c1), ("mt", c0, c1))
+    for h in range(2):
+        sc(("xg", Q * h, Q * h + Q), ind("xe", 0, W, "mo", 32 * h, 32 * h + 32))
+    to_a(bank(2, 64, 64), "ehl", "t2", O + 1024)
+    for h in range(2):
+        mm([(bank(h), a("idb"), ("xg", Q * h, Q * h + Q), False, True)])
+        sc(("xx", Q * h, Q * h + Q), bank(h))
     tt(tmp[3], bank(2, 0, 128), a("va"), A.is_lt)
-    tt(tmp[0], bank(3, 0, 128), a("va"), A.is_equal)
-    tt(a("mt"), a("uj"), tmp[0], A.mult)
-    cp(a("mo"), a("mt"))
     tt(a("lamf"), a("mt"), tmp[3], A.mult)
     ts(a("nr"), a("lamf"), 0, A.is_gt)
-    tt(("xx", 0, XV), ind("xe", 0, W, "mo", 0, XV // 16), ("x2", 0, XV), A.add)
-    for h in range(2):
-        c0 = XV + half * h
-        sc(("xg", half * h, half * h + half), ind("xe", 0, W, "mo", c0 // 16, (c0 + half) // 16))
+    tt(("xx", 1024, V), ind("xe", 0, W, "mo", 64, 128), ("x2", 0, 1024), A.add)
 
-    def weights(banks, q):
-        for d in range(D):
-            msum(bank(banks[d]), [(a("sel8"), ("w8", V * d + Q * q, V * d + Q * q + Q))])
-    mm([(bank(4, 256, 128), a("idn"), a("nr"), False, True)])
+    def weights(banks, q, d0=0):
+        for d, bk in enumerate(banks, d0):
+            msum(bank(bk), [(a("sel8"), ("w8", V * d + Q * q, V * d + Q * q + Q))])
+    msum(bank(7, 0, 256), [(a("gn"), ("pgw", 512, 768))])
     msum(bank(4, 0, 128), [(a("gn"), a("nr"))])
     msum(bank(4, 128, 128), [(a("nt"), a("nr"))])
-    for h in range(2):
-        mm([(bank(h, 0, half), a("idb"), ("xg", half * h, half * h + half), False, True)])
-        sc(("xx", XV + half * h, XV + half * h + half), bank(h, 0, half))
-    weights((3, 5, 7), 0)
+    msum(bank(6), [(a("gn"), ("pgw", 0, 512))])
+    weights((3, 5), 0)
     weights((0, 1, 2), 2)
     scan(a("inc"), a("six"), bank(4, 0, 128), col(14), A.add, A.subtract)
     tt(a("nnx"), a("inc"), bank(4, 128, 128), A.add)
-    tt(a("lamx"), a("lamf"), bank(4, 256, 128), A.max)
     ts(a("no"), a("nnx"), STEP - REP0, A.add)
-    tt(a("rmin"), a("nnx"), bank(4, 256, 128), A.min)
-    ts(a("lam"), a("lamx"), -O, A.add)
-    ts(a("rhoo"), a("rmin"), STEP, A.add)
     arrive("4")
 
     def part(name, q, c0=0):
@@ -558,73 +558,63 @@ def rank_program(g, core, T, topo):
 
     def times(d, q, bk, out=None):
         tt(out or part("p%d" % d, q), part("p%d" % d, q), bank(bk), A.mult)
+    sc(("pg", 0, 768), ind("xx", 0, L, "bnb", 0, 48))
     gathers(0)
-    cp(("nx", 0, NXV), ind("hl", O, O + V, "no", 0, NXV // 16))
+    cp(("nx", 0, Q), ind("hl", O, O + V, "no", 0, Q // 16))
+    tt(("pg", 0, 512), ("pg", 0, 512), bank(6), A.mult)
+    tt(bank(7, 0, 256), ("pg", 512, 768), bank(7, 0, 256), A.mult)
+    tt(bank(7, 0, 256), ("pg", 0, 256), bank(7, 0, 256), A.add)
+    tt(("sb", 0, 256), ("pg", 256, 512), bank(7, 0, 256), A.add)
+    send("5")
+    weights((7,), 0, 2)
+    cp(("nx", Q, NXV), ind("hl", O, O + V, "no", Q // 16, NXV // 16))
     gathers(2)
     gathers(1)
+    gathers(3)
     sc(("nx", NXV, V), ind("hl", O, O + V, "no", NXV // 16, 128))
     sc(("nxb", 0, 256), ind("nx", 0, V, "blo", 0, 16))
     send("6")
-    gathers(3)
+    alias("5")
     alias("6")
-    order = ((0, (3, 5, 7)), (2, (0, 1, 2)), (1, (4, 5, 7)), (3, (6, 1, 2)))
-    times(0, 0, 3, bank(3))
+
+    def summed(d):
+        mm([(bank(5), a("idf"), part("p%d" % d, 0), d == 0, d == 2)])
+    for d, bk in enumerate((3, 5, 7)):
+        times(d, 0, bk)
+        if d == 0:
+            weights((4, 6, 3), 1)
+    summed(0)
+    summed(1)
+    order = ((2, (0, 1, 2)), (1, (4, 6, 3)), (3, (7, 1, 2)))
+    times(0, 2, 0, bank(0))
     for i, (q, bk) in enumerate(order):
         times(1, q, bk[1])
         times(2, q, bk[2])
         tt(bank(bk[0]), part("p1", q), bank(bk[0]), A.add)
+        if i == 0:
+            weights(order[2][1], 3)
+            summed(2)
+            sc(part("sx", 0, O), bank(5))
+        if i == 1:
+            msum(bank(0, 0, 128), [(a("idf"), a("vo")), (a("idn"), a("nr"))])
         if i < 2:
-            weights(order[i + 2][1], order[i + 2][0])
-        if i < 3:
             times(0, order[i + 1][0], order[i + 1][1][0], bank(order[i + 1][1][0]))
-        if q % 2:
-            tt(part("sx", q, O), part("p2", q), bank(bk[0]), A.add)
-        else:
-            tt(bank(bk[0]), part("p2", q), bank(bk[0]), A.add)
-            sc(part("sx", q, O), bank(bk[0]))
-    sc(("sb", 0, 256), ind("sx", O, O + V, "blo", 0, 16))
-    send("5")
-    alias("5")
-    lst = ind("lw", 0, REP0 + V, "rhoo", 0, 128)
-    cp(lst, ("hl", O, O + V))
-    for q in (3, 1):
-        sc(part("p0", q), part("sx", q, O))
+        tt(part("sx", q, O), part("p2", q), bank(bk[0]), A.add)
+    tt(a("rmin"), a("nnx"), bank(0, 0, 128), A.min)
+    tt(a("lamx"), a("lamf"), bank(0, 0, 128), A.max)
+    ts(a("rhoo"), a("rmin"), STEP, A.add)
+    ts(a("lam"), a("lamx"), -O, A.add)
+    arrive("5")
+    cuts = (V, 1792, 1280, 768, 256, 0)
+    for c1, c0 in zip(cuts, cuts[1:]):
+        sc(("p0", c0, c1), ind("sx", 0, W, "mo", c0 // 16, c1 // 16))
+    for i, (c1, c0) in enumerate(zip(cuts, cuts[1:])):
+        tt(ind("yy", 0, REP0 + c1, "rhoo", c0 // 16, c1 // 16), ("p0", c0, c1), ("sx", O + c0, O + c1), A.add)
+        dma("y", "y%d" % i, T.y[:, c0:c1], T.yy[:, REP0 + c0:REP0 + c1], [("yy", REP0 + c0, REP0 + c1)], [])
     arrive("6")
     for h in range(2):
         sc(("cg", 1024 * h, 1024 * h + 1024), ind("nx", 0, L, "lam", 64 * h, 64 * h + 64))
         to_a(bank(1, 64 * h, 64), "ehl", "cg", 1024 * h)
-    for h in (1, 0):
-        to_a(bank(5 + 2 * h, 0, 64), "ehl", "lw", REP0 + 1024 * h)
-    arrive("5")
-
-    def mates(q):
-        return ind("sx", 0, W, "mo", 32 * q, 32 * q + 32)
-
-    def values(eng, q, c0, c1):
-        eng(("yy", Q * q + 16 * c0, Q * q + 16 * c1), ind("sp", Q * q, V + 8, "l1", 32 * q + c0, 32 * q + c1))
-
-    def store(q):
-        dma("y", "y%d" % q, T.y[:, Q * q:Q * q + Q], T.yy[:, Q * q:Q * q + Q], [part("yy", q)], [])
-    def reps(q):
-        ts(("l1", 32 * q, 32 * q + 32), bank(5 + 2 * (q // 2), 32 * (q % 2), 32), -base - Q * q, A.add, V - Q * q, A.min)
-    sc(part("p1", 2), mates(2))
-    sc(part("p1", 0), mates(0))
-    tt(part("sp", 3), mates(3), part("p0", 3), A.add)
-    cp(a("cmf"), bank(1, 0, 128))
-    dma("y", "cm", T.cm[:], T.cmf[:], [a("cmf")], [])
-    tt(part("sp", 2), part("p1", 2), bank(0), A.add)
-    reps(3)
-    reps(2)
-    values(sc, 3, 0, 32)
-    store(3)
-    tt(part("sp", 1), mates(1), part("p0", 1), A.add)
-    reps(1)
-    reps(0)
-    values(sc, 2, 0, 32)
-    store(2)
-    tt(part("sp", 0), part("p1", 0), bank(3), A.add)
-    values(sc, 1, 0, 32)
-    store(1)
-    values(cp, 0, 0, 32)
-    store(0)
+    sc(a("cmf"), bank(1, 0, 128))
+    dma("s", "cm", T.cm[:], T.cmf[:], [a("cmf")], [])
     need("g", [("loc", sent[0])] + [(s, count[s]) for s in ("v", "s", "t", "p")] + sorted(totals.items()))

@@ -7,9 +7,10 @@ O = 16
 W = O + L
 STEP, GONE, KEEP = 4096, 16384, 32768
 REP0 = 2080
-NXV = 1152
+T1V = 256
+NX1 = 1536
 Q = 512
-LISTS = "gm gf idf six va vo w0s w1s wm ta tb tc pa c32 zf ua mt lamf inc nnx rmin lamx".split()
+LISTS = "gm gf idf va vo w1s wm ta tb tc pa c32 zf ua mt lamf inc nnx rmin lamx".split()
 
 
 def buffers(*groups):
@@ -23,8 +24,8 @@ def buffers(*groups):
 SCRATCH = buffers(
     ("bli lr0 bsh bms ubi ubj", 16, "int32"), ("nbi", 384, "int32"), ("pi", 8, "int32"), ("bki bkj", 48, "int32"),
     ("ui uj", 128, "int32"), ("r0", 2, "int32"),
-    ("wa", 384, "bfloat16"), ("w8", 6144, "bfloat16"), ("s0 s1", 160, "bfloat16"), ("e1n ehl", 144, "bfloat16"),
-    ("gn nt nr g10 g20 g21 idb idp idn pair sel8", 128, "bfloat16"), ("xe hl t2", W, "bfloat16"), ("m1 nx", L, "bfloat16"),
+    ("wa", 384, "bfloat16"), ("w8", 6144, "bfloat16"), ("wb", V, "bfloat16"), ("s0 s1", 160, "bfloat16"), ("e1n ehl", 144, "bfloat16"),
+    ("gn nt rep g10 g20 g21 idb idp idn pair sel8", 128, "bfloat16"), ("xe hl t2", W, "bfloat16"), ("m1 nx", L, "bfloat16"),
     ("xb m1b t2b nxb hlb eqb", 256, "bfloat16"), ("fb pgw", 768, "bfloat16"),
     ("f0 f1 f2 g5 cg", V, "bfloat16"), ("x2 xg", 1024, "bfloat16"), ("rX r2 r3 r6", C, "bfloat16"),
     ("blo pcb bmo ro1 lr1 gho zz bpo", 16, "uint16"), ("r1", 2, "uint16"), ("boff bnb", 48, "uint16"),
@@ -32,8 +33,8 @@ SCRATCH = buffers(
     ("pc", 24, "float32"), ("ub zb cb id16 kk kt bc bq", 16, "float32"), ("r4 r5", C, "float32"), ("g48", 400, "float32"),
     ("bkf", 48, "float32"), ("xi", 160, "float32"), ("eall", 144, "float32"),
     ("cmf", 128, "float32"), ("lists", 128 * len(LISTS), "float32"),
-    ("nbf ks ws", 384, "float32"), ("jm m16 m0 bs pgs gbb xcb xm xxb sb", 256, "float32"), ("pg bmask", 768, "float32"),
-    ("gs", 1024, "float32"), ("rt t1 xx", L, "float32"), ("sx", W, "float32"), ("p0 p1 p2", V, "float32"),
+    ("nbf ks ws", 384, "float32"), ("jm m16 m0 bs pgs gbb xcb xm xxb sb", 256, "float32"), ("pg", 768, "float32"),
+    ("bmask", 256, "float32"), ("rt t1 xx", L, "float32"), ("sx", W, "float32"), ("p0 p1 p2", V, "float32"),
     ("yy", REP0 + V, "float32"))
 PSUM = {"q%d" % i: 1024 for i in range(4)}
 for _n in PSUM:
@@ -43,8 +44,8 @@ ROWS8 = ("w8", "sel8")
 EXCH = {"0": ("bli", "lr0", 0, 2), "1": ("ro1", "lr1", 0, 2), "X": ("xb", "xe", O + V, C), "2": ("m1b", "m1", V, C),
         "3": ("t2b", "t2", O + V, C), "4": ("xxb", "xx", V, C), "5": ("sb", "sx", O + V, C), "6": ("nxb", "nx", V, C)}
 ORDER = ["0", "1", "2", "X", "3", "4", "5", "6"]
-UNHURRIED = ("0", "X")
-DMAS = ["bl", "z0", "z1", "nb", "w0", "w1", "w2", "x", "x2", "w8", "sel", "cm"] + ["y%d" % i for i in range(5)]
+UNHURRIED = ("0", "X", "5")
+DMAS = ["bl", "z0", "z1", "nb", "w0", "w1", "w2", "x", "x2", "w8", "wb", "a1", "a2", "sel", "cm"] + ["y%d" % i for i in range(5)]
 SEMAPHORES = (["v", "s", "t", "p", "loc", "rloc"] + ["d" + n for n in DMAS] + ["arr" + k for k in ORDER]
               + ["hop" + k for k in ORDER])
 
@@ -225,9 +226,10 @@ def rank_program(g, core, T, topo):
         n = out[2] - out[1]
         mm([(out, (lhs, 15 - k, 143 - k), (src, base + k, base + 16 * n, 16), k == 0 and not onto, k == 15) for k in range(16)])
 
-    def dma(queue, sem, out, in_, reads, writes):
+    def dma(queue, sem, out, in_, reads, writes, adding=False):
         need(queue, deps(queue, reads, writes))
-        q_of[queue].dma_start(out, in_).then_inc(T.sem["d" + sem], 16)
+        ins = g.dma_start(out, in_, accum_op=A.add) if adding else q_of[queue].dma_start(out, in_)
+        ins.then_inc(T.sem["d" + sem], 16)
         totals["d" + sem] = totals.get("d" + sem, 0) + 16
         note(queue, reads, writes, ("d" + sem, totals["d" + sem]))
 
@@ -268,9 +270,9 @@ def rank_program(g, core, T, topo):
         totals["arr" + k] = n
         note("net", [], [(land, c0, c0 + w * N)], ("arr" + k, n))
 
-    def alias(k):
+    def alias(k, eng=sc):
         src, land, c0, w = EXCH[k]
-        sc((land, c0 + w * rank, c0 + w * rank + w), (src, w * rank, w * rank + w))
+        eng((land, c0 + w * rank, c0 + w * rank + w), (src, w * rank, w * rank + w))
 
     def col(i):
         return ("pc", i, i + 1)
@@ -310,11 +312,9 @@ def rank_program(g, core, T, topo):
     cp(col(4), ("pi", 1, 2))
     tt(col(5), ("pi", 0, 1), ("pi", 1, 2), A.subtract)
     ts(("id16", 0, 16), ("xi", 0, 16), col(4), A.is_equal)
-    ts(a("idf"), ("xi", 16, 144), col(1), A.is_equal)
+    ts(a("idp"), ("xi", 16, 144), col(1), A.is_equal, STEP, A.mult)
     ts(a("gf"), a("gm"), col(5), A.is_equal)
     dma("y", "z1", T.lr1[:, own[0]:own[1]], T.zz[:, 0:2], [("zz", 0, 2)], [("lr1",) + own])
-    dma("y", "x2", T.x2[:], T.x[:, 1024:V], [], [("x2", 0, 1024)])
-    dma("y", "w8", T.w8[0:8, :], T.w[:], [], [("w8", 0, D * V)])
     sa(("rt", 0, 128), ("xi", 0, 128), 1, base)
     for n in (128, 256, 512, 1024):
         sa(("rt", n, 2 * n), ("rt", 0, n), 1, n)
@@ -334,15 +334,14 @@ def rank_program(g, core, T, topo):
                         gg == 0, gg == 1))
     mm(grp)
     ts(("bsh", 0, 16), ("bli", 0, 16), 4, A.arith_shift_right)
-    ts(("m16", 0, 256), ("jm", 0, 256), col(4), A.is_equal)
-    for d in range(D):
-        ts(("boff", 16 * d, 16 * d + 16), ("bsh", 0, 16), 128 * d, A.add)
+    ts(a("idn"), a("idp"), -1, A.mult)
+    cp(("boff", 0, 16), ("bsh", 0, 16))
     nb = [("nbi", 128 * d, 128 * d + 128) for d in range(D)]
     tmp = [bank(6, 128 * i, 128) for i in range(4)]
     tmq = [bank(5, 128 * i, 128) for i in range(4)]
     sc(("bmask", 0, 256), ind("id16", 0, 16, "bmo", 0, 16))
-    sa(("m0", 0, 256), ("jm", 0, 256), 1, 0, SIGN)
     sc(("gbb", 0, 256), ind("rt", 0, V, "blo", 0, 16))
+    sa(("m0", 0, 256), ("jm", 0, 256), 1, 0, SIGN)
     sc(("rt",) + mine, ("gbb", C * rank, C * rank + C))
     cp(tmq[0], nb[0])
     tt(tmp[0], nb[1], tmq[0], A.subtract)
@@ -360,53 +359,63 @@ def rank_program(g, core, T, topo):
     tt(("pg", 0, 256), ind("pa", 0, 128, "boff", 0, 16), ("bmask", 0, 256), A.mult)
     msum(bank(7, 0, 256), [(a("gf"), ("pg", 0, 256))])
     cp(a("po"), a("pa"))
-    sa(a("idp"), a("idf"), STEP, 0)
-    sa(a("idn"), a("idf"), -STEP, 0)
-    for d in (1, 2):
-        sc(("bmask", 256 * d, 256 * d + 256), ("bmask", 0, 256))
     sc(("ws", 0, 384), bank(2, 0, 384))
+    ts(("m16", 0, 256), ("jm", 0, 256), col(4), A.is_equal)
     tt(a("g21"), wp[2], a("w1s"), A.is_gt)
     tt(a("g20"), wp[2], a("ws"), A.is_gt)
     signs = ((("idn", "g10"), ("idn", "g20")), (("idp", "g10"), ("idn", "g21")), (("idp", "g20"), ("idp", "g21")))
     for d in range(D):
         msum(bank(3, 128 * d, 128), [(a(m), a(z)) for m, z in signs[d]])
-    for j in range(2):
-        cp(("blo48", 1 + j, 25, 3), ("bli", j, 16, 2))
-    ts(col(7), col(4), 1, A.is_equal)
-    ts(col(8), col(4), 1, A.not_equal)
+    for d in range(D):
+        ts(a("nbf", d), nb[d], O + STEP * (2 - d), A.add)
     tt(("bs", 0, 256), ("m16", 0, 256), bank(7, 0, 256), A.mult)
     scan(("pgs", 0, 256), ("m0", 0, 256), ("bs", 0, 256), 0.0, A.mult, A.add)
     bp = ("pgs", 15, 256, 16)
-
-    def name_slots(out, src, kk):
-        tt(("kt", 0, 16), src, (kk, 0, 16), A.add)
-        ts((out, 0, 16), ("kt", 0, 16), 48 * rank + 15, A.max, 48 * rank + 48, A.min)
-    name_slots("ro1", bp, "kk")
+    tt(("kt", 0, 16), bp, ("kk", 0, 16), A.add)
+    ts(("ro1", 0, 16), ("kt", 0, 16), 48 * rank + 15, A.max, 48 * rank + 48, A.min)
     send("1")
-    sc(a("gn"), a("gf"))
-    dma("y", "sel", T.sel8[0:8, :], T.gn[0::16, :], [a("gn")], [a("sel8")])
-    sc(("t1", 1024, V), ind("rt", 0, L, "po", 64, 128))
-    sc(("xb", 0, 256), ind("xe", O, O + V, "blo", 0, 16))
-    run("g", [a("gn")], [a("nt")], lambda: g.affine_select(T.nt[:], T.gn[:], [[-1, 128]], A.is_gt, 0.0, 0, 1))
-    ts(col(6), col(5), 15, A.add)
-    ts(("bc", 0, 16), ("xi", 0, 16), col(8), A.mult)
-    ts(col(12), col(8), 16 * rank, A.mult)
-    for d in range(D):
-        ts(a("nbf", d), nb[d], O + STEP * (2 - d), A.add)
-    ts(("eall", 0, 143), ("xi", 0, 143), col(6), A.is_equal)
+    for t, c in (("hl", 255), ("t2", 255), ("xe", 0), ("sx", 0)):
+        iota((t, 0, O), [[0, O]], c, 0)
+
+    def border(out, src, d):
+        tt((out, 256 * d, 256 * d + 256), ind(src, 0, 384, "boff", 16 * d, 16 * d + 16), ("bmask", 0, 256), A.mult)
+    high, low = ("id16", 0, 1), ("id16", 1, 2)
+    sa(a("idf"), a("idp"), 1.0 / STEP, 0)
+    sc(("t1", T1V, V), ind("rt", 0, L, "po", T1V // 16, 128))
     tt(("ks", 0, 384), ("nbf", 0, 384), bank(3, 0, 384), A.add)
-    tt(("pg", 0, 768), ind("ks", 0, 384, "boff", 0, 48), ("bmask", 0, 768), A.mult)
-    to_a(bank(4, 64, 48), "eall", "pg")
-    cp(("t1", 0, 1024), ind("rt", 0, L, "po", 0, 64))
+    for d in (1, 2):
+        ts(("boff", 16 * d, 16 * d + 16), ("bsh", 0, 16), 128 * d, A.add)
+    kb = [("q%d" % d, Q - 64, Q + 64) for d in range(D)]
+    for d in range(D):
+        for h in range(2):
+            mm([((kb[d][0], Q - 64 + 64 * h, Q + 64 * h), a("idf"), ("ks", 128 * d + 64 * h, 128 * d + 64 * h + 64), True, False)])
+    ts(col(6), col(5), 15, A.add)
+    border("pg", "ks", 0)
+    ts(("eall", 0, 143), ("xi", 0, 143), col(6), A.is_equal)
+    for d in (1, 2):
+        border("pg", "ks", d)
+    to_a(bank(7, 128, 48), "eall", "pg")
+    for j in range(2):
+        cp(("blo48", 1 + j, 25, 3), ("bli", j, 16, 2))
+    sc(("xb", 0, 256), ind("xe", O, O + V, "blo", 0, 16))
+    sa(col(9), high, -GONE, 0)
+    sa(col(8), low, -1, 1)
+    sa(col(12), low, -16 * rank, 16 * rank)
+    sa(("bc", 0, 16), ("xi", 0, 16), col(8), 0)
+    sa(("bq", 0, N), ("xi", 0, N), 16, -16 * rank)
+    sa(("e1n", 0, 143), ("eall", 0, 143), col(9), 0)
+    sa(("hl", O, O + 128), ("xi", 0, 128), low, col(12))
+    sa(("bq", 0, N), ("bq", 0, N), col(8), 0)
+
+    def twice(i):
+        sa(("hl", O + 128 * i, O + 256 * i), ("hl", O, O + 128 * i), 1, ("bc", i, i + 1))
+    twice(1)
+    twice(2)
+    sc(("g48", 0, 400), ind("rt", 0, L, "blo48", 0, 25))
+    cp(("t1", 0, T1V), ind("rt", 0, L, "po", 0, T1V // 16))
     cp(("bpo", 0, 16), bp)
     cp(("t1",) + mine, ("ind", ("t1", 0, V), ("blo",) + own))
-    sc(("g48", 0, 400), ind("rt", 0, L, "blo48", 0, 25))
-    sc(("q0", 0, 1024), ("rt", 1024, V))
-    sa(("hl", O, O + 128), ("xi", 0, 128), col(7), col(12))
-    for i in (1, 2, 4, 8):
-        sa(("hl", O + 128 * i, O + 256 * i), ("hl", O, O + 128 * i), 1, ("bc", i, i + 1))
-    ts(col(9), col(4), 0, A.is_equal, -GONE, A.mult)
-    ts(("e1n", 0, 143), ("xi", 0, 143), col(6), A.is_equal, col(9), A.mult)
+    cp(("nbo", 0, 384), ("nbi", 0, 384))
     arrive("1")
     for eng, q0, q1 in ((cp, 0, rank), (sc, rank + 1, N)):
         if q0 < q1:
@@ -414,93 +423,85 @@ def rank_program(g, core, T, topo):
     tt(("m1b", 0, 256), ind("t1", 0, L, "bpo", 0, 16), ("gbb", 0, 256), A.is_equal)
     send("2")
     send("X")
-    sc(("gs", 0, 1024), ind("t1", 0, L, "po", 64, 128))
-    tt(("m1", 0, 1024), ind("t1", 0, L, "po", 0, 64), ("rt", 0, 1024), A.is_equal)
-    to_a(bank(6, 128, 16), "e1n", "m1b")
-    to_a(bank(7, 0, 64), "e1n", "m1", 0)
-    tt(("m1", 1024, V), ("gs", 0, 1024), ("q0", 0, 1024), A.is_equal)
-    to_a(bank(7, 64, 64), "e1n", "m1", 1024)
-    sc(("bkf", 0, 48), bank(4, 64, 48))
-    alias("2")
-    sa(("cb", 0, 16), bp, -1.0 / GONE, -(O + KEEP) / GONE)
-    sa(a("c32"), a("pa"), -1.0 / GONE, -(O + KEEP) / GONE)
-    cp(("bki", 0, 48), ("bkf", 0, 48))
     arrive("0")
     cp(("gho", 0, 16), ("lr0", 0, 16))
-    ts(("bq", 0, N), ("bc", 0, N), 16, A.mult, col(12), A.subtract)
-    ts(("bkj", 0, 48), ("bki", 0, 48), STEP - 1, A.bitwise_and)
-    ts(col(15), col(4), base, A.add)
-    ts(("bnb", 0, 48), ("bkj", 0, 48), -O, A.add)
-    alias("X")
-    sc(("hlb", 0, 256), ind("hl", O, O + V, "blo", 0, 16))
-    sc(a("idb"), a("idf"))
+    to_a(bank(6, 128, 16), "e1n", "m1b")
+    twice(4)
+    twice(8)
+    sc(("bkf", 0, 48), bank(7, 128, 48))
+    for h in range(2):
+        tt(("m1", 1024 * h, 1024 * h + 1024), ind("t1", 0, L, "po", 64 * h, 64 * h + 64), ("rt", 1024 * h, 1024 * h + 1024),
+           A.is_equal)
+        to_a(bank(7, 64 * h, 64), "e1n", "m1", 1024 * h)
+    sa(("cb", 0, 16), bp, -1.0 / GONE, -(O + KEEP) / GONE)
+    sa(a("c32"), a("pa"), -1.0 / GONE, -(O + KEEP) / GONE)
     for q in range(N):
         sa(("hl", O + V + C * q, O + V + C * q + C), ind("hl", O, O + V, "gho", 2 * q, 2 * q + 2), 1, ("bq", q, q + 1))
-    sa(a("va"), ("xi", 0, 128), 16, col(15))
+    alias("2")
+    cp(("bki", 0, 48), ("bkf", 0, 48))
     tt(("zb", 0, 16), ("cb", 0, 16), bank(6, 128, 16), A.mult)
-    kb = [("q%d" % d, Q - 64, Q + 64) for d in range(D)]
+    ts(("bkj", 0, 48), ("bki", 0, 48), STEP - 1, A.bitwise_and)
+    ts(("bnb", 0, 48), ("bkj", 0, 48), -O, A.add)
     mm([(bank(6, 0, 48), a("idf"), ("bkf", 0, 48), True, False)])
-    for d in range(D):
-        for h in range(2):
-            mm([((kb[d][0], Q - 64 + 64 * h, Q + 64 * h), a("idf"), ("ks", 128 * d + 64 * h, 128 * d + 64 * h + 64), True, False)])
-    cp(("nbo", 0, 384), ("nbi", 0, 384))
-    ts(col(10), col(4), 0, A.is_equal, 128, A.mult)
-    ts(col(13), col(4), 2, A.is_lt)
-    tt(col(11), col(10), col(7), A.add)
-    ts(col(14), col(4), -16 - (STEP - REP0), A.add)
-    ts(("ehl", 0, 143), ("xi", 0, 143), col(6), A.is_equal, col(11), A.mult)
-    tt(a("zf"), a("c32"), bank(7, 0, 128), A.mult)
-    for t, c in (("hl", 255), ("t2", 255), ("xe", 0), ("sx", 0)):
-        fill((t, 0, O), c)
-    msum(bank(7, 256, 256), [(a("idb"), ("xb", 0, 256))])
+    sa(col(11), high, 128, low)
+    sa(col(13), high, 1, low)
+    sa(col(15), col(4), 1, base)
+    alias("X")
+    sa(a("va"), ("xi", 0, 128), 16, col(15))
+    sc(a("gn"), a("gf"))
+    dma("y", "sel", T.sel8[0:8, :], T.gn[0::16, :], [a("gn")], [a("sel8")])
+    sa(("ehl", 0, 143), ("eall", 0, 143), col(11), 0)
+    sa(a("idb"), a("idp"), 1.0 / STEP, 0)
+    sc(("hlb", 0, 256), ind("hl", O, O + V, "blo", 0, 16))
+    for d in (1, 2):
+        border("pgw", "ws", d)
     arrive("2")
     sc(("fb", 0, 384), ind("m1", 0, L, "bnb", 0, 24))
     cp(("fb", 384, 768), ind("m1", 0, L, "bnb", 24, 48))
     to_a(bank(6, 0, 48), "e1n", "fb", 0, True)
 
-    def flags(eng, d, h):
-        eng(("f%d" % d, 1024 * h, 1024 * h + 1024), ind("m1", 0, L, "nbo", 128 * d + 64 * h, 128 * d + 64 * h + 64))
-
-    def keys(d, h):
+    def flags(d, h, n):
+        for eng, c0, c1 in ((cp, 64 * h, 64 * h + n), (sc, 64 * h + n, 64 * h + 64)):
+            if c0 < c1:
+                eng(("f%d" % d, 16 * c0, 16 * c1), ind("m1", 0, L, "nbo", 128 * d + c0, 128 * d + c1))
         to_a((kb[d][0], kb[d][1] + 64 * h, kb[d][1] + 64 * h + 64), "e1n", "f%d" % d, 1024 * h, True)
 
-    def choose(z, k, u, ui, uj, meanwhile=None):
+    def choose(z, k, u, ui, uj):
         tt(u, z, k[0], A.max)
         tt(u, u, k[1], A.max)
-        if meanwhile:
-            meanwhile()
         tt(ui, u, k[2], A.max)
         ts(uj, ui, STEP - 1, A.bitwise_and)
-    flags(cp, 0, 0)
-    flags(sc, 0, 1)
-    keys(0, 0)
+    flags(0, 0, 32)
+    flags(1, 0, 24)
     choose(("zb", 0, 16), [bank(6, 16 * d, 16) for d in range(D)], ("ub", 0, 16), ("ubi", 0, 16), ("ubj", 0, 16))
     cp(("pcb", 0, 16), ("ubj", 0, 16))
     cp(("t2b", 0, 256), ind("hl", 0, W, "pcb", 0, 16))
     send("3")
-    keys(0, 1)
-    flags(sc, 1, 1)
-    flags(cp, 1, 0)
-    keys(1, 1)
-    keys(1, 0)
-    flags(sc, 2, 1)
-    cp(("f2", 0, 640), ind("m1", 0, L, "nbo", 256, 296))
-    sc(("f2", 640, 1024), ind("m1", 0, L, "nbo", 296, 320))
-    keys(2, 1)
-    keys(2, 0)
+
+    def late_loads(after):
+        dma("y", "x2", T.x2[:], T.x[:, 1024:V], [after], [("x2", 0, 1024)])
+        dma("y", "w8", T.w8[0:8, :], T.w[:], [], [("w8", 0, D * V)])
+        for c in range(16):
+            dma("y", "wb", T.wb[c::16, :], T.w[:, 0:V], [], [])
+        note("y", [], [("wb", 0, V)], ("dwb", totals["dwb"]))
+    tt(a("zf"), a("c32"), bank(7, 0, 128), A.mult)
+    for d, h, n in ((2, 0, 10), (0, 1, 32), (1, 1, 32), (2, 1, 32)):
+        flags(d, h, n)
+    late_loads(("f1", 1024, V))
     arrive("X")
     sc(("xcb", 0, 256), ind("xe", 0, W, "pcb", 0, 16))
-    alias("3")
-    sa(a("vo"), a("va"), 1, O - base)
+    msum(bank(7, 256, 256), [(a("idb"), ("xb", 0, 256))])
+    for h in range(2):
+        c0, c1 = 64 * h, 64 * h + 64
+        choose(("zf", c0, c1), [(k[0], k[1] + c0, k[1] + c1) for k in kb], ("ua", c0, c1), ("ui", c0, c1), ("uj", c0, c1))
+        cp(("pco", c0, c1), ("uj", c0, c1))
     sa(a("pair"), a("gf"), col(13), 0)
-    sa(a("six"), a("gf"), 0, 16)
-    choose(a("zf"), kb, a("ua"), a("ui"), a("uj"),
-           lambda: tt(("pgw", 0, 768), ind("ws", 0, 384, "boff", 0, 48), ("bmask", 0, 768), A.mult))
-    cp(a("pco"), a("uj"))
-    cp(("t2", O, O + 1024), ind("hl", 0, W, "pco", 0, 64))
-    sc(("t2", O + 1024, O + V), ind("hl", 0, W, "pco", 64, 128))
+    sc(("t2", O, O + 1024), ind("hl", 0, W, "pco", 0, 64))
+    cp(("t2", O + 1024, O + 1600), ind("hl", 0, W, "pco", 64, 100))
+    sc(("t2", O + 1600, O + V), ind("hl", 0, W, "pco", 100, 128))
     for h in range(2):
         mm([(bank(h), a("idb"), ("xe", O + Q * h, O + Q * h + Q), True, False)])
+    alias("3", cp)
     arrive("3")
     tt(("eqb", 0, 256), ind("t2", 0, W, "pcb", 0, 16), ("hlb", 0, 256), A.is_equal)
     msum(bank(7, 0, 256), [(a("pair"), ("eqb", 0, 256))])
@@ -513,101 +514,114 @@ def rank_program(g, core, T, topo):
     tt(("xm", 0, 256), ("xcb", 0, 256), bank(6, 0, 256), A.mult)
     tt(("xxb", 0, 256), ("xm", 0, 256), bank(7, 256, 256), A.add)
     send("4")
+    run("g", [a("gn")], [a("nt")], lambda: g.affine_select(T.nt[:], T.gn[:], [[-1, 128]], A.is_ge, 0.0, 0, 1))
     iota(("yy", REP0, REP0 + V), [[0, V]], 0, 0)
     to_a(bank(3, 0, 64), "ehl", "g5", 0)
     back(cp, 64, 88)
     back(sc, 88, 128)
     to_a(bank(5, 0, 64), "ehl", "g5", 1024)
     alias("4")
+    sa(a("vo"), a("va"), 1, O - base - STEP)
     for h in range(2):
         c0, c1 = 64 * h, 64 * h + 64
         tt(bank(6, c0, 64), bank(3 + 2 * h, 0, 64), ("va", c0, c1), A.is_equal)
         tt(("mt", c0, c1), ("uj", c0, c1), bank(6, c0, 64), A.mult)
         cp(("mo", c0, c1), ("mt", c0, c1))
+        if h == 0:
+            border("pgw", "ws", 0)
     for h in range(2):
         sc(("xg", Q * h, Q * h + Q), ind("xe", 0, W, "mo", 32 * h, 32 * h + 32))
     to_a(bank(2, 64, 64), "ehl", "t2", O + 1024)
     for h in range(2):
         mm([(bank(h), a("idb"), ("xg", Q * h, Q * h + Q), False, True)])
         sc(("xx", Q * h, Q * h + Q), bank(h))
+    tt(("xx", 1024, V), ind("xe", 0, W, "mo", 64, 128), ("x2", 0, 1024), A.add)
     tt(tmp[3], bank(2, 0, 128), a("va"), A.is_lt)
     tt(a("lamf"), a("mt"), tmp[3], A.mult)
-    ts(a("nr"), a("lamf"), 0, A.is_gt)
-    tt(("xx", 1024, V), ind("xe", 0, W, "mo", 64, 128), ("x2", 0, 1024), A.add)
+    ts(a("rep"), a("lamf"), 0, A.is_equal)
 
     def weights(banks, q, d0=0):
         for d, bk in enumerate(banks, d0):
             msum(bank(bk), [(a("sel8"), ("w8", V * d + Q * q, V * d + Q * q + Q))])
     msum(bank(7, 0, 256), [(a("gn"), ("pgw", 512, 768))])
-    msum(bank(4, 0, 128), [(a("gn"), a("nr"))])
-    msum(bank(4, 128, 128), [(a("nt"), a("nr"))])
+    weights((0,), 1, 2)
+    msum(bank(4, 0, 128), [(a("gn"), a("rep"))])
+    msum(bank(4, 128, 128), [(a("nt"), a("rep"))])
     msum(bank(6), [(a("gn"), ("pgw", 0, 512))])
-    weights((3, 5), 0)
-    weights((0, 1, 2), 2)
-    scan(a("inc"), a("six"), bank(4, 0, 128), col(14), A.add, A.subtract)
-    tt(a("nnx"), a("inc"), bank(4, 128, 128), A.add)
-    ts(a("no"), a("nnx"), STEP - REP0, A.add)
+    msum(bank(7, 256, 128), [(a("idf"), a("vo")), (a("idp"), a("rep"))])
     arrive("4")
 
     def part(name, q, c0=0):
         return (name, c0 + Q * q, c0 + Q * q + Q)
 
-    def gathers(q):
-        for d in range(D):
-            sc(part("p%d" % d, q), ind("xx", 0, L, "nbo", 128 * d + 32 * q, 128 * d + 32 * q + 32))
+    def gather(d, q):
+        sc(part("p%d" % d, q), ind("xx", 0, L, "nbo", 128 * d + 32 * q, 128 * d + 32 * q + 32))
+
+    def added(q):
+        dma("g", "a%d" % q, ap(part("p0", q)), ap(part("p2", q)), [part("p0", q), part("p2", q)], [part("p0", q)], True)
 
     def times(d, q, bk, out=None):
         tt(out or part("p%d" % d, q), part("p%d" % d, q), bank(bk), A.mult)
+
+    def fused(c0, c1):
+        tt(("p0", c0, c1), ind("xx", 0, L, "nbo", c0 // 16, c1 // 16), ("wb", c0, c1), A.mult)
+
+    def summed(d):
+        mm([(bank(3), a("idf"), part("p%d" % d, 0), d == 0, d == 2)])
+
+    def plus(out, d, q, bk):
+        tt(out, part("p%d" % d, q), bank(bk), A.add)
     sc(("pg", 0, 768), ind("xx", 0, L, "bnb", 0, 48))
-    gathers(0)
-    cp(("nx", 0, Q), ind("hl", O, O + V, "no", 0, Q // 16))
-    tt(("pg", 0, 512), ("pg", 0, 512), bank(6), A.mult)
+    for d, q in ((1, 0), (2, 1), (2, 0), (2, 2), (1, 1), (1, 2), (1, 3), (2, 3)):
+        gather(d, q)
+    fused(0, Q)
+    scan(a("inc"), bank(4, 0, 128), a("nbf"), float(REP0 - STEP), A.add, A.min)
+    tt(a("nnx"), a("inc"), bank(4, 128, 128), A.subtract)
+    weights((5, 4), 0, 1)
+    weights((1,), 2, 2)
+    summed(0)
+    ts(a("no"), a("nnx"), STEP - REP0, A.add)
     tt(bank(7, 0, 256), ("pg", 512, 768), bank(7, 0, 256), A.mult)
+    tt(("pg", 0, 512), ("pg", 0, 512), bank(6), A.mult)
+    times(1, 0, 5)
+    weights((2,), 1, 1)
+    weights((6,), 2, 1)
+    summed(1)
     tt(bank(7, 0, 256), ("pg", 0, 256), bank(7, 0, 256), A.add)
+    fused(Q, 2 * Q)
     tt(("sb", 0, 256), ("pg", 256, 512), bank(7, 0, 256), A.add)
     send("5")
-    weights((7,), 0, 2)
-    cp(("nx", Q, NXV), ind("hl", O, O + V, "no", Q // 16, NXV // 16))
-    gathers(2)
-    gathers(1)
-    gathers(3)
-    sc(("nx", NXV, V), ind("hl", O, O + V, "no", NXV // 16, 128))
+    times(2, 1, 0)
+    added(1)
+    times(2, 0, 4)
+    fused(2 * Q, 3 * Q)
+    times(2, 2, 1)
+    added(2)
+    weights((0, 5), 3, 1)
+    summed(2)
+    sc(("nx", 0, V), ind("hl", O, O + V, "no", 0, 128))
     sc(("nxb", 0, 256), ind("nx", 0, V, "blo", 0, 16))
     send("6")
     alias("5")
-    alias("6")
-
-    def summed(d):
-        mm([(bank(5), a("idf"), part("p%d" % d, 0), d == 0, d == 2)])
-    for d, bk in enumerate((3, 5, 7)):
-        times(d, 0, bk)
-        if d == 0:
-            weights((4, 6, 3), 1)
-    summed(0)
-    summed(1)
-    order = ((2, (0, 1, 2)), (1, (4, 6, 3)), (3, (7, 1, 2)))
-    times(0, 2, 0, bank(0))
-    for i, (q, bk) in enumerate(order):
-        times(1, q, bk[1])
-        times(2, q, bk[2])
-        tt(bank(bk[0]), part("p1", q), bank(bk[0]), A.add)
-        if i == 0:
-            weights(order[2][1], 3)
-            summed(2)
-            sc(part("sx", 0, O), bank(5))
-        if i == 1:
-            msum(bank(0, 0, 128), [(a("idf"), a("vo")), (a("idn"), a("nr"))])
-        if i < 2:
-            times(0, order[i + 1][0], order[i + 1][1][0], bank(order[i + 1][1][0]))
-        tt(part("sx", q, O), part("p2", q), bank(bk[0]), A.add)
-    tt(a("rmin"), a("nnx"), bank(0, 0, 128), A.min)
-    tt(a("lamx"), a("lamf"), bank(0, 0, 128), A.max)
+    sc(part("sx", 0, O), bank(3))
+    fused(3 * Q, V)
+    times(1, 1, 2, bank(2))
+    times(1, 2, 6, bank(6))
+    tt(a("rmin"), a("nnx"), bank(7, 256, 128), A.min)
+    tt(a("lamx"), a("lamf"), bank(7, 256, 128), A.max)
+    times(1, 3, 0, bank(0))
+    times(2, 3, 5)
+    plus(bank(0), 0, 3, 0)
+    plus(part("sx", 1, O), 0, 1, 2)
+    plus(part("sx", 3, O), 2, 3, 0)
+    plus(part("sx", 2, O), 0, 2, 6)
     ts(a("rhoo"), a("rmin"), STEP, A.add)
     ts(a("lam"), a("lamx"), -O, A.add)
+    alias("6", cp)
     arrive("5")
     cuts = (V, 1792, 1280, 768, 256, 0)
     for c1, c0 in zip(cuts, cuts[1:]):
-        sc(("p0", c0, c1), ind("sx", 0, W, "mo", c0 // 16, c1 // 16))
+        (cp if c1 == V else sc)(("p0", c0, c1), ind("sx", 0, W, "mo", c0 // 16, c1 // 16))
     for i, (c1, c0) in enumerate(zip(cuts, cuts[1:])):
         tt(ind("yy", 0, REP0 + c1, "rhoo", c0 // 16, c1 // 16), ("p0", c0, c1), ("sx", O + c0, O + c1), A.add)
         dma("y", "y%d" % i, T.y[:, c0:c1], T.yy[:, REP0 + c0:REP0 + c1], [("yy", REP0 + c0, REP0 + c1)], [])

from concourse.mybir import AluOpType, ActivationFunctionType
from concourse.bass import DstId, RemoteDMATransfer

N, V, C, D = 8, 2048, 32, 3
L = V + N * C
O = 16
W = O + L
STEP, GONE, KEEP = 4096, 16384, 32768
REP0 = 2080
T1V = 256
NX1 = 1536
Q = 512
LISTS = "gm gf idf va vo w1s wm ta tb tc pa c32 zf ua mt lamf inc nnx rmin lamx".split()


def buffers(*groups):
    out = {}
    for names, width, dtype in groups:
        for n in names.split():
            out[n] = ("sbuf", [128, width], dtype)
    return out


SCRATCH = buffers(
    ("bli lr0 bsh bms ubi ubj", 16, "int32"), ("nbi", 384, "int32"), ("pi", 8, "int32"), ("bki bkj", 48, "int32"),
    ("ui uj", 128, "int32"), ("r0", 2, "int32"),
    ("wa", 384, "bfloat16"), ("w8", 6144, "bfloat16"), ("wb", V, "bfloat16"), ("s0 s1", 160, "bfloat16"), ("e1n ehl", 144, "bfloat16"),
    ("gn nt rep g10 g20 g21 idb idp idn pair sel8", 128, "bfloat16"), ("xe hl t2", W, "bfloat16"), ("m1 nx", L, "bfloat16"),
    ("xb m1b t2b nxb hlb eqb", 256, "bfloat16"), ("fb pgw", 768, "bfloat16"),
    ("f0 f1 f2 g5 cg", V, "bfloat16"), ("x2 xg", 1024, "bfloat16"), ("rX r2 r3 r6", C, "bfloat16"),
    ("blo pcb bmo ro1 lr1 gho zz bpo", 16, "uint16"), ("r1", 2, "uint16"), ("boff bnb", 48, "uint16"),
    ("blo48", 26, "uint16"), ("po pco mo lam no rhoo", 128, "uint16"), ("nbo", 384, "uint16"),
    ("pc", 24, "float32"), ("ub zb cb id16 kk kt bc bq", 16, "float32"), ("r4 r5", C, "float32"), ("g48", 400, "float32"),
    ("bkf", 48, "float32"), ("xi", 160, "float32"), ("eall", 144, "float32"),
    ("cmf", 128, "float32"), ("lists", 128 * len(LISTS), "float32"),
    ("nbf ks ws", 384, "float32"), ("jm m16 m0 bs pgs gbb xcb xm xxb sb", 256, "float32"), ("pg", 768, "float32"),
    ("bmask", 256, "float32"), ("rt t1 xx", L, "float32"), ("sx", W, "float32"), ("p0 p1 p2", V, "float32"),
    ("yy", REP0 + V, "float32"))
PSUM = {"q%d" % i: 1024 for i in range(4)}
for _n in PSUM:
    SCRATCH[_n] = ("psum", [128, PSUM[_n]], "float32")
SCRATCH["tr"] = ("sbuf", [128, D, 128], "bfloat16")
ROWS8 = ("w8", "sel8")
EXCH = {"0": ("bli", "lr0", 0, 2), "1": ("ro1", "lr1", 0, 2), "X": ("xb", "xe", O + V, C), "2": ("m1b", "m1", V, C),
        "3": ("t2b", "t2", O + V, C), "4": ("xxb", "xx", V, C), "5": ("sb", "sx", O + V, C), "6": ("nxb", "nx", V, C)}
ORDER = ["0", "1", "2", "X", "3", "4", "5", "6"]
UNHURRIED = ("0", "X", "5")
DMAS = ["bl", "z0", "z1", "nb", "w0", "w1", "w2", "x", "x2", "w8", "wb", "a1", "a2", "sel", "cm"] + ["y%d" % i for i in range(5)]
SEMAPHORES = (["v", "s", "t", "p", "loc", "rloc"] + ["d" + n for n in DMAS] + ["arr" + k for k in ORDER]
              + ["hop" + k for k in ORDER])


def pick(engines, i, n):
    m = 0
    for e in engines[i * n:(i + 1) * n]:
        m |= 1 << e
    return m


def plan(src, T, topo, k=None):
    near, far = [], []
    for d in T.cores:
        if d != src:
            (near if topo.may_write(src, d) else far).append(d)
    hops = [c for c in topo.cores_of(src) if c != src and all(topo.may_write(c, d) for d in far)]
    if k in UNHURRIED:
        straight = [[(d, pick(topo.engines(src, d), i, 2)) for i, d in enumerate(near)]]
    else:
        straight = [[(d, pick(topo.engines(src, d), i, 4)) for i, d in enumerate(near[:2])],
                    [(d, topo.mask(src, d)) for d in near[2:]]]
    over = []
    for i, d in enumerate(far):
        h = hops[i]
        over.append((h, pick(topo.engines(src, h), i, 4), d, topo.mask(h, d)))
    return straight, over


def bits(m):
    return bin(m).count("1")


def hop_program(g, core, T, topo):
    for src in topo.cores_of(core):
        if T.rank_of(src) is None:
            continue
        r = T.rank_of(src)
        for h, m_in, d, m_out in plan(src, T, topo)[1]:
            if h != core:
                continue
            rid, pid = topo.addr(d, core)
            for k in ORDER:
                _, land, c0, w = EXCH[k]
                g.wait_ge(T.sem["hop" + k], bits(m_in))
                g.remote_dma(T[land][:, c0 + w * r:c0 + w * r + w], T["r" + k][:], T.sem["arr" + k], T.sem.rloc,
                             pid, rid, m_out)
            g.wait_ge(T.sem.rloc, bits(m_out) * len(ORDER))


def rank_program(g, core, T, topo):
    rank = T.rank_of(core)
    if rank is None:
        hop_program(g, core, T, topo)
        return
    A = AluOpType
    COPY, IDENT, SIGN = ActivationFunctionType.Copy, ActivationFunctionType.Identity, ActivationFunctionType.Sign
    q_of = {"v": g.vector, "s": g.scalar, "t": g.tensor, "g": g, "y": g.sync}
    count = {"v": 0, "s": 0, "t": 0, "p": 0}
    waited = {"v": {}, "s": {}, "t": {}, "g": {}, "y": {}}
    log = {}
    totals = {}

    def need(queue, tokens):
        best = {}
        for s, n in tokens:
            best[s] = max(n, best.get(s, 0))
        for s in sorted(best):
            if waited[queue].get(s, 0) < best[s]:
                q_of[queue].wait_ge(T.sem[s], best[s])
                waited[queue][s] = best[s]

    def deps(queue, reads, writes):
        out = []
        for regs, wr in ((reads, False), (writes, True)):
            for name, lo, hi in regs:
                ps = name in PSUM
                for l, h, w, tok, qq in log.get(name, []):
                    if ps and qq != queue:
                        if l // 512 * 512 < -(-hi // 512) * 512 and lo // 512 * 512 < -(-h // 512) * 512:
                            out.append(tok)
                    elif l < hi and lo < h and (w or wr) and not (ps and queue == "t"):
                        out.append(tok)
        return out

    def note(queue, reads, writes, tok):
        for regs, wr in ((reads, False), (writes, True)):
            for name, lo, hi in regs:
                log.setdefault(name, []).append((lo, hi, wr, tok, queue))

    def ap(r):
        if r[0] == "ind":
            return ap(r[1]).indirect(ap(r[2]))
        name, lo, hi = r[0], r[1], r[2]
        if name in LISTS:
            c0 = 128 * LISTS.index(name)
            return T.lists[:, c0 + lo:c0 + hi]
        if name == "tr":
            return T.tr[:, :, lo:hi]
        if name in ROWS8:
            return T[name][0:8, lo:hi]
        return T[name][:, lo:hi] if len(r) == 3 else T[name][:, lo:hi:r[3]]

    def regs(rs):
        out = []
        for r in rs:
            if isinstance(r, tuple):
                if r[0] == "ind":
                    out += regs([r[1], r[2]])
                else:
                    out.append((r[0], r[1], r[2]))
        return out

    def val(x):
        return ap(x) if isinstance(x, tuple) else x

    def run(queue, reads, outs, emit):
        rd, wr = regs(reads), []
        for o in outs:
            if o[0] == "ind":
                wr += regs([o[1]])
                rd += regs([o[2]])
            else:
                wr += regs([o])
        need(queue, deps(queue, rd, wr))
        s = "p" if queue == "g" else queue
        count[s] += 1
        emit().then_inc(T.sem[s], 1)
        note(queue, rd, wr, (s, count[s]))

    def tt(out, a, b, op):
        run("v", [a, b], [out], lambda: g.vector.tensor_tensor(ap(out), ap(a), ap(b), op))

    def ts(out, a, s1, op0, s2=None, op1=None):
        if op1 is None:
            run("v", [a, s1], [out], lambda: g.vector.tensor_scalar(ap(out), ap(a), val(s1), None, op0))
        else:
            run("v", [a, s1, s2], [out], lambda: g.vector.tensor_scalar(ap(out), ap(a), val(s1), val(s2), op0, op1))

    def cp(out, a):
        run("v", [a], [out], lambda: g.vector.tensor_copy(ap(out), ap(a)))

    def fill(out, c):
        run("v", [], [out], lambda: g.vector.memset(ap(out), c))

    def scan(out, d0, d1, first, op0, op1):
        run("v", [d0, d1, first], [out], lambda: g.vector.tensor_tensor_scan(ap(out), ap(d0), ap(d1), val(first), op0, op1))

    def sc(out, a):
        run("s", [a], [out], lambda: g.scalar.activation(ap(out), ap(a), COPY))

    def sa(out, a, scale, bias, func=IDENT):
        sv, bv = [ap(z) if isinstance(z, tuple) else float(z) for z in (scale, bias)]
        run("s", [a, scale, bias], [out], lambda: g.scalar.activation(ap(out), ap(a), func, bias=bv, scale=sv))

    def iota(out, pattern, base, ch):
        run("g", [], [out], lambda: g.iota(ap(out), pattern, base, ch, allow_small_or_imprecise_dtypes=True))

    def mm(group):
        rd = regs([m[1] for m in group] + [m[2] for m in group])
        wr = regs([m[0] for m in group])
        need("t", deps("t", rd, wr))
        ins = None
        for o, l, r, st, sp in group:
            ins = g.tensor.matmul(ap(o), ap(l), ap(r), st, sp)
        count["t"] += 1
        ins.then_inc(T.sem.t, 1)
        note("t", list(dict.fromkeys(rd)), list(dict.fromkeys(wr)), ("t", count["t"]))

    def msum(out, terms):
        mm([(out, l, r, i == 0, i == len(terms) - 1) for i, (l, r) in enumerate(terms)])

    def bank(k, lo=0, n=Q):
        c0 = Q * (k % 2) + lo
        return ("q%d" % (k // 2), c0, c0 + n)

    def to_a(out, lhs, src, base=0, onto=False):
        n = out[2] - out[1]
        mm([(out, (lhs, 15 - k, 143 - k), (src, base + k, base + 16 * n, 16), k == 0 and not onto, k == 15) for k in range(16)])

    def dma(queue, sem, out, in_, reads, writes, adding=False):
        need(queue, deps(queue, reads, writes))
        ins = g.dma_start(out, in_, accum_op=A.add) if adding else q_of[queue].dma_start(out, in_)
        ins.then_inc(T.sem["d" + sem], 16)
        totals["d" + sem] = totals.get("d" + sem, 0) + 16
        note(queue, reads, writes, ("d" + sem, totals["d" + sem]))

    over = plan(core, T, topo)[1]
    sent = [0]

    def send(k):
        src, land, c0, w = EXCH[k]
        need("g", deps("g", [(src, 0, w * N)], []))

        def block(d):
            q = T.rank_of(d)
            return T[src][:, w * q:w * q + w]
        calls = []
        for h, m_in, d, _ in over:
            rid, pid = topo.addr(h, core)
            calls.append(RemoteDMATransfer(dst_ids=[DstId(rid=rid, pnc=pid)], dma_engine_mask=m_in,
                                           remote_sem=T.sem["hop" + k], src=block(d), dst=T["r" + k][:]))
            sent[0] += bits(m_in)
        g.remote_dma_fused(calls, local_sem=T.sem.loc)
        for some in plan(core, T, topo, k)[0]:
            calls = []
            for d, m in some:
                rid, pid = topo.addr(d, core)
                calls.append(RemoteDMATransfer(dst_ids=[DstId(rid=rid, pnc=pid)], dma_engine_mask=m, remote_sem=T.sem["arr" + k],
                                               src=block(d), dst=T[land][:, c0 + w * rank:c0 + w * rank + w]))
                sent[0] += bits(m)
            g.remote_dma_fused(calls, local_sem=T.sem.loc)

    def arrive(k):
        n = 0
        for c in T.cores:
            if c != core:
                near, far = plan(c, T, topo, k)
                n += sum(bits(m) for some in near for d, m in some if d == core)
                n += sum(bits(m) for _, _, d, m in far if d == core)
        _, land, c0, w = EXCH[k]
        totals["arr" + k] = n
        note("net", [], [(land, c0, c0 + w * N)], ("arr" + k, n))

    def alias(k, eng=sc):
        src, land, c0, w = EXCH[k]
        eng((land, c0 + w * rank, c0 + w * rank + w), (src, w * rank, w * rank + w))

    def col(i):
        return ("pc", i, i + 1)

    def a(name, i=0):
        return (name, 128 * i, 128 * i + 128)

    def ind(win, lo, hi, lst, c0, c1):
        return ("ind", (win, lo, hi), (lst, c0, c1))

    base = rank * V
    own = (2 * rank, 2 * rank + 2)
    mine = (V + C * rank, V + C * rank + C)
    dma("y", "bl", T.bli[:], T.bl[:], [], [("bli", 0, 16)])
    for d in range(D):
        dma("y", "w%d" % d, T.wa[:, 128 * d:128 * d + 128], T.w[:, V * d:V * d + V], [], [a("wa", d)])
    dma("y", "nb", T.nbi[:], T.nb[:], [], [("nbi", 0, 384)])
    dma("y", "x", T.xe[:, O:O + V], T.x[:], [], [("xe", O, O + V)])
    dma("s", "z0", T.lr0[:, own[0]:own[1]], T.bl[:, own[0]:own[1]], [], [("lr0",) + own])

    fill(("zz", 0, 16), 0)
    fill(("blo48", 0, 26), V + C * ((rank + 1) % N))
    iota(("pi", 0, 1), [[1, 1]], 0, 1)
    iota(("xi", 0, 160), [[1, 160]], 0, 0)
    iota(("gm", 0, 128), [[16, 8], [0, 16]], 0, 0)
    iota(("jm", 0, 256), [[0, 16], [1, 16]], 0, 0)
    iota(("kk", 0, 16), [[-C, N], [0, 2]], 48 * rank + 16 - V, 0)
    send("0")

    ts(("pi", 2, 3), ("pi", 0, 1), 4, A.arith_shift_right, 1, A.bitwise_and)
    ts(("pi", 1, 2), ("pi", 0, 1), 15, A.bitwise_and)
    ts(col(1), ("pi", 0, 1), 16, A.add)
    cp(col(3), ("pi", 2, 3))
    ts(col(2), ("pi", 2, 3), -1, A.mult, 1, A.add)
    ts(("s0", 0, 160), ("xi", 0, 160), col(1), A.is_equal, col(2), A.mult)
    ts(("s1", 0, 160), ("xi", 0, 160), col(1), A.is_equal, col(3), A.mult)
    cp(col(4), ("pi", 1, 2))
    tt(col(5), ("pi", 0, 1), ("pi", 1, 2), A.subtract)
    ts(("id16", 0, 16), ("xi", 0, 16), col(4), A.is_equal)
    ts(a("idp"), ("xi", 16, 144), col(1), A.is_equal, STEP, A.mult)
    ts(a("gf"), a("gm"), col(5), A.is_equal)
    dma("y", "z1", T.lr1[:, own[0]:own[1]], T.zz[:, 0:2], [("zz", 0, 2)], [("lr1",) + own])
    sa(("rt", 0, 128), ("xi", 0, 128), 1, base)
    for n in (128, 256, 512, 1024):
        sa(("rt", n, 2 * n), ("rt", 0, n), 1, n)
    sa(("rt", V, L), ("rt", 0, 256), 0, -1)
    ts(("bms", 0, 16), ("bli", 0, 16), 15, A.bitwise_and)
    cp(("blo", 0, 16), ("bli", 0, 16))
    cp(("bmo", 0, 16), ("bms", 0, 16))
    for d in range(D):
        run("v", [a("wa", d)], [a("tr")], lambda: g.vector.transpose(T.tr[:, d, :], ap(a("wa", d))))
    wp = [bank(2, 128 * d, 128) for d in range(D)]
    grp = []
    for i in range(8):
        b, h = i // 2, i % 2
        for gg in range(2):
            st = 16 - 16 * (gg - h)
            grp.append((("q1", i, 384, 8), ("s%d" % h, st, st + 128), ("tr", 32 * b + 16 * gg, 32 * b + 16 * gg + 16),
                        gg == 0, gg == 1))
    mm(grp)
    ts(("bsh", 0, 16), ("bli", 0, 16), 4, A.arith_shift_right)
    ts(a("idn"), a("idp"), -1, A.mult)
    cp(("boff", 0, 16), ("bsh", 0, 16))
    nb = [("nbi", 128 * d, 128 * d + 128) for d in range(D)]
    tmp = [bank(6, 128 * i, 128) for i in range(4)]
    tmq = [bank(5, 128 * i, 128) for i in range(4)]
    sc(("bmask", 0, 256), ind("id16", 0, 16, "bmo", 0, 16))
    sc(("gbb", 0, 256), ind("rt", 0, V, "blo", 0, 16))
    sa(("m0", 0, 256), ("jm", 0, 256), 1, 0, SIGN)
    sc(("rt",) + mine, ("gbb", C * rank, C * rank + C))
    cp(tmq[0], nb[0])
    tt(tmp[0], nb[1], tmq[0], A.subtract)
    tt(tmq[1], nb[2], tmq[0], A.subtract)
    cp(a("w1s"), wp[1])
    tt(a("g10"), a("w1s"), wp[0], A.is_gt)
    tt(a("wm"), a("w1s"), wp[0], A.max)
    tt(a("ta"), a("g10"), tmp[0], A.mult)
    tt(tmp[1], wp[2], a("wm"), A.is_gt)
    tt(a("tc"), tmq[1], a("ta"), A.subtract)
    tt(a("tb"), a("ta"), tmq[0], A.add)
    tt(tmp[2], a("tc"), tmp[1], A.mult)
    tt(a("pa"), a("tb"), tmp[2], A.add)

    tt(("pg", 0, 256), ind("pa", 0, 128, "boff", 0, 16), ("bmask", 0, 256), A.mult)
    msum(bank(7, 0, 256), [(a("gf"), ("pg", 0, 256))])
    cp(a("po"), a("pa"))
    sc(("ws", 0, 384), bank(2, 0, 384))
    ts(("m16", 0, 256), ("jm", 0, 256), col(4), A.is_equal)
    tt(a("g21"), wp[2], a("w1s"), A.is_gt)
    tt(a("g20"), wp[2], a("ws"), A.is_gt)
    signs = ((("idn", "g10"), ("idn", "g20")), (("idp", "g10"), ("idn", "g21")), (("idp", "g20"), ("idp", "g21")))
    for d in range(D):
        msum(bank(3, 128 * d, 128), [(a(m), a(z)) for m, z in signs[d]])
    for d in range(D):
        ts(a("nbf", d), nb[d], O + STEP * (2 - d), A.add)
    tt(("bs", 0, 256), ("m16", 0, 256), bank(7, 0, 256), A.mult)
    scan(("pgs", 0, 256), ("m0", 0, 256), ("bs", 0, 256), 0.0, A.mult, A.add)
    bp = ("pgs", 15, 256, 16)
    tt(("kt", 0, 16), bp, ("kk", 0, 16), A.add)
    ts(("ro1", 0, 16), ("kt", 0, 16), 48 * rank + 15, A.max, 48 * rank + 48, A.min)
    send("1")
    for t, c in (("hl", 255), ("t2", 255), ("xe", 0), ("sx", 0)):
        iota((t, 0, O), [[0, O]], c, 0)

    def border(out, src, d):
        tt((out, 256 * d, 256 * d + 256), ind(src, 0, 384, "boff", 16 * d, 16 * d + 16), ("bmask", 0, 256), A.mult)
    high, low = ("id16", 0, 1), ("id16", 1, 2)
    sa(a("idf"), a("idp"), 1.0 / STEP, 0)
    sc(("t1", T1V, V), ind("rt", 0, L, "po", T1V // 16, 128))
    tt(("ks", 0, 384), ("nbf", 0, 384), bank(3, 0, 384), A.add)
    for d in (1, 2):
        ts(("boff", 16 * d, 16 * d + 16), ("bsh", 0, 16), 128 * d, A.add)
    kb = [("q%d" % d, Q - 64, Q + 64) for d in range(D)]
    for d in range(D):
        for h in range(2):
            mm([((kb[d][0], Q - 64 + 64 * h, Q + 64 * h), a("idf"), ("ks", 128 * d + 64 * h, 128 * d + 64 * h + 64), True, False)])
    ts(col(6), col(5), 15, A.add)
    border("pg", "ks", 0)
    ts(("eall", 0, 143), ("xi", 0, 143), col(6), A.is_equal)
    for d in (1, 2):
        border("pg", "ks", d)
    to_a(bank(7, 128, 48), "eall", "pg")
    for j in range(2):
        cp(("blo48", 1 + j, 25, 3), ("bli", j, 16, 2))
    sc(("xb", 0, 256), ind("xe", O, O + V, "blo", 0, 16))
    sa(col(9), high, -GONE, 0)
    sa(col(8), low, -1, 1)
    sa(col(12), low, -16 * rank, 16 * rank)
    sa(("bc", 0, 16), ("xi", 0, 16), col(8), 0)
    sa(("bq", 0, N), ("xi", 0, N), 16, -16 * rank)
    sa(("e1n", 0, 143), ("eall", 0, 143), col(9), 0)
    sa(("hl", O, O + 128), ("xi", 0, 128), low, col(12))
    sa(("bq", 0, N), ("bq", 0, N), col(8), 0)

    def twice(i):
        sa(("hl", O + 128 * i, O + 256 * i), ("hl", O, O + 128 * i), 1, ("bc", i, i + 1))
    twice(1)
    twice(2)
    sc(("g48", 0, 400), ind("rt", 0, L, "blo48", 0, 25))
    cp(("t1", 0, T1V), ind("rt", 0, L, "po", 0, T1V // 16))
    cp(("bpo", 0, 16), bp)
    cp(("t1",) + mine, ("ind", ("t1", 0, V), ("blo",) + own))
    cp(("nbo", 0, 384), ("nbi", 0, 384))
    arrive("1")
    for eng, q0, q1 in ((cp, 0, rank), (sc, rank + 1, N)):
        if q0 < q1:
            eng(("t1", V + C * q0, V + C * q1), ind("g48", 0, 400, "lr1", 2 * q0, 2 * q1))
    tt(("m1b", 0, 256), ind("t1", 0, L, "bpo", 0, 16), ("gbb", 0, 256), A.is_equal)
    send("2")
    send("X")
    arrive("0")
    cp(("gho", 0, 16), ("lr0", 0, 16))
    to_a(bank(6, 128, 16), "e1n", "m1b")
    twice(4)
    twice(8)
    sc(("bkf", 0, 48), bank(7, 128, 48))
    for h in range(2):
        tt(("m1", 1024 * h, 1024 * h + 1024), ind("t1", 0, L, "po", 64 * h, 64 * h + 64), ("rt", 1024 * h, 1024 * h + 1024),
           A.is_equal)
        to_a(bank(7, 64 * h, 64), "e1n", "m1", 1024 * h)
    sa(("cb", 0, 16), bp, -1.0 / GONE, -(O + KEEP) / GONE)
    sa(a("c32"), a("pa"), -1.0 / GONE, -(O + KEEP) / GONE)
    for q in range(N):
        sa(("hl", O + V + C * q, O + V + C * q + C), ind("hl", O, O + V, "gho", 2 * q, 2 * q + 2), 1, ("bq", q, q + 1))
    alias("2")
    cp(("bki", 0, 48), ("bkf", 0, 48))
    tt(("zb", 0, 16), ("cb", 0, 16), bank(6, 128, 16), A.mult)
    ts(("bkj", 0, 48), ("bki", 0, 48), STEP - 1, A.bitwise_and)
    ts(("bnb", 0, 48), ("bkj", 0, 48), -O, A.add)
    mm([(bank(6, 0, 48), a("idf"), ("bkf", 0, 48), True, False)])
    sa(col(11), high, 128, low)
    sa(col(13), high, 1, low)
    sa(col(15), col(4), 1, base)
    alias("X")
    sa(a("va"), ("xi", 0, 128), 16, col(15))
    sc(a("gn"), a("gf"))
    dma("y", "sel", T.sel8[0:8, :], T.gn[0::16, :], [a("gn")], [a("sel8")])
    sa(("ehl", 0, 143), ("eall", 0, 143), col(11), 0)
    sa(a("idb"), a("idp"), 1.0 / STEP, 0)
    sc(("hlb", 0, 256), ind("hl", O, O + V, "blo", 0, 16))
    for d in (1, 2):
        border("pgw", "ws", d)
    arrive("2")
    sc(("fb", 0, 384), ind("m1", 0, L, "bnb", 0, 24))
    cp(("fb", 384, 768), ind("m1", 0, L, "bnb", 24, 48))
    to_a(bank(6, 0, 48), "e1n", "fb", 0, True)

    def flags(d, h, n):
        for eng, c0, c1 in ((cp, 64 * h, 64 * h + n), (sc, 64 * h + n, 64 * h + 64)):
            if c0 < c1:
                eng(("f%d" % d, 16 * c0, 16 * c1), ind("m1", 0, L, "nbo", 128 * d + c0, 128 * d + c1))
        to_a((kb[d][0], kb[d][1] + 64 * h, kb[d][1] + 64 * h + 64), "e1n", "f%d" % d, 1024 * h, True)

    def choose(z, k, u, ui, uj):
        tt(u, z, k[0], A.max)
        tt(u, u, k[1], A.max)
        tt(ui, u, k[2], A.max)
        ts(uj, ui, STEP - 1, A.bitwise_and)
    flags(0, 0, 32)
    flags(1, 0, 24)
    choose(("zb", 0, 16), [bank(6, 16 * d, 16) for d in range(D)], ("ub", 0, 16), ("ubi", 0, 16), ("ubj", 0, 16))
    cp(("pcb", 0, 16), ("ubj", 0, 16))
    cp(("t2b", 0, 256), ind("hl", 0, W, "pcb", 0, 16))
    send("3")

    def late_loads(after):
        dma("y", "x2", T.x2[:], T.x[:, 1024:V], [after], [("x2", 0, 1024)])
        dma("y", "w8", T.w8[0:8, :], T.w[:], [], [("w8", 0, D * V)])
        for c in range(16):
            dma("y", "wb", T.wb[c::16, :], T.w[:, 0:V], [], [])
        note("y", [], [("wb", 0, V)], ("dwb", totals["dwb"]))
    tt(a("zf"), a("c32"), bank(7, 0, 128), A.mult)
    for d, h, n in ((2, 0, 10), (0, 1, 32), (1, 1, 32), (2, 1, 32)):
        flags(d, h, n)
    late_loads(("f1", 1024, V))
    arrive("X")
    sc(("xcb", 0, 256), ind("xe", 0, W, "pcb", 0, 16))
    msum(bank(7, 256, 256), [(a("idb"), ("xb", 0, 256))])
    for h in range(2):
        c0, c1 = 64 * h, 64 * h + 64
        choose(("zf", c0, c1), [(k[0], k[1] + c0, k[1] + c1) for k in kb], ("ua", c0, c1), ("ui", c0, c1), ("uj", c0, c1))
        cp(("pco", c0, c1), ("uj", c0, c1))
    sa(a("pair"), a("gf"), col(13), 0)
    sc(("t2", O, O + 1024), ind("hl", 0, W, "pco", 0, 64))
    cp(("t2", O + 1024, O + 1600), ind("hl", 0, W, "pco", 64, 100))
    sc(("t2", O + 1600, O + V), ind("hl", 0, W, "pco", 100, 128))
    for h in range(2):
        mm([(bank(h), a("idb"), ("xe", O + Q * h, O + Q * h + Q), True, False)])
    alias("3", cp)
    arrive("3")
    tt(("eqb", 0, 256), ind("t2", 0, W, "pcb", 0, 16), ("hlb", 0, 256), A.is_equal)
    msum(bank(7, 0, 256), [(a("pair"), ("eqb", 0, 256))])
    to_a(bank(2, 0, 64), "ehl", "t2", O)

    def back(eng, c0, c1):
        eng(("g5", 16 * c0, 16 * c1), ind("t2", 0, W, "pco", c0, c1))
    back(sc, 0, 64)
    ts(bank(6, 0, 256), bank(7, 0, 256), -1, A.add, 0, A.max)
    tt(("xm", 0, 256), ("xcb", 0, 256), bank(6, 0, 256), A.mult)
    tt(("xxb", 0, 256), ("xm", 0, 256), bank(7, 256, 256), A.add)
    send("4")
    run("g", [a("gn")], [a("nt")], lambda: g.affine_select(T.nt[:], T.gn[:], [[-1, 128]], A.is_ge, 0.0, 0, 1))
    iota(("yy", REP0, REP0 + V), [[0, V]], 0, 0)
    to_a(bank(3, 0, 64), "ehl", "g5", 0)
    back(cp, 64, 88)
    back(sc, 88, 128)
    to_a(bank(5, 0, 64), "ehl", "g5", 1024)
    alias("4")
    sa(a("vo"), a("va"), 1, O - base - STEP)
    for h in range(2):
        c0, c1 = 64 * h, 64 * h + 64
        tt(bank(6, c0, 64), bank(3 + 2 * h, 0, 64), ("va", c0, c1), A.is_equal)
        tt(("mt", c0, c1), ("uj", c0, c1), bank(6, c0, 64), A.mult)
        cp(("mo", c0, c1), ("mt", c0, c1))
        if h == 0:
            border("pgw", "ws", 0)
    for h in range(2):
        sc(("xg", Q * h, Q * h + Q), ind("xe", 0, W, "mo", 32 * h, 32 * h + 32))
    to_a(bank(2, 64, 64), "ehl", "t2", O + 1024)
    for h in range(2):
        mm([(bank(h), a("idb"), ("xg", Q * h, Q * h + Q), False, True)])
        sc(("xx", Q * h, Q * h + Q), bank(h))
    tt(("xx", 1024, V), ind("xe", 0, W, "mo", 64, 128), ("x2", 0, 1024), A.add)
    tt(tmp[3], bank(2, 0, 128), a("va"), A.is_lt)
    tt(a("lamf"), a("mt"), tmp[3], A.mult)
    ts(a("rep"), a("lamf"), 0, A.is_equal)

    def weights(banks, q, d0=0):
        for d, bk in enumerate(banks, d0):
            msum(bank(bk), [(a("sel8"), ("w8", V * d + Q * q, V * d + Q * q + Q))])
    msum(bank(7, 0, 256), [(a("gn"), ("pgw", 512, 768))])
    weights((0,), 1, 2)
    msum(bank(4, 0, 128), [(a("gn"), a("rep"))])
    msum(bank(4, 128, 128), [(a("nt"), a("rep"))])
    msum(bank(6), [(a("gn"), ("pgw", 0, 512))])
    msum(bank(7, 256, 128), [(a("idf"), a("vo")), (a("idp"), a("rep"))])
    arrive("4")

    def part(name, q, c0=0):
        return (name, c0 + Q * q, c0 + Q * q + Q)

    def gather(d, q):
        sc(part("p%d" % d, q), ind("xx", 0, L, "nbo", 128 * d + 32 * q, 128 * d + 32 * q + 32))

    def added(q):
        dma("g", "a%d" % q, ap(part("p0", q)), ap(part("p2", q)), [part("p0", q), part("p2", q)], [part("p0", q)], True)

    def times(d, q, bk, out=None):
        tt(out or part("p%d" % d, q), part("p%d" % d, q), bank(bk), A.mult)

    def fused(c0, c1):
        tt(("p0", c0, c1), ind("xx", 0, L, "nbo", c0 // 16, c1 // 16), ("wb", c0, c1), A.mult)

    def summed(d):
        mm([(bank(3), a("idf"), part("p%d" % d, 0), d == 0, d == 2)])

    def plus(out, d, q, bk):
        tt(out, part("p%d" % d, q), bank(bk), A.add)
    sc(("pg", 0, 768), ind("xx", 0, L, "bnb", 0, 48))
    for d, q in ((1, 0), (2, 1), (2, 0), (2, 2), (1, 1), (1, 2), (1, 3), (2, 3)):
        gather(d, q)
    fused(0, Q)
    scan(a("inc"), bank(4, 0, 128), a("nbf"), float(REP0 - STEP), A.add, A.min)
    tt(a("nnx"), a("inc"), bank(4, 128, 128), A.subtract)
    weights((5, 4), 0, 1)
    weights((1,), 2, 2)
    summed(0)
    ts(a("no"), a("nnx"), STEP - REP0, A.add)
    tt(bank(7, 0, 256), ("pg", 512, 768), bank(7, 0, 256), A.mult)
    tt(("pg", 0, 512), ("pg", 0, 512), bank(6), A.mult)
    times(1, 0, 5)
    weights((2,), 1, 1)
    weights((6,), 2, 1)
    summed(1)
    tt(bank(7, 0, 256), ("pg", 0, 256), bank(7, 0, 256), A.add)
    fused(Q, 2 * Q)
    tt(("sb", 0, 256), ("pg", 256, 512), bank(7, 0, 256), A.add)
    send("5")
    times(2, 1, 0)
    added(1)
    times(2, 0, 4)
    fused(2 * Q, 3 * Q)
    times(2, 2, 1)
    added(2)
    weights((0, 5), 3, 1)
    summed(2)
    sc(("nx", 0, V), ind("hl", O, O + V, "no", 0, 128))
    sc(("nxb", 0, 256), ind("nx", 0, V, "blo", 0, 16))
    send("6")
    alias("5")
    sc(part("sx", 0, O), bank(3))
    fused(3 * Q, V)
    times(1, 1, 2, bank(2))
    times(1, 2, 6, bank(6))
    tt(a("rmin"), a("nnx"), bank(7, 256, 128), A.min)
    tt(a("lamx"), a("lamf"), bank(7, 256, 128), A.max)
    times(1, 3, 0, bank(0))
    times(2, 3, 5)
    plus(bank(0), 0, 3, 0)
    plus(part("sx", 1, O), 0, 1, 2)
    plus(part("sx", 3, O), 2, 3, 0)
    plus(part("sx", 2, O), 0, 2, 6)
    ts(a("rhoo"), a("rmin"), STEP, A.add)
    ts(a("lam"), a("lamx"), -O, A.add)
    alias("6", cp)
    arrive("5")
    cuts = (V, 1792, 1280, 768, 256, 0)
    for c1, c0 in zip(cuts, cuts[1:]):
        (cp if c1 == V else sc)(("p0", c0, c1), ind("sx", 0, W, "mo", c0 // 16, c1 // 16))
    for i, (c1, c0) in enumerate(zip(cuts, cuts[1:])):
        tt(ind("yy", 0, REP0 + c1, "rhoo", c0 // 16, c1 // 16), ("p0", c0, c1), ("sx", O + c0, O + c1), A.add)
        dma("y", "y%d" % i, T.y[:, c0:c1], T.yy[:, REP0 + c0:REP0 + c1], [("yy", REP0 + c0, REP0 + c1)], [])
    arrive("6")
    for h in range(2):
        sc(("cg", 1024 * h, 1024 * h + 1024), ind("nx", 0, L, "lam", 64 * h, 64 * h + 64))
        to_a(bank(1, 64 * h, 64), "ehl", "cg", 1024 * h)
    sc(a("cmf"), bank(1, 0, 128))
    dma("s", "cm", T.cm[:], T.cmf[:], [a("cmf")], [])
    need("g", [("loc", sent[0])] + [(s, count[s]) for s in ("v", "s", "t", "p")] + sorted(totals.items()))
